import numpy as np, ml_dtypes
CORES = [3,11,19,27,35,43,51,59]
N = 8
BF = ml_dtypes.bfloat16
W, V, Q, S, RO = 3072, 384, 3, 3, 3
RK = np.arange(N)[:, None, None]; GR = np.arange(8)[None, :, None]; VE = np.arange(V)[None, None, :]
def unfold(a, m):
    return np.ascontiguousarray(a.reshape(N, 8, 16, m).transpose(0, 1, 3, 2))
def fold(a):
    return np.ascontiguousarray(a.transpose(0, 1, 3, 2)).reshape(N, 128, -1)
def pack(T, U, P, x):
    return {"tx": fold(T).astype(np.float32).astype(BF), "pu": fold(U).astype(np.int32), "p0": fold(P).astype(np.int32), "x0": fold(x).astype(np.float32).astype(BF)}
def pair(rng, P):
    m = rng.integers(0, 17, (N, 8, V // 2, 1))
    P[:, :, 1::2] = np.where(np.arange(16) < m, P[:, :, 0::2], P[:, :, 1::2])
    return P
def parts(rng):
    T = rng.integers(0, 128, (N, 8, W, 16)); U = rng.integers(0, W, (N, 8, W, 16))
    U = np.where(rng.random((N, 8, W, 1)) < 0.25, U[..., :1], U)
    P = rng.integers(0, W, (N, 8, V, 16))
    for k in range(1, 16):
        nxt = U[RK, GR, P[..., k - 1], rng.integers(0, 16, (N, 8, V))]
        P[..., k] = np.where(rng.random((N, 8, V)) < 0.5, nxt, P[..., k])
    P = pair(rng, P)
    near = np.clip(T[RK, GR, P[..., 15]] + rng.integers(-20, 21, (N, 8, V, 16)), 0, 127)
    x = np.where(rng.random((N, 8, V, 1)) < 0.5, near, rng.integers(0, 128, (N, 8, V, 16)))
    return T, U, P, x
def setup_inputs(rng):
    return pack(*parts(rng))
def setup_inputs_ties(rng):
    T, U, P, x = parts(rng)
    few = rng.integers(0, 128, (N, 8, 6, 16)); few[:, :, 0] = 0; few[:, :, 1] = 127
    T = few[RK, GR, rng.integers(0, 6, (N, 8, W))]; x = few[RK, GR, rng.integers(0, 6, (N, 8, V))]
    return pack(T, U, P, x)
def setup_inputs_cuts(rng):
    T, U, P, x = parts(rng); h = W // 2; s = V // 4
    for g in range(8):
        o = rng.permutation(W); P[:, g] = o[h + P[:, g] % h]
        for j in range(s):
            m = (1, Q - 1, Q, N)[j if j < 4 else int(rng.integers(0, 4))]
            nm = o[s + np.arange(N)]; nm[rng.permutation(N)[:m]] = o[j]
            P[:, g, 2 * j + 1] = P[:, g, 2 * j]; P[:, g, 2 * j:2 * j + 2, 15] = nm[:, None]
    return pack(T, U, P, x)
def setup_inputs_crowd(rng):
    T, U, P, x = parts(rng); h = V // 2; r = np.arange(N)[:, None]; j = np.arange(h)[None, :]
    for g in (0, 1, 2, 3, 4, 5, 7):
        o = rng.permutation(W); nm = np.repeat(o[1:N + 1, None], V, axis=1); n = N + 1
        if g in (0, 7):
            if g == 7: o = np.concatenate([np.array([W - 1]), rng.permutation(W - 1)])
            nm = np.stack([rng.permutation(o[i * V:(i + 1) * V]) for i in np.minimum(rng.permutation(N) // Q, N // Q - 1)]); n = (N // Q) * V
        elif g in (1, 4):
            o = 1 + rng.permutation(W - 1); n = ((N - 1) // (Q - 1) + 1) * h
            nm = o[(rng.permutation(N) // (Q - 1))[:, None] * h + np.arange(V)[None, :] // 2]
        elif g == 2: nm[rng.permutation(N)[:Q]] = o[0]
        elif g == 5:
            s = int(rng.integers(0, N - Q + 1)); nm[s:s + Q - 1, :192] = o[0]; nm = nm[:, rng.permutation(V)]
        else: o = np.arange(W)[::-1]; n = 512
        a, b = o[:n], o[n:]
        T[:, g] = T[:, g] >> 2; x[:, g] = x[:, g] >> 2; T[:, g, a] = T[:, g, a] + 96
        P[:, g] = b[P[:, g] % len(b)]; U[:, g] = b[U[:, g] % len(b)]; P[:, g, 1::2] = np.array(P[:, g, 0::2])
        if g == 3:
            m = rng.integers(1, 15, (N, h)); c = W - 512 + 4 * rng.integers(0, 128, (N, h))
            P[r, g, 2 * j, m] = c; P[r, g, 2 * j + 1, m] = c + 1
        else: P[:, g, :, 15] = nm
        if g in (0, 7): P[:, g, :, 14] = np.array(P[:1, g, :, 14]); U[:, g] = np.array(U[:1, g, :, :1])
    return pack(T, U, P, x)
def setup_inputs_few(rng):
    T, U, P, x = parts(rng)
    for g in (0, 2, 4, 6):
        a = np.concatenate([np.array([0, W - 1]), rng.integers(0, W, 10)]); P[:, g] = a[P[:, g] % 12]
        if g in (0, 4): U[:, g] = a[U[:, g] % 12]
    P[:, 2] = np.array(P[:, 2, :, :1]); U[:, 4, ::2] = rng.integers(0, W, (N, W // 2, 16)); U[:, 6] = np.arange(W)[:, None]
    return pack(T, U, P, x)
def setup_inputs_spread(rng):
    T = np.minimum((np.exp2(7 * rng.random((N, 8, W, 1))) * rng.random((N, 8, W, 16))).astype(np.int64), 127)
    x = np.minimum((np.exp2(7 * rng.random((N, 8, V, 1))) * rng.random((N, 8, V, 16))).astype(np.int64), 127)
    U = np.minimum((W * rng.random((N, 8, W, 16)) ** 2).astype(np.int64), W - 1)
    P = np.minimum((W * rng.random((N, 8, V, 16)) ** 3).astype(np.int64), W - 1)
    return pack(T, U, pair(rng, P), x)
def check_inputs(d):
    bad = []
    for k, hi in (("tx", 127), ("pu", W - 1), ("p0", W - 1), ("x0", 127)):
        a = np.asarray(d[k]).astype(np.float64)
        if not (np.all(a >= 0) and np.all(a <= hi)): bad.append("range of " + k)
        elif np.any(np.floor(a) != a): bad.append("whole numbers of " + k)
    return bad
def reference(tx, pu, p0, x0):
    T = unfold(tx.astype(np.float32).astype(np.int32), W); U = unfold(pu.astype(np.int64), W)
    P = unfold(p0.astype(np.int64), V); x = unfold(x0.astype(np.float32).astype(np.int32), V)
    row = np.arange(16); cut = np.zeros((8, W), bool); R4 = RK[..., None]; G4 = GR[..., None]
    for rnd in range(RO):
        d = np.add.reduce(np.abs(T[R4, G4, P] - x[:, :, :, None, :]), axis=4)
        differ = P != P[:, :, np.arange(V) ^ 1]
        q = np.where(np.any(differ, axis=3), np.argmax(differ, axis=3), 15)
        f = np.argmax(np.where(row >= np.maximum(q, 1)[..., None], d, -1), axis=3)
        old = cut[G4, P] & (row >= 1)
        k = np.where(np.any(old, axis=3), np.argmax(old, axis=3), f)
        charged = np.zeros((N, 8, W), bool); charged[RK, GR, P[RK, GR, VE, f]] = True
        cut = cut | (np.add.reduce(charged.astype(np.int64), axis=0) >= Q)
        T[:, cut] = 256
        pup = U[RK, GR, P[RK, GR, VE, k - 1]]
        e = np.add.reduce(np.abs(T[R4, G4, pup] - x[:, :, :, None, :]), axis=4)
        b = np.argmin(e, axis=3); best = pup[RK, GR, VE, b]
        take = e[RK, GR, VE, b] < d[RK, GR, VE, k]
        P[RK, GR, VE, k] = np.where(take, best, P[RK, GR, VE, k])
        x = np.where(take[..., None], (x + T[RK, GR, best]) >> 1, x)
        if rnd + 1 < RO: P = np.roll(P, S, axis=0); x = np.roll(x, S, axis=0)
    return {"yp": fold(P).astype(np.float32), "yx": fold(x).astype(np.float32).astype(BF), "yc": np.repeat(cut[None], N, axis=0).astype(np.float32)}

@@ -1,0 +1,424 @@
+from concourse.bass import DstId, RemoteDMATransfer
+from concourse.mybir import dt, AluOpType, ActivationFunctionType
+
+A = AluOpType
+F = ActivationFunctionType
+NR, W, V, RO, STEP = 8, 3072, 384, 3, 3
+BIG = 1048576.0
+NG = 3
+UPD = (0, 1, 0, 1, 0, 1)
+
+f, b, i, u = "float32", "bfloat16", "int32", "uint16"
+SB = {
+    "TX": (b, W), "PU": (i, W), "PI": (i, V), "CU": (u, V), "CD": (f, V), "ONK": (b, V), "YP": (f, V), "YX": (b, V),
+    "ONE": (b, 1536), "IDB": (b, 128), "IDF": (f, 128), "IDH": (b, 128), "BO": (b, 128), "BOF": (f, 128), "BO4": (b, 128),
+    "BM": (b, 8), "BG": (b, 8), "XT": (b, 8, 32), "CK": (b, 8, 32), "CE": (b, 8, 32), "CP": (b, 8, 32), "TRI": (b, 8, 32),
+    "IOI": (i, 128), "MASK": (f, 128), "EX": (b, 1536), "IOM": (b, 128), "IOL": (b, 24), "ZER": (b, 128), "RSK": (f, 256),
+    "RSE": (f, 256), "FA": (b, 96), "FB": (b, 96), "CNI": (i, 128), "YC": (f, 2, 128), "YCA": (b, 2, 128),
+    "OX": (b, RO * V), "OP": (u, RO * V), "PK": (b, RO * 96), "TH": (f, 24),
+}
+for n in range(RO):
+    SB.update({"LP%d" % n: (u, V), "LX%d" % n: (b, V), "FL%d" % n: (b, 8, 96), "NC%d" % n: (b, 2, 128)})
+for n in range(NG):
+    SB["G%d" % n] = (b, 2048)
+TWO = {"PF": (f, V), "M": (b, 2048), "SP": (f, 128), "SQ": (f, 128), "MK": (f, 128), "LB": (f, 8), "CI": (i, 8),
+       "CF": (f, 8), "OL": (b, 8, 24), "OM": (b, 8, 24), "OH": (b, 8, 128), "PL": (u, 8), "OB": (b, 128), "DX": (b, 128),
+       "DY": (b, 128), "UU": (f, 128), "WI": (i, 128)}
+THREE = {"DF": (b, 128), "DZ": (f, 256), "PM": (f, 256), "SC": (f, 272), "OT": (b, 8, 32), "OF": (b, 136), "OK": (b, 136),
+         "SK": (f, 272), "AJ": (f, 256)}
+for n, s in TWO.items():
+    SB.update({n + "0": s, n + "1": s})
+for n, s in THREE.items():
+    SB.update({n + "0": s, n + "1": s, n + "2": s})
+SCRATCH = {n: ("sbuf", [128] + list(s[1:]), s[0]) for n, s in SB.items()}
+BANKS = {"XR0": [512], "XR1": [512], "K0": [512], "K1": [512], "K2": [512], "PA": [512], "PB": [512], "HI": [8, 24]}
+SCRATCH.update({n: ("psum", [128] + s, f) for n, s in BANKS.items()})
+SEMAPHORES = ["cv", "cs", "cp", "cg", "loc"] + ["d%d" % n for n in range(16)] + ["fl%d" % n for n in range(RO)] + \
+    ["a%d%d" % (s, n) for s in range(RO - 1) for n in range(3)]
+
+
+def make_plan(g, T):
+    eng = {"v": g.vector, "s": g.scalar, "p": g.tensor, "g": g, "y": g.sync}
+    nodes = []
+    wr, rd, touch, last = {}, {}, {}, {}
+
+    def add(e, reads, writes, emit, sem, inc, cost, acc=False, lag=0.1, own=True, after=()):
+        deps, me = set(after), len(nodes)
+        bks = sorted(set(k.split(":")[0] for k in list(reads) + list(writes) if k.split(":")[0] in BANKS))
+        for bk in bks:
+            h = touch.setdefault(bk, [e, [], []])
+            if h[0] != e:
+                h[:] = [e, [], h[1]]
+            deps.update(h[2])
+            h[1].append(me)
+        for k in reads:
+            if k in wr:
+                deps.add(wr[k])
+        for k in writes:
+            if not acc:
+                if k in wr:
+                    deps.add(wr[k])
+                deps.update(rd.get(k, ()))
+        nodes.append({"e": e, "deps": sorted(deps), "emit": emit, "sem": sem, "inc": inc, "cost": cost, "lag": lag, "own": own})
+        if e == "p":
+            for bk in bks:
+                if bk in last:
+                    nodes[me]["prev"] = last[bk]
+                last[bk] = me
+        for k in reads:
+            rd.setdefault(k, []).append(me)
+        for k in writes:
+            wr[k] = me
+            rd[k] = []
+        return me
+
+    fns = {"mm": ("p", g.tensor.matmul), "tt": ("v", g.vector.tensor_tensor), "ts": ("v", g.vector.tensor_scalar),
+           "cp": ("v", g.vector.tensor_copy), "ms": ("v", g.vector.memset), "scan": ("v", g.vector.tensor_tensor_scan),
+           "act": ("s", g.scalar.activation), "iota": ("g", g.iota), "asel": ("g", g.affine_select)}
+
+    def op(name, reads, writes, out, *args, acc=False, w=1.0, **kw):
+        e, fn = fns[name]
+        n = 1
+        for s in out.shape[1:]:
+            n *= int(s)
+        if e == "p":
+            cost = 0.0008 * max(64, n) * w
+        elif e == "g":
+            cost = 0.15 + 0.002 * n
+        else:
+            if name == "tt" and not any(k.split(":")[0] in BANKS for k in reads):
+                w = max(w, 2.0)
+            cost = 0.06 + 0.001 * n * w
+        return add(e, reads, writes, lambda: fn(out, *args, **kw), "c" + e, 1, cost, acc=acc)
+
+    def dma(e, reads, writes, sem, out, in_):
+        return add(e, reads, writes, lambda: eng[e].dma_start(out, in_), sem, 16, 0.1, lag=4.0)
+
+    def send(reads, transfers, n):
+        return add("g", reads, [], lambda: g.remote_dma_fused(transfers, local_sem=T.sem.loc), "loc", n, 1.0, own=False)
+
+    def arrives(sem, n, writes, sent, lag):
+        add("x", [], writes, None, sem, n, 0.0, lag=lag, after=[sent])
+
+    def finish():
+        n = len(nodes)
+        succ = [[] for _ in range(n)]
+        for k, x in enumerate(nodes):
+            x["all"] = sorted(set(x["deps"] + ([x["prev"]] if "prev" in x else [])))
+            for d in x["all"]:
+                succ[d].append(k)
+        prio = [0.0] * n
+        for k in range(n - 1, -1, -1):
+            x = nodes[k]
+            prio[k] = x["cost"] + max([prio[s] + (0.0 if nodes[s].get("prev") == k else x["lag"]) for s in succ[k]] + [0.0])
+        left = [len(x["all"]) for x in nodes]
+        ready = {e: [] for e in "vspgyx"}
+        free = {e: 0.0 for e in "vspgyx"}
+        start = [0.0] * n
+        for k in range(n):
+            if not left[k]:
+                ready[nodes[k]["e"]].append(k)
+        order = []
+        while len(order) < n:
+            best = None
+            for e, lst in ready.items():
+                if lst:
+                    t = min(start[k] for k in lst)
+                    t = t if e == "x" else max(free[e], t)
+                    if best is None or t < best[0]:
+                        best = (t, e)
+            t, e = best
+            k = max((k for k in ready[e] if start[k] <= t + 1e-9), key=lambda k: (prio[k], -k))
+            ready[e].remove(k)
+            order.append(k)
+            x = nodes[k]
+            free[e] = t + x["cost"]
+            for s in succ[k]:
+                start[s] = max(start[s], t + x["cost"] + (0.0 if nodes[s].get("prev") == k else x["lag"]))
+                left[s] -= 1
+                if not left[s]:
+                    ready[nodes[s]["e"]].append(s)
+        cnt, known, event, clock = {}, {e: {} for e in eng}, {}, {}
+        for k in order:
+            x = nodes[k]
+            e = x["e"]
+            if e == "x":
+                event[k] = (x["sem"], x["inc"])
+                clock[event[k]] = {x["sem"]: x["inc"]}
+                continue
+            need = {}
+            for d in x["deps"]:
+                s, m = event[d]
+                need[s] = max(need.get(s, 0), m)
+            todo = [(s, m) for s, m in need.items() if known[e].get(s, 0) < m]
+            todo = [p for p in todo if not any(q != p and clock[q].get(p[0], 0) >= p[1] for q in todo)]
+            for p in todo:
+                eng[e].wait_ge(T.sem[p[0]], p[1])
+                for s, m in clock[p].items():
+                    known[e][s] = max(known[e].get(s, 0), m)
+            ins = x["emit"]()
+            cnt[x["sem"]] = cnt.get(x["sem"], 0) + x["inc"]
+            if x["own"]:
+                ins.then_inc(T.sem[x["sem"]], x["inc"])
+            event[k] = (x["sem"], cnt[x["sem"]])
+            clock[event[k]] = dict(known[e])
+            clock[event[k]][x["sem"]] = cnt[x["sem"]]
+        for s, m in cnt.items():
+            if known["g"].get(s, 0) < m:
+                g.wait_ge(T.sem[s], m)
+
+    return op, dma, send, arrives, finish
+
+
+def rank_program(g, core, T, topo):
+    rank = T.rank_of(core)
+    if rank is None:
+        return
+    op, dma, send, arrives, finish = make_plan(g, T)
+    peers = [c for c in T.cores if c != core]
+    nxt = T.cores[(rank + STEP) % NR]
+    efl = [e for e in topo.engines(core, peers[0]) if all(e in topo.engines(core, c) for c in peers)]
+    enx = topo.engines(core, nxt)
+    hn = len(enx) // 2
+
+    def to(c):
+        return DstId(rid=topo.addr(c)[0], pnc=topo.addr(c)[1])
+
+    def bits(es):
+        return sum(1 << e for e in es)
+
+    TXK = ["TX.%d" % j for j in range(6)]
+    X0 = ["LX0.%d" % j for j in range(3)]
+
+    def cs(n, r=0):
+        return slice(V * r + 128 * n, V * r + 128 * n + 128)
+
+    dma("y", [], ["PI"], "d0", T.PI[:], T.p0[:])
+    dma("y", [], X0, "d1", T.LX0[:], T.x0[:])
+    for j in range(3):
+        dma("y", [], TXK[2 * j:2 * j + 2], "d%d" % (2 + j), T.TX[:, 1024 * j:1024 * j + 1024], T.tx[:, 1024 * j:1024 * j + 1024])
+    dma("y", [], ["PU"], "d5", T.PU[:], T.pu[:])
+    lo = {"allow_small_or_imprecise_dtypes": True}
+    op("ms", [], ["ONE"], T.ONE[:], 1.0)
+    op("asel", ["ONE"], ["IDB"], T.IDB[:], T.ONE[:, 0:128], [[-1, 128]], A.is_equal, 0.0, 0, 1)
+    op("asel", ["ONE"], ["BO"], T.BO[:], T.ONE[:, 0:128], [[-16, 8], [0, 16]], A.is_ge, 0.0, 0, 1)
+    op("asel", ["BO"], ["BO"], T.BO[:], T.BO[:], [[16, 8], [0, 16]], A.is_ge, 0.0, 15, -1)
+    op("ms", [], ["TRI"], T.TRI[:], 0.0)
+    op("cp", ["BO"], ["TRI"], T.TRI[:, :, 0:16], T.BO[:])
+    op("asel", ["TRI"], ["TRI"], T.TRI[:], T.TRI[:], [[16, 8], [1, 32]], A.is_ge, 0.0, -1, -1)
+    op("ms", [], ["TRI"], T.TRI[:, :, 0:2], 0.0)
+    op("ms", [], ["XT"], T.XT[:], 0.0)
+    op("ts", ["BO"], ["XT"], T.XT[:, :, 0:16], T.BO[:], 64.0, None, A.mult)
+    op("ms", [], ["CP"], T.CP[:], 0.0)
+    op("ms", [], ["CP"], T.CP[:, :, 16:32], 1.0)
+    op("ms", [], ["ZER"], T.ZER[:], 0.0)
+    for n, c in (("RSK", BIG), ("RSE", -BIG)):
+        op("ms", [], [n], T[n][:], 0.0)
+        op("ms", [], [n], T[n][:, 0:256:32], c)
+    for j in range(3):
+        for n, k in (("OF", 128), ("OK", 128), ("SC", 256), ("SK", 256)):
+            n += "%d" % j
+            op("ms", [], [n + ".e"], T[n][:, k:k + (8 if k == 128 else 16)], 0.0)
+        op("ms", [], ["PM%d.e" % j], T["PM%d" % j][:, 255:256], 1.0)
+    op("cp", ["PI"], ["LP0.0", "LP0.1", "LP0.2"], T.LP0[:], T.PI[:])
+    op("cp", ["PI"], ["PF0.0", "PF0.1", "PF0.2"], T.PF0[:], T.PI[:])
+    op("ts", X0, X0, T.LX0[:], T.LX0[:], 128.0, None, A.add)
+    for j in range(6):
+        c = slice(512 * j, 512 * j + 512)
+        if j % 2 == 0:
+            op("ts", [TXK[j]], [TXK[j]], T.TX[:, c], T.TX[:, c], 128.0, None, A.add, w=0.5)
+        else:
+            op("act", [TXK[j]], [TXK[j]], T.TX[:, c], T.TX[:, c], F.Identity, bias=128.0)
+    op("ts", ["BO"], ["BM"], T.BM[:], T.BO[:, 0:128:16], -64.0, None, A.mult)
+    op("ts", ["BO"], ["BG"], T.BG[:], T.BO[:, 0:128:16], 32.0, None, A.mult)
+    op("cp", ["BO"], ["BOF"], T.BOF[:], T.BO[:])
+    op("iota", [], ["CK"], T.CK[:], [[0, 8], [1, 32]], -15, 0, **lo)
+    op("ms", [], ["CK"], T.CK[:, :, 16:32], BIG)
+    op("ms", [], ["CK"], T.CK[:, :, 0:1], 131072.0)
+    op("iota", [], ["IOM"], T.IOM[:], [[1, 128]], 0, 0, **lo)
+    op("iota", [], ["IOL"], T.IOL[:], [[128, 24]], 0, 0, **lo)
+    op("iota", [], ["IOI"], T.IOI[:], [[1, 128]], 0, -1)
+    op("iota", [], ["CE"], T.CE[:], [[0, 8], [-1, 32]], -17, 0, **lo)
+    op("asel", ["ONE"], ["EX"], T.EX[:], T.ONE[:], [[-1, 12], [-12, 8], [0, 16]], A.is_equal, 0.0, 0, 1)
+    op("ts", ["IOI"], ["IOI"], T.IOI[:], T.IOI[:], 15, None, A.bitwise_and)
+    op("ts", ["IOI"], ["MASK"], T.MASK[:], T.IOI[:], 0.0, None, A.is_equal)
+    op("cp", ["IDB"], ["IDF"], T.IDF[:], T.IDB[:])
+    op("ts", ["IDB"], ["IDH"], T.IDH[:], T.IDB[:], 0.5, None, A.mult)
+    op("ts", ["BO"], ["BO4"], T.BO4[:], T.BO[:], 4096.0, None, A.mult)
+    op("ms", [], ["CE"], T.CE[:, :, 16:32], -BIG)
+    op("ms", [], ["CE"], T.CE[:, :, 16:17], 0.0)
+
+    def mm(reads, writes, out, lhsT, rhs, start, stop, w=1.0):
+        return op("mm", reads, writes, out, lhsT, rhs, start, stop, acc=not start, w=w)
+
+    def distances(p, r, n, lists, lkey):
+        K, M, XR, X, G = T["K%d" % (p % 3)], T["M%d" % (p % 2)], T["XR%d" % (p % 2)], T["LX%d" % r][:, cs(n)], T["G%d" % (p % NG)]
+        kk, mk, xr, xk, gk = "K%d:k" % (p % 3), "M%d." % (p % 2), "XR%d:" % (p % 2), "LX%d.%d" % (r, n), "G%d." % (p % NG)
+        mm([xk, "XT"], [kk], K[:, 0:256], X, T.XT[:], True, False)
+        for j in range(4):
+            mm(["IDB", xk], [xr + "%d" % j], XR[:, j::4], T.IDB[:], X, True, True)
+        for h in range(2):
+            op("act", TXK + [lkey], [gk + "%d" % h], G[:, 1024 * h:1024 * h + 1024],
+               T.TX[:, 0:W].indirect(lists[:, 128 * n + 64 * h:128 * n + 64 * h + 64]), F.Copy, w=1.5)
+        for k in range(16):
+            mm([gk + "0", gk + "1", "BG"], [kk], K[:, k:256:32], G[:, k::16], T.BG[:], False, False)
+        for h in range(2):
+            for j in range(4):
+                c = slice(1024 * h + j, 1024 * h + 1024, 4)
+                op("tt", [gk + "%d" % h] + [xr + "%d" % q for q in range(4)], [mk + "%d.%d" % (h, j)], M[:, c], G[:, c],
+                   XR[:, 256 * h:256 * h + 256], A.max)
+        for k in (0, 4, 8, 12, 1, 5, 9, 13, 2, 6, 10, 14, 3, 7, 11, 15):
+            mm([mk + "%d.%d" % (h, k % 4) for h in range(2)] + ["BM"], [kk], K[:, k:256:32], M[:, k::16], T.BM[:], False, False)
+
+    def one_hot(z, src, skey, dz, S, O, minmax):
+        op("scan", [skey, dz], [S], T[S][:, 0:256], T[dz][:], src, 0.0, A.add, minmax)
+        op("tt", [skey, S, S + ".e"], ["OT" + z], T["OT" + z][:], src, T[S][:, 16:272], A.is_equal)
+        op("cp", ["OT" + z], [O], T[O][:, 0:128], T["OT" + z][:, :, 0:16], w=0.5)
+
+    def to_list(y):
+        op("tt", ["PB:r", "MASK"], ["MK" + y], T["MK" + y][:], T.PB[:, 128:256], T.MASK[:], A.mult)
+        mm(["MK" + y, "BOF"], ["PB:l"], T.PB[:, 256:264], T["MK" + y][:], T.BOF[:, 0:128:16], True, True, w=4)
+        op("cp", ["PB:l"], ["PL" + y], T["PL" + y][:], T.PB[:, 256:264])
+
+    def first_half(r, n, p):
+        z, y = "%d" % (p % 3), "%d" % (p % 2)
+        PF, pfk, pk = T["PF%d" % (r % 2)], "PF%d.%d" % (r % 2, n), "LP%d.%d" % (r, n)
+        K, kk, ck = T["K" + z], "K%s:k" % z, "K%s:c" % z
+        if r:
+            op("cp", [pk], [pfk], PF[:, cs(n)], T["LP%d" % r][:, cs(n)])
+        for j in range(2):
+            op("tt", [pfk], ["DF%s.%d" % (z, j)], T["DF" + z][:, j:128:2], PF[:, 128 * n:128 * n + 128:2], PF[:, 128 * n + 1:128 * n + 128:2],
+               A.not_equal)
+        mm(["DF%s.0" % z, "DF%s.1" % z, "TRI"], [ck], K[:, 256:512], T["DF" + z][:], T.TRI[:], True, False)
+        mm(["IDB", "CP"], [ck], K[:, 256:512], T.IDB[:], T.CP[:], False, True)
+        op("act", [ck], ["DZ" + z], T["DZ" + z][:], K[:, 256:512], F.Relu, bias=BIG, scale=-BIG)
+        if r:
+            op("act", ["DZ" + z], ["PM" + z], T["PM" + z][:, 0:255], T["DZ" + z][:, 1:256], F.Identity, bias=1.0 / 1024, scale=1.0 / BIG)
+        distances(p, r, n, T["LP%d" % r], pk)
+        mm(["IDB", "CK"], [kk], K[:, 0:256], T.IDB[:], T.CK[:], False, True)
+        one_hot(z, K[:, 0:256], kk, "DZ" + z, "SC" + z, "OF" + z, A.min)
+        mm(["OF" + z, "IDB"], ["PA:n"], T.PA[:, 0:128], T["OF" + z][:, 0:128], T.IDB[:], True, True)
+        op("tt", ["PA:n", pfk], ["SP" + y], T["SP" + y][:], T.PA[:, 0:128], PF[:, cs(n)], A.mult)
+        mm(["SP" + y, "BOF"], ["PA:c"], T.PA[:, 128:136], T["SP" + y][:], T.BOF[:, 0:128:16], True, True, w=4)
+        op("cp", ["PA:c"], ["CI" + y], T["CI" + y][:], T.PA[:, 128:136])
+        op("act", ["PA:c"], ["LB" + y], T["LB" + y][:], T.PA[:, 128:136], F.Identity, bias=63.5, scale=-1.0)
+        op("ts", ["CI" + y], ["CI" + y], T["CI" + y][:], T["CI" + y][:], 127, None, A.bitwise_and)
+        for j in range(8):
+            op("act", ["LB" + y, "IOL"], ["OL%s.%d" % (y, j)], T["OL" + y][:, j, :], T.IOL[:], F.Abs, bias=T["LB" + y][:, j:j + 1])
+        op("cp", ["CI" + y], ["CF" + y], T["CF" + y][:], T["CI" + y][:])
+        op("act", ["OL%s.%d" % (y, j) for j in range(8)], ["OM" + y], T["OM" + y][:], T["OL" + y][:], F.Relu, bias=64.5, scale=-1.0)
+        for j in range(8):
+            op("ts", ["CF" + y, "IOM"], ["OH%s.%d" % (y, j)], T["OH" + y][:, j, :], T.IOM[:], T["CF" + y][:, j:j + 1], None, A.is_equal, w=0.5)
+        for j in range(8):
+            mm(["OH%s.%d" % (y, j), "OM" + y], ["HI:h"], T.HI[:, j, 0:24], T["OH" + y][:, j, :], T["OM" + y][:, j, :], False, False)
+        if n == 2:
+            spread(r)
+        th, tc = "TH%d" % n, T.TH[:, 8 * n:8 * n + 8]
+        if r == 0:
+            O = "OF" + z
+            op("ts", ["SC" + z], [th], tc, T["SC" + z][:, 31:256:32], -15.0, None, A.max)
+        else:
+            O = "OK" + z
+            op("tt", [kk, "PM" + z, "PM%s.e" % z], ["AJ" + z], T["AJ" + z][:], K[:, 0:256], T["PM" + z][:], A.mult)
+            one_hot(z, T["AJ" + z][:], "AJ" + z, "RSK", "SK" + z, O, A.min)
+            op("ts", ["SK" + z], [th], tc, T["SK" + z][:, 31:256:32], -15.0 / 1024, 1024.0, A.max, A.mult)
+        mm([O, O + ".e", "IDB"], ["PB:n"], T.PB[:, 0:128], T[O][:, 1:129], T.IDB[:], True, True)
+        mm([O, "IDB"], ["PB:o"], T.PB[:, 384:512], T[O][:, 0:128], T.IDB[:], True, True)
+        op("tt", ["PB:n", pfk], ["SQ" + y], T["SQ" + y][:], T.PB[:, 0:128], PF[:, cs(n)], A.mult)
+        op("act", ["PB:o"], ["ONK.%d" % n], T.ONK[:, cs(n)], T.PB[:, 384:512], F.Copy)
+        mm(["SQ" + y, "BOF"], ["PB:r"], T.PB[:, 128:256], T["SQ" + y][:], T.BOF[:], True, True, w=4)
+        to_list(y)
+        op("cp", ["PL" + y, "PU"], ["CU.%d" % n], T.CU[:, cs(n)], T.PU[:, 0:W].indirect(T["PL" + y][:]), w=1.5)
+        op("cp", ["CU.%d" % n], ["CD.%d" % n], T.CD[:, cs(n)], T.CU[:, cs(n)])
+
+    def spread(r):
+        mm(["ZER", "ONE"], ["HI:h"], T.HI[:], T.ZER[:], T.ONE[:, 0:192], False, True)
+        pk, PK = "PK%d" % r, T.PK[:, 96 * r:96 * r + 96]
+        op("ts", ["HI:h"], ["FA"], T.FA[:], T.HI[:, :, 0:12], 1.0, None, A.min)
+        op("ts", ["HI:h"], ["FB"], T.FB[:], T.HI[:, :, 12:24], 1.0, 16.0, A.min, A.mult)
+        op("tt", ["FA", "FB"], [pk], PK, T.FA[:], T.FB[:], A.add)
+        s = send([pk], [RemoteDMATransfer(dst_ids=[to(c) for c in peers], dma_engine_mask=bits(efl), remote_sem=T.sem["fl%d" % r],
+                                          srcs=[PK], dsts=[T["FL%d" % r][:, rank, :] for c in peers])], len(efl))
+        arrives("fl%d" % r, 7 * len(efl), ["FL%d" % r], s, 6.0)
+
+    def cuts(r):
+        pk, fl, nc = "PK%d" % r, "FL%d" % r, "NC%d" % r
+        cnt = T.PA[0:96, 0:128]
+        others = [k for k in range(NR) if k != rank]
+        mm([pk, "IDB"], ["PA:n"], cnt, T.PK[:, 96 * r:96 * r + 96], T.IDB[:], True, False)
+        for k in others:
+            mm([fl, "IDB"], ["PA:n"], cnt, T[fl][:, k, :], T.IDB[:], False, k == others[-1])
+        op("cp", ["PA:n"], ["CNI"], T.CNI[0:96, :], cnt)
+        op("ts", ["PA:n"], [nc + ".1"], T[nc][0:96, 1, :], cnt, 47.5, 256.0, A.is_lt, A.mult)
+        op("ts", ["CNI"], ["CNI"], T.CNI[0:96, :], T.CNI[0:96, :], 15, None, A.bitwise_and)
+        op("ts", ["CNI"], [nc + ".0"], T[nc][0:96, 0, :], T.CNI[0:96, :], 2.5, 256.0, A.is_lt, A.mult)
+        banks = ("PB", "XR0", "XR1", "PA")
+        for q, j in enumerate((3, 4, 5, 0, 1, 2)):
+            bank, c = banks[q % len(banks)], slice(512 * j, 512 * j + 512)
+            keys = [bank + ":%d" % l for l in range(4)]
+            for l in range(4):
+                L = 4 * j + l
+                out = T[bank][:, 128 * l:128 * l + 128]
+                if UPD[q]:
+                    mm([TXK[j], "IDB"], [keys[l]], out, T.IDB[:], T.TX[:, 128 * L:128 * L + 128], True, False)
+                mm([nc + ".%d" % (L // 12), "EX"], [keys[l]], out, T.EX[0:96, 128 * (L % 12):128 * (L % 12) + 128],
+                   T[nc][0:96, L // 12, :], not UPD[q], True)
+            if UPD[q]:
+                op("act", keys, [TXK[j]], T.TX[:, c], T[bank][:], F.Relu, bias=-256.0)
+            else:
+                op("tt", keys + [TXK[j]], [TXK[j]], T.TX[:, c], T.TX[:, c], T[bank][:], A.min)
+
+    def second_half(r, n, p):
+        z, y, xk, x = "%d" % (p % 3), "%d" % (p % 2), "LX%d.%d" % (r, n), T["LX%d" % r][:, cs(n)]
+        PF, pfk, oxk, opk = T["PF%d" % (r % 2)], "PF%d.%d" % (r % 2, n), "OX%d.%d" % (r, n), "OP%d.%d" % (r, n)
+        K, kk = T["K" + z], "K%s:k" % z
+        distances(p, r, n, T.CU, "CU.%d" % n)
+        mm(["IDF", "TH%d" % n], [kk], K[:, 16:256:32], T.IDF[:], T.TH[:, 8 * n:8 * n + 8], False, False, w=4)
+        mm(["IDB", "CE"], [kk], K[:, 0:256], T.IDB[:], T.CE[:], False, True)
+        one_hot(z, K[:, 0:256], kk, "RSE", "SC" + z, "OF" + z, A.max)
+        mm(["OF" + z, "IDB"], ["PA:n"], T.PA[:, 0:128], T["OF" + z][:, 0:128], T.IDB[:], True, True)
+        op("tt", ["PA:n", "CD.%d" % n], ["SP" + y], T["SP" + y][:], T.PA[:, 0:128], T.CD[:, cs(n)], A.mult)
+        op("act", ["PA:n"], ["OB" + y], T["OB" + y][:], T.PA[:, 0:128], F.Copy)
+        mm(["SP" + y, "BOF"], ["PB:r"], T.PB[:, 128:256], T["SP" + y][:], T.BOF[:], True, True, w=4)
+        mm(["OB" + y, "BO"], ["PB:n"], T.PB[:, 0:128], T.BO[:], T["OB" + y][:], True, True)
+        mm(["SP" + y, "BOF"], ["PB:o"], T.PB[:, 384:512], T.BOF[:], T["SP" + y][:], True, False, w=4)
+        mm(["OB" + y, "BO4"], ["PB:o"], T.PB[:, 384:512], T.BO4[:], T["OB" + y][:], False, True)
+        to_list(y)
+        op("tt", ["PL" + y, xk] + TXK, ["DX" + y], T["DX" + y][:], T.TX[:, 0:W].indirect(T["PL" + y][:]), x, A.subtract)
+        op("tt", ["DX" + y, "PB:n"], ["DY" + y], T["DY" + y][:], T["DX" + y][:], T.PB[:, 0:128], A.mult)
+        mm([xk, "IDB"], ["PA:x"], T.PA[:, 128:256], T.IDB[:], x, True, False)
+        mm(["DY" + y, "IDH"], ["PA:x"], T.PA[:, 128:256], T.IDH[:], T["DY" + y][:], False, True)
+        op("act", ["PA:x"], [oxk], T.OX[:, cs(n, r)], T.PA[:, 128:256], F.Identity, bias=-0.2)
+        op("tt", ["ONK.%d" % n, "PB:o"], ["UU" + y], T["UU" + y][:], T.ONK[:, cs(n)], T.PB[:, 384:512], A.mult)
+        op("tt", ["UU" + y, pfk], ["WI" + y], T["WI" + y][:], PF[:, cs(n)], T["UU" + y][:], A.max)
+        op("ts", ["WI" + y], ["WI" + y], T["WI" + y][:], T["WI" + y][:], 4095, None, A.bitwise_and)
+        if r < RO - 1:
+            op("cp", ["WI" + y], [opk], T.OP[:, cs(n, r)], T["WI" + y][:])
+            sem = T.sem["a%d%d" % (r, n)]
+            s = send([oxk, opk], [
+                RemoteDMATransfer(dst_ids=[to(nxt)], dma_engine_mask=bits(es), remote_sem=sem, src=T[o][:, cs(n, r)],
+                                  dst=T["%s%d" % (l, r + 1)][:, cs(n)])
+                for es, o, l in ((enx[:hn], "OP", "LP"), (enx[hn:], "OX", "LX"))], 2 * hn)
+            arrives("a%d%d" % (r, n), 2 * hn, ["LP%d.%d" % (r + 1, n), "LX%d.%d" % (r + 1, n)], s, 4.0)
+        else:
+            op("cp", ["WI" + y], ["YP.%d" % n], T.YP[:, cs(n)], T["WI" + y][:])
+            op("act", [oxk], ["YX.%d" % n], T.YX[:, cs(n)], T.OX[:, cs(n, r)], F.Identity, bias=-128.0)
+            dma("y", ["YP.%d" % n], [], "d%d" % (6 + n), T.yp[:, cs(n)], T.YP[:, cs(n)])
+            dma("y", ["YX.%d" % n], [], "d%d" % (9 + n), T.yx[:, cs(n)], T.YX[:, cs(n)])
+
+    for r in range(RO):
+        p = 6 * r
+        mm(["ZER", "ONE"], ["HI:h"], T.HI[:], T.ZER[:], T.ONE[:, 0:192], True, False)
+        for n in range(3):
+            first_half(r, n, p + n)
+        cuts(r)
+        for n in range(3):
+            second_half(r, n, p + 3 + n)
+        if r == RO - 1:
+            k = ["NC%d.%d" % (q, j) for q in range(RO) for j in range(2)]
+            op("tt", k[0:4], ["YCA"], T.YCA[0:96], T.NC0[0:96], T.NC1[0:96], A.min)
+            op("tt", ["YCA"] + k[4:6], ["YCA"], T.YCA[0:96], T.YCA[0:96], T.NC2[0:96], A.min)
+            op("ts", ["YCA"], ["YC"], T.YC[0:96], T.YCA[0:96], 128.0, None, A.is_lt)
+            for j in range(2):
+                dma("y", ["YC"], [], "d%d" % (12 + j), T.yc[:, 1536 * j:1536 * j + 1536], T.YC[0:96, j, :])
+    finish()

@@ -4,53 +4,53 @@ from concourse.mybir import dt, AluOpType, ActivationFunctionType
 A = AluOpType
 F = ActivationFunctionType
 NR, W, V, RO, STEP = 8, 3072, 384, 3, 3
-BIG = 1048576.0
+U, H = 96, 192
+BIG = 16777216.0
+OFF = 1536.0
+CUT = 2176.0
 NG = 3
-UPD = (0, 1, 0, 1, 0, 1)
+CH = (0, 64, 96)
+VG = set()
 
-f, b, i, u = "float32", "bfloat16", "int32", "uint16"
+f, b, i, u, h = "float32", "bfloat16", "int32", "uint16", "float16"
 SB = {
-    "TX": (b, W), "PU": (i, W), "PI": (i, V), "CU": (u, V), "CD": (f, V), "ONK": (b, V), "YP": (f, V), "YX": (b, V),
-    "ONE": (b, 1536), "IDB": (b, 128), "IDF": (f, 128), "IDH": (b, 128), "BO": (b, 128), "BOF": (f, 128), "BO4": (b, 128),
-    "BM": (b, 8), "BG": (b, 8), "XT": (b, 8, 32), "CK": (b, 8, 32), "CE": (b, 8, 32), "CP": (b, 8, 32), "TRI": (b, 8, 32),
-    "IOI": (i, 128), "MASK": (f, 128), "EX": (b, 1536), "IOM": (b, 128), "IOL": (b, 24), "ZER": (b, 128), "RSK": (f, 256),
-    "RSE": (f, 256), "FA": (b, 96), "FB": (b, 96), "CNI": (i, 128), "YC": (f, 2, 128), "YCA": (b, 2, 128),
-    "OX": (b, RO * V), "OP": (u, RO * V), "PK": (b, RO * 96), "TH": (f, 24),
+    "LX": (b, RO * V), "PF": (h, RO * V), "OX": (b, RO * V), "OP": (h, RO * V), "LP": (u, V), "CU": (u, V), "CD": (h, V),
+    "PI": (i, V), "YP": (f, V), "YX": (b, V), "YC": (f, 2, 128), "A0": (b, 2, 128), "FS": (b, 2 * RO, 96),
+    "FL": (b, 2 * RO, 8, 96), "OK": (b, 4, 136), "ZK": (f, 4, 128),
+    "ONE": (b, 384), "IDB": (b, 128), "IDN": (b, 128), "IDP": (h, 128), "IDZ": (b, 256), "IDH": (b, 128), "ID4": (b, 128),
+    "BO": (b, 128), "BP": (h, 128), "B64": (b, 128), "BG": (b, 16), "BM": (b, 16), "XT": (b, 256), "TRI": (b, 128),
+    "WK": (b, 16, 8), "EE": (h, 144), "TB": (h, 8, 25), "CK": (b, 256), "CE": (b, 128), "CT": (b, 8, 25), "CX": (b, 384),
+    "CY": (b, 128), "RS": (f, 128), "RE": (f, 128), "KP": (f, 128), "ZB": (f, 1), "ZI": (i, 1), "IOM": (b, 128), "ZER": (b, 128),
 }
-for n in range(RO):
-    SB.update({"LP%d" % n: (u, V), "LX%d" % n: (b, V), "FL%d" % n: (b, 8, 96), "NC%d" % n: (b, 2, 128)})
 for n in range(NG):
-    SB["G%d" % n] = (b, 2048)
-TWO = {"PF": (f, V), "M": (b, 2048), "SP": (f, 128), "SQ": (f, 128), "MK": (f, 128), "LB": (f, 8), "CI": (i, 8),
-       "CF": (f, 8), "OL": (b, 8, 24), "OM": (b, 8, 24), "OH": (b, 8, 128), "PL": (u, 8), "OB": (b, 128), "DX": (b, 128),
-       "DY": (b, 128), "UU": (f, 128), "WI": (i, 128)}
-THREE = {"DF": (b, 128), "DZ": (f, 256), "PM": (f, 256), "SC": (f, 272), "OT": (b, 8, 32), "OF": (b, 136), "OK": (b, 136),
-         "SK": (f, 272), "AJ": (f, 256)}
+    SB["G%d" % n] = (b, 16 * U)
+TWO = {"TX": (b, W), "PU": (i, W), "M": (b, 16 * U), "DF": (b, 48), "ZZ": (b, U), "S1": (f, 128), "S2": (f, 128), "ZF": (f, 128),
+       "OF": (b, 128), "SP": (h, U), "SQ": (h, U), "HH": (b, 8), "NN": (f, 8), "TM": (b, 8, 25), "OH": (b, 8, 128), "PL": (u, 8),
+       "FR": (b, 128), "OB": (b, U), "OT": (b, U), "DX": (b, U), "DY": (b, U), "S3": (f, 128), "S4": (f, 128), "PM": (u, 8)}
 for n, s in TWO.items():
     SB.update({n + "0": s, n + "1": s})
-for n, s in THREE.items():
-    SB.update({n + "0": s, n + "1": s, n + "2": s})
 SCRATCH = {n: ("sbuf", [128] + list(s[1:]), s[0]) for n, s in SB.items()}
-BANKS = {"XR0": [512], "XR1": [512], "K0": [512], "K1": [512], "K2": [512], "PA": [512], "PB": [512], "HI": [8, 24]}
+BANKS = {"XR0": [512], "XR1": [512], "K0": [512], "K1": [512], "PA": [512], "PB": [512], "HI": [4, 24], "CF": [512]}
 SCRATCH.update({n: ("psum", [128] + s, f) for n, s in BANKS.items()})
-SEMAPHORES = ["cv", "cs", "cp", "cg", "loc"] + ["d%d" % n for n in range(16)] + ["fl%d" % n for n in range(RO)] + \
-    ["a%d%d" % (s, n) for s in range(RO - 1) for n in range(3)]
+SEMAPHORES = ["cv", "cs", "cp", "cg", "loc"] + ["d%d" % n for n in range(56)] + ["fl%d" % n for n in range(2 * RO)] + \
+    ["a%d%d" % (s, n) for s in range(RO - 1) for n in range(4)]
 
 
 def make_plan(g, T):
     eng = {"v": g.vector, "s": g.scalar, "p": g.tensor, "g": g, "y": g.sync}
     nodes = []
     wr, rd, touch, last = {}, {}, {}, {}
+    nd = [0]
 
-    def add(e, reads, writes, emit, sem, inc, cost, acc=False, lag=0.1, own=True, after=()):
+    def add(e, reads, writes, emit, sem, inc, cost, acc=False, lag=0.08, own=True, after=()):
         deps, me = set(after), len(nodes)
         bks = sorted(set(k.split(":")[0] for k in list(reads) + list(writes) if k.split(":")[0] in BANKS))
         for bk in bks:
-            h = touch.setdefault(bk, [e, [], []])
-            if h[0] != e:
-                h[:] = [e, [], h[1]]
-            deps.update(h[2])
-            h[1].append(me)
+            t = touch.setdefault(bk, [e, [], []])
+            if t[0] != e:
+                t[:] = [e, [], t[1]]
+            deps.update(t[2])
+            t[1].append(me)
         for k in reads:
             if k in wr:
                 deps.add(wr[k])
@@ -82,20 +82,21 @@ def make_plan(g, T):
         for s in out.shape[1:]:
             n *= int(s)
         if e == "p":
-            cost = 0.0008 * max(64, n) * w
+            cost = 0.0005 * max(64, n) * w
         elif e == "g":
             cost = 0.15 + 0.002 * n
         else:
-            if name == "tt" and not any(k.split(":")[0] in BANKS for k in reads):
-                w = max(w, 2.0)
-            cost = 0.06 + 0.001 * n * w
+            if name == "tt" and w == 1.0 and not any(k.split(":")[0] in BANKS for k in reads):
+                w = 2.0
+            cost = 0.03 + 0.001 * max(64, n * w)
         return add(e, reads, writes, lambda: fn(out, *args, **kw), "c" + e, 1, cost, acc=acc)
 
-    def dma(e, reads, writes, sem, out, in_):
-        return add(e, reads, writes, lambda: eng[e].dma_start(out, in_), sem, 16, 0.1, lag=4.0)
+    def dma(e, reads, writes, out, in_, lag=2.3):
+        nd[0] += 1
+        return add(e, reads, writes, lambda: eng[e].dma_start(out, in_), "d%d" % (nd[0] - 1), 16, 0.06, lag=lag)
 
     def send(reads, transfers, n):
-        return add("g", reads, [], lambda: g.remote_dma_fused(transfers, local_sem=T.sem.loc), "loc", n, 1.0, own=False)
+        return add("g", reads, [], lambda: g.remote_dma_fused(transfers, local_sem=T.sem.loc), "loc", n, 0.7, own=False)
 
     def arrives(sem, n, writes, sent, lag):
         add("x", [], writes, None, sem, n, 0.0, lag=lag, after=[sent])
@@ -110,7 +111,7 @@ def make_plan(g, T):
         prio = [0.0] * n
         for k in range(n - 1, -1, -1):
             x = nodes[k]
-            prio[k] = x["cost"] + max([prio[s] + (0.0 if nodes[s].get("prev") == k else x["lag"]) for s in succ[k]] + [0.0])
+            prio[k] = x["cost"] + max([prio[s] + (0.0 if nodes[s].get("prev") == k else x["lag"]) for s in succ[k]] + [x["lag"]])
         left = [len(x["all"]) for x in nodes]
         ready = {e: [] for e in "vspgyx"}
         free = {e: 0.0 for e in "vspgyx"}
@@ -187,238 +188,261 @@ def rank_program(g, core, T, topo):
     def bits(es):
         return sum(1 << e for e in es)
 
-    TXK = ["TX.%d" % j for j in range(6)]
-    X0 = ["LX0.%d" % j for j in range(3)]
+    def cs(q, r=0):
+        return slice(V * r + U * q, V * r + U * q + U)
 
-    def cs(n, r=0):
-        return slice(V * r + 128 * n, V * r + 128 * n + 128)
+    def txk(a):
+        return ["TX%d.0" % a, "TX%d.1" % a]
 
-    dma("y", [], ["PI"], "d0", T.PI[:], T.p0[:])
-    dma("y", [], X0, "d1", T.LX0[:], T.x0[:])
-    for j in range(3):
-        dma("y", [], TXK[2 * j:2 * j + 2], "d%d" % (2 + j), T.TX[:, 1024 * j:1024 * j + 1024], T.tx[:, 1024 * j:1024 * j + 1024])
-    dma("y", [], ["PU"], "d5", T.PU[:], T.pu[:])
+    for a in range(2):
+        rows, c = slice(64 * a, 64 * a + 64), slice(H * a, H * a + H)
+        for j in range(2):
+            p = slice(64 * j, 64 * j + 64)
+            dma("y" if a or j else "s", [], ["TX%d.%d" % (a, j)], T["TX%d" % a][p, :], T.tx[rows, :], lag=3.5)
+        for j in range(2):
+            p = slice(64 * j, 64 * j + 64)
+            dma("y" if a else "s", [], ["PI%d.%d" % (a, j)], T.PI[p, c], T.p0[rows, H * j:H * j + H])
+            dma("y", [], ["X%d.%d" % (a, j)], T.LX[p, c], T.x0[rows, H * j:H * j + H])
+    for a in range(2):
+        for j in range(2):
+            dma("y", [], ["PU%d.%d" % (a, j)], T["PU%d" % a][64 * j:64 * j + 64, :], T.pu[64 * a:64 * a + 64, :], lag=8.0 + 5 * a)
+        dma("y", [], ["A0.%d" % a], T.A0[0:96, a, :], T.tx[64 * a:64 * a + 64:16, :])
+    for a in range(2):
+        c = slice(H * a, H * a + H)
+        pi = ["PI%d.0" % a, "PI%d.1" % a]
+        op("cp", pi, ["LP.%d" % (2 * a), "LP.%d" % (2 * a + 1)], T.LP[:, c], T.PI[:, c])
+        op("ts", pi, ["PF0.%d" % (2 * a), "PF0.%d" % (2 * a + 1)], T.PF[:, c], T.PI[:, c], -OFF, None, A.add)
+        op("ts", ["X%d.0" % a, "X%d.1" % a], ["LX0.%d" % (2 * a), "LX0.%d" % (2 * a + 1)], T.LX[:, c], T.LX[:, c], 128.0, None, A.add, w=0.5)
+
     lo = {"allow_small_or_imprecise_dtypes": True}
-    op("ms", [], ["ONE"], T.ONE[:], 1.0)
+    op("ms", [], ["ONE"], T.ONE[:], 1.0, w=0.5)
     op("asel", ["ONE"], ["IDB"], T.IDB[:], T.ONE[:, 0:128], [[-1, 128]], A.is_equal, 0.0, 0, 1)
     op("asel", ["ONE"], ["BO"], T.BO[:], T.ONE[:, 0:128], [[-16, 8], [0, 16]], A.is_ge, 0.0, 0, 1)
     op("asel", ["BO"], ["BO"], T.BO[:], T.BO[:], [[16, 8], [0, 16]], A.is_ge, 0.0, 15, -1)
-    op("ms", [], ["TRI"], T.TRI[:], 0.0)
-    op("cp", ["BO"], ["TRI"], T.TRI[:, :, 0:16], T.BO[:])
-    op("asel", ["TRI"], ["TRI"], T.TRI[:], T.TRI[:], [[16, 8], [1, 32]], A.is_ge, 0.0, -1, -1)
-    op("ms", [], ["TRI"], T.TRI[:, :, 0:2], 0.0)
-    op("ms", [], ["XT"], T.XT[:], 0.0)
-    op("ts", ["BO"], ["XT"], T.XT[:, :, 0:16], T.BO[:], 64.0, None, A.mult)
-    op("ms", [], ["CP"], T.CP[:], 0.0)
-    op("ms", [], ["CP"], T.CP[:, :, 16:32], 1.0)
-    op("ms", [], ["ZER"], T.ZER[:], 0.0)
-    for n, c in (("RSK", BIG), ("RSE", -BIG)):
-        op("ms", [], [n], T[n][:], 0.0)
-        op("ms", [], [n], T[n][:, 0:256:32], c)
-    for j in range(3):
-        for n, k in (("OF", 128), ("OK", 128), ("SC", 256), ("SK", 256)):
-            n += "%d" % j
-            op("ms", [], [n + ".e"], T[n][:, k:k + (8 if k == 128 else 16)], 0.0)
-        op("ms", [], ["PM%d.e" % j], T["PM%d" % j][:, 255:256], 1.0)
-    op("cp", ["PI"], ["LP0.0", "LP0.1", "LP0.2"], T.LP0[:], T.PI[:])
-    op("cp", ["PI"], ["PF0.0", "PF0.1", "PF0.2"], T.PF0[:], T.PI[:])
-    op("ts", X0, X0, T.LX0[:], T.LX0[:], 128.0, None, A.add)
-    for j in range(6):
-        c = slice(512 * j, 512 * j + 512)
-        if j % 2 == 0:
-            op("ts", [TXK[j]], [TXK[j]], T.TX[:, c], T.TX[:, c], 128.0, None, A.add, w=0.5)
-        else:
-            op("act", [TXK[j]], [TXK[j]], T.TX[:, c], T.TX[:, c], F.Identity, bias=128.0)
-    op("ts", ["BO"], ["BM"], T.BM[:], T.BO[:, 0:128:16], -64.0, None, A.mult)
-    op("ts", ["BO"], ["BG"], T.BG[:], T.BO[:, 0:128:16], 32.0, None, A.mult)
-    op("cp", ["BO"], ["BOF"], T.BOF[:], T.BO[:])
-    op("iota", [], ["CK"], T.CK[:], [[0, 8], [1, 32]], -15, 0, **lo)
-    op("ms", [], ["CK"], T.CK[:, :, 16:32], BIG)
-    op("ms", [], ["CK"], T.CK[:, :, 0:1], 131072.0)
+    op("asel", ["BO"], ["TRI"], T.TRI[:], T.BO[:], [[1, 128]], A.is_ge, 0.0, 0, -1)
+    op("ms", [], ["TRI"], T.TRI[:, 0:128:16], 0.0)
+    for n, src, c in (("IDN", "IDB", -1.0), ("IDP", "IDB", -1.0), ("IDH", "IDB", 0.5), ("ID4", "IDB", 4096.0),
+                      ("BP", "BO", 1.0), ("B64", "BO", 64.0)):
+        op("ts", [src], [n], T[n][:], T[src][:], c, None, A.mult, w=0.5)
+    for j in range(2):
+        op("ts", ["BO"], ["BM"], T.BM[:, 8 * j:8 * j + 8], T.BO[:, 0:128:16], -64.0, None, A.mult)
+        op("ts", ["BO"], ["BG"], T.BG[:, 8 * j:8 * j + 8], T.BO[:, 0:128:16], 32.0, None, A.mult)
+        op("ts", ["BO"], ["XT"], T.XT[:, 128 * j:128 * j + 128], T.BO[:], 32.0, None, A.mult, w=0.5)
+        op("ts", ["IDB"], ["IDZ"], T.IDZ[:, 128 * j:128 * j + 128], T.IDB[:], 131072.0, None, A.mult, w=0.5)
+    op("iota", [], ["WK"], T.WK[:], [[-128, 16], [0, 8]], 2048, 0, **lo)
+    op("asel", ["WK"], ["WK"], T.WK[:], T.WK[:], [[0, 16], [-16, 8]], A.is_equal, 0.0, 0, 1)
+    op("ms", [], ["WK"], T.WK[:, 0, :], 0.0)
+    op("ms", [], ["EE"], T.EE[:], 0.0)
+    op("cp", ["BO"], ["EE"], T.EE[:, 15:143:16], T.BO[:, 0:128:16])
+    op("cp", ["BO"], ["TB"], T.TB[:, :, 0:16], T.BO[:])
+    op("cp", ["TB"], ["TB"], T.TB[:, :, 16:25], T.TB[:, :, 0:9])
+    op("ts", ["TB"], ["TB"], T.TB[:, :, 1:25:2], T.TB[:, :, 1:25:2], -1.0, None, A.mult)
+    for n, pat, base, c in (("CK", [[0, 16], [1, 16]], 0, -65536.0), ("CE", [[0, 8], [-1, 16]], 0, -65536.0),
+                            ("CT", [[0, 8], [-128, 25]], int(OFF), 0.5)):
+        op("ms", [], [n], T[n][0:32], 0.0)
+        op("iota", [], [n], T[n][0:1], pat, base, 0, **lo)
+        op("ms", [], [n], T[n][32:33], c)
+    op("ts", ["CT"], ["CT"], T.CT[0:33, :, 1:25:2], T.CT[0:33, :, 1:25:2], -1.0, None, A.mult)
+    op("ms", [], ["CX"], T.CX[0:1, :], -128.0)
+    op("ms", [], ["CY"], T.CY[0:1, :], -8192.0)
+    for n, c0, c1 in (("RS", 0.0, BIG), ("RE", BIG, -65280.0), ("KP", 1.0, 0.0)):
+        op("ms", [], [n], T[n][:], c0)
+        op("ms", [], [n], T[n][:, 0:128:16], c1)
+    op("iota", [], ["ZI"], T.ZI[:], [[0, 1]], 0, 1)
+    op("ts", ["ZI"], ["ZI"], T.ZI[:], T.ZI[:], 15, None, A.bitwise_and)
+    op("ts", ["ZI"], ["ZB"], T.ZB[:], T.ZI[:], 15.0, None, A.not_equal)
     op("iota", [], ["IOM"], T.IOM[:], [[1, 128]], 0, 0, **lo)
-    op("iota", [], ["IOL"], T.IOL[:], [[128, 24]], 0, 0, **lo)
-    op("iota", [], ["IOI"], T.IOI[:], [[1, 128]], 0, -1)
-    op("iota", [], ["CE"], T.CE[:], [[0, 8], [-1, 32]], -17, 0, **lo)
-    op("asel", ["ONE"], ["EX"], T.EX[:], T.ONE[:], [[-1, 12], [-12, 8], [0, 16]], A.is_equal, 0.0, 0, 1)
-    op("ts", ["IOI"], ["IOI"], T.IOI[:], T.IOI[:], 15, None, A.bitwise_and)
-    op("ts", ["IOI"], ["MASK"], T.MASK[:], T.IOI[:], 0.0, None, A.is_equal)
-    op("cp", ["IDB"], ["IDF"], T.IDF[:], T.IDB[:])
-    op("ts", ["IDB"], ["IDH"], T.IDH[:], T.IDB[:], 0.5, None, A.mult)
-    op("ts", ["BO"], ["BO4"], T.BO4[:], T.BO[:], 4096.0, None, A.mult)
-    op("ms", [], ["CE"], T.CE[:, :, 16:32], -BIG)
-    op("ms", [], ["CE"], T.CE[:, :, 16:17], 0.0)
+    op("ms", [], ["ZER"], T.ZER[:], 0.0)
+    op("ms", [], ["ZK.%d" % q for q in range(4)], T.ZK[:], 0.0)
+    op("ms", [], ["OK.e"], T.OK[:, :, 128:136], 0.0)
+    for j in range(2):
+        op("ms", [], ["ZF%d" % j], T["ZF%d" % j][:], 0.0)
 
-    def mm(reads, writes, out, lhsT, rhs, start, stop, w=1.0):
-        return op("mm", reads, writes, out, lhsT, rhs, start, stop, acc=not start, w=w)
+    v = slice(0, U)
+    I96 = T.IDB[v, v]
 
-    def distances(p, r, n, lists, lkey):
-        K, M, XR, X, G = T["K%d" % (p % 3)], T["M%d" % (p % 2)], T["XR%d" % (p % 2)], T["LX%d" % r][:, cs(n)], T["G%d" % (p % NG)]
-        kk, mk, xr, xk, gk = "K%d:k" % (p % 3), "M%d." % (p % 2), "XR%d:" % (p % 2), "LX%d.%d" % (r, n), "G%d." % (p % NG)
-        mm([xk, "XT"], [kk], K[:, 0:256], X, T.XT[:], True, False)
-        for j in range(4):
-            mm(["IDB", xk], [xr + "%d" % j], XR[:, j::4], T.IDB[:], X, True, True)
-        for h in range(2):
-            op("act", TXK + [lkey], [gk + "%d" % h], G[:, 1024 * h:1024 * h + 1024],
-               T.TX[:, 0:W].indirect(lists[:, 128 * n + 64 * h:128 * n + 64 * h + 64]), F.Copy, w=1.5)
-        for k in range(16):
-            mm([gk + "0", gk + "1", "BG"], [kk], K[:, k:256:32], G[:, k::16], T.BG[:], False, False)
-        for h in range(2):
-            for j in range(4):
-                c = slice(1024 * h + j, 1024 * h + 1024, 4)
-                op("tt", [gk + "%d" % h] + [xr + "%d" % q for q in range(4)], [mk + "%d.%d" % (h, j)], M[:, c], G[:, c],
-                   XR[:, 256 * h:256 * h + 256], A.max)
-        for k in (0, 4, 8, 12, 1, 5, 9, 13, 2, 6, 10, 14, 3, 7, 11, 15):
-            mm([mk + "%d.%d" % (h, k % 4) for h in range(2)] + ["BM"], [kk], K[:, k:256:32], M[:, k::16], T.BM[:], False, False)
+    def mm(reads, writes, out, lhsT, rhs, start, stop):
+        return op("mm", reads, writes, out, lhsT, rhs, start, stop, acc=not start)
 
-    def one_hot(z, src, skey, dz, S, O, minmax):
-        op("scan", [skey, dz], [S], T[S][:, 0:256], T[dz][:], src, 0.0, A.add, minmax)
-        op("tt", [skey, S, S + ".e"], ["OT" + z], T["OT" + z][:], src, T[S][:, 16:272], A.is_equal)
-        op("cp", ["OT" + z], [O], T[O][:, 0:128], T["OT" + z][:, :, 0:16], w=0.5)
-
-    def to_list(y):
-        op("tt", ["PB:r", "MASK"], ["MK" + y], T["MK" + y][:], T.PB[:, 128:256], T.MASK[:], A.mult)
-        mm(["MK" + y, "BOF"], ["PB:l"], T.PB[:, 256:264], T["MK" + y][:], T.BOF[:, 0:128:16], True, True, w=4)
-        op("cp", ["PB:l"], ["PL" + y], T["PL" + y][:], T.PB[:, 256:264])
-
-    def first_half(r, n, p):
-        z, y = "%d" % (p % 3), "%d" % (p % 2)
-        PF, pfk, pk = T["PF%d" % (r % 2)], "PF%d.%d" % (r % 2, n), "LP%d.%d" % (r, n)
-        K, kk, ck = T["K" + z], "K%s:k" % z, "K%s:c" % z
-        if r:
-            op("cp", [pk], [pfk], PF[:, cs(n)], T["LP%d" % r][:, cs(n)])
-        for j in range(2):
-            op("tt", [pfk], ["DF%s.%d" % (z, j)], T["DF" + z][:, j:128:2], PF[:, 128 * n:128 * n + 128:2], PF[:, 128 * n + 1:128 * n + 128:2],
-               A.not_equal)
-        mm(["DF%s.0" % z, "DF%s.1" % z, "TRI"], [ck], K[:, 256:512], T["DF" + z][:], T.TRI[:], True, False)
-        mm(["IDB", "CP"], [ck], K[:, 256:512], T.IDB[:], T.CP[:], False, True)
-        op("act", [ck], ["DZ" + z], T["DZ" + z][:], K[:, 256:512], F.Relu, bias=BIG, scale=-BIG)
-        if r:
-            op("act", ["DZ" + z], ["PM" + z], T["PM" + z][:, 0:255], T["DZ" + z][:, 1:256], F.Identity, bias=1.0 / 1024, scale=1.0 / BIG)
-        distances(p, r, n, T["LP%d" % r], pk)
-        mm(["IDB", "CK"], [kk], K[:, 0:256], T.IDB[:], T.CK[:], False, True)
-        one_hot(z, K[:, 0:256], kk, "DZ" + z, "SC" + z, "OF" + z, A.min)
-        mm(["OF" + z, "IDB"], ["PA:n"], T.PA[:, 0:128], T["OF" + z][:, 0:128], T.IDB[:], True, True)
-        op("tt", ["PA:n", pfk], ["SP" + y], T["SP" + y][:], T.PA[:, 0:128], PF[:, cs(n)], A.mult)
-        mm(["SP" + y, "BOF"], ["PA:c"], T.PA[:, 128:136], T["SP" + y][:], T.BOF[:, 0:128:16], True, True, w=4)
-        op("cp", ["PA:c"], ["CI" + y], T["CI" + y][:], T.PA[:, 128:136])
-        op("act", ["PA:c"], ["LB" + y], T["LB" + y][:], T.PA[:, 128:136], F.Identity, bias=63.5, scale=-1.0)
-        op("ts", ["CI" + y], ["CI" + y], T["CI" + y][:], T["CI" + y][:], 127, None, A.bitwise_and)
-        for j in range(8):
-            op("act", ["LB" + y, "IOL"], ["OL%s.%d" % (y, j)], T["OL" + y][:, j, :], T.IOL[:], F.Abs, bias=T["LB" + y][:, j:j + 1])
-        op("cp", ["CI" + y], ["CF" + y], T["CF" + y][:], T["CI" + y][:])
-        op("act", ["OL%s.%d" % (y, j) for j in range(8)], ["OM" + y], T["OM" + y][:], T["OL" + y][:], F.Relu, bias=64.5, scale=-1.0)
-        for j in range(8):
-            op("ts", ["CF" + y, "IOM"], ["OH%s.%d" % (y, j)], T["OH" + y][:, j, :], T.IOM[:], T["CF" + y][:, j:j + 1], None, A.is_equal, w=0.5)
-        for j in range(8):
-            mm(["OH%s.%d" % (y, j), "OM" + y], ["HI:h"], T.HI[:, j, 0:24], T["OH" + y][:, j, :], T["OM" + y][:, j, :], False, False)
-        if n == 2:
-            spread(r)
-        th, tc = "TH%d" % n, T.TH[:, 8 * n:8 * n + 8]
-        if r == 0:
-            O = "OF" + z
-            op("ts", ["SC" + z], [th], tc, T["SC" + z][:, 31:256:32], -15.0, None, A.max)
-        else:
-            O = "OK" + z
-            op("tt", [kk, "PM" + z, "PM%s.e" % z], ["AJ" + z], T["AJ" + z][:], K[:, 0:256], T["PM" + z][:], A.mult)
-            one_hot(z, T["AJ" + z][:], "AJ" + z, "RSK", "SK" + z, O, A.min)
-            op("ts", ["SK" + z], [th], tc, T["SK" + z][:, 31:256:32], -15.0 / 1024, 1024.0, A.max, A.mult)
-        mm([O, O + ".e", "IDB"], ["PB:n"], T.PB[:, 0:128], T[O][:, 1:129], T.IDB[:], True, True)
-        mm([O, "IDB"], ["PB:o"], T.PB[:, 384:512], T[O][:, 0:128], T.IDB[:], True, True)
-        op("tt", ["PB:n", pfk], ["SQ" + y], T["SQ" + y][:], T.PB[:, 0:128], PF[:, cs(n)], A.mult)
-        op("act", ["PB:o"], ["ONK.%d" % n], T.ONK[:, cs(n)], T.PB[:, 384:512], F.Copy)
-        mm(["SQ" + y, "BOF"], ["PB:r"], T.PB[:, 128:256], T["SQ" + y][:], T.BOF[:], True, True, w=4)
-        to_list(y)
-        op("cp", ["PL" + y, "PU"], ["CU.%d" % n], T.CU[:, cs(n)], T.PU[:, 0:W].indirect(T["PL" + y][:]), w=1.5)
-        op("cp", ["CU.%d" % n], ["CD.%d" % n], T.CD[:, cs(n)], T.CU[:, cs(n)])
-
-    def spread(r):
-        mm(["ZER", "ONE"], ["HI:h"], T.HI[:], T.ZER[:], T.ONE[:, 0:192], False, True)
-        pk, PK = "PK%d" % r, T.PK[:, 96 * r:96 * r + 96]
-        op("ts", ["HI:h"], ["FA"], T.FA[:], T.HI[:, :, 0:12], 1.0, None, A.min)
-        op("ts", ["HI:h"], ["FB"], T.FB[:], T.HI[:, :, 12:24], 1.0, 16.0, A.min, A.mult)
-        op("tt", ["FA", "FB"], [pk], PK, T.FA[:], T.FB[:], A.add)
-        s = send([pk], [RemoteDMATransfer(dst_ids=[to(c) for c in peers], dma_engine_mask=bits(efl), remote_sem=T.sem["fl%d" % r],
-                                          srcs=[PK], dsts=[T["FL%d" % r][:, rank, :] for c in peers])], len(efl))
-        arrives("fl%d" % r, 7 * len(efl), ["FL%d" % r], s, 6.0)
-
-    def cuts(r):
-        pk, fl, nc = "PK%d" % r, "FL%d" % r, "NC%d" % r
-        cnt = T.PA[0:96, 0:128]
-        others = [k for k in range(NR) if k != rank]
-        mm([pk, "IDB"], ["PA:n"], cnt, T.PK[:, 96 * r:96 * r + 96], T.IDB[:], True, False)
-        for k in others:
-            mm([fl, "IDB"], ["PA:n"], cnt, T[fl][:, k, :], T.IDB[:], False, k == others[-1])
-        op("cp", ["PA:n"], ["CNI"], T.CNI[0:96, :], cnt)
-        op("ts", ["PA:n"], [nc + ".1"], T[nc][0:96, 1, :], cnt, 47.5, 256.0, A.is_lt, A.mult)
-        op("ts", ["CNI"], ["CNI"], T.CNI[0:96, :], T.CNI[0:96, :], 15, None, A.bitwise_and)
-        op("ts", ["CNI"], [nc + ".0"], T[nc][0:96, 0, :], T.CNI[0:96, :], 2.5, 256.0, A.is_lt, A.mult)
-        banks = ("PB", "XR0", "XR1", "PA")
-        for q, j in enumerate((3, 4, 5, 0, 1, 2)):
-            bank, c = banks[q % len(banks)], slice(512 * j, 512 * j + 512)
-            keys = [bank + ":%d" % l for l in range(4)]
-            for l in range(4):
-                L = 4 * j + l
-                out = T[bank][:, 128 * l:128 * l + 128]
-                if UPD[q]:
-                    mm([TXK[j], "IDB"], [keys[l]], out, T.IDB[:], T.TX[:, 128 * L:128 * L + 128], True, False)
-                mm([nc + ".%d" % (L // 12), "EX"], [keys[l]], out, T.EX[0:96, 128 * (L % 12):128 * (L % 12) + 128],
-                   T[nc][0:96, L // 12, :], not UPD[q], True)
-            if UPD[q]:
-                op("act", keys, [TXK[j]], T.TX[:, c], T[bank][:], F.Relu, bias=-256.0)
+    def distances(p, r, step, q, lists, lkey):
+        y, a = "%d" % (p % 2), q // 2
+        K, M, XR, X, G = T["K" + y], T["M" + y], T["XR" + y], T.LX[:, cs(q, r)], T["G%d" % (p % NG)]
+        kk, mk, xr, xk, gk = "K%s:k" % y, "M%s." % y, "XR%s:x" % y, "LX%d.%d" % (r, q), "G%d." % (p % NG)
+        nc, nk = len(CH) - 1, 256 if step == 0 and r else 128
+        mm([xk, "XT"], [kk], K[v, 0:nk], X, T.XT[:, 0:nk], True, False)
+        for c in range(nc):
+            src = T["TX%d" % a][:, 0:W].indirect(lists[:, U * q + CH[c]:U * q + CH[c + 1]])
+            dst = G[:, 16 * CH[c]:16 * CH[c + 1]]
+            if (r, step, a, q % 2, c) in VG:
+                op("cp", txk(a) + [lkey], [gk + "%d" % c], dst, src, w=1.56)
             else:
-                op("tt", keys + [TXK[j]], [TXK[j]], T.TX[:, c], T.TX[:, c], T[bank][:], A.min)
+                op("act", txk(a) + [lkey], [gk + "%d" % c], dst, src, F.Copy, w=1.56)
+        gs = [gk + "%d" % c for c in range(nc)]
+        for k in range(16):
+            mm(gs + ["BG"], [kk], K[v, k:nk:16], G[:, k::16], T.BG[:, 0:nk // 16], False, False)
+        if step == 0 and r:
+            for k in range(16):
+                mm(gs + ["WK"], ["CF:f"], T.CF[v, k:128:16], G[:, k::16], T.WK[:, k, :], k == 0, k == 15)
+            op("act", ["CF:f"], ["FR" + y], T["FR" + y][v, :], T.CF[v, 0:128], F.Relu, bias=-245760.0)
+        for c in range(nc):
+            for j in range(4):
+                s = slice(16 * CH[c] + j, 16 * CH[c + 1], 4)
+                op("tt", [gk + "%d" % c, xr], [mk + "%d.%d" % (c, j)], M[:, s], G[:, s], XR[:, 4 * CH[c]:4 * CH[c + 1]], A.max)
+        for j in range(4):
+            for k in range(j, 16, 4):
+                mm([mk + "%d.%d" % (c, j) for c in range(nc)] + ["BM"], [kk], K[v, k:nk:16], M[:, k::16], T.BM[:, 0:nk // 16], False, False)
 
-    def second_half(r, n, p):
-        z, y, xk, x = "%d" % (p % 3), "%d" % (p % 2), "LX%d.%d" % (r, n), T["LX%d" % r][:, cs(n)]
-        PF, pfk, oxk, opk = T["PF%d" % (r % 2)], "PF%d.%d" % (r % 2, n), "OX%d.%d" % (r, n), "OP%d.%d" % (r, n)
-        K, kk = T["K" + z], "K%s:k" % z
-        distances(p, r, n, T.CU, "CU.%d" % n)
-        mm(["IDF", "TH%d" % n], [kk], K[:, 16:256:32], T.IDF[:], T.TH[:, 8 * n:8 * n + 8], False, False, w=4)
-        mm(["IDB", "CE"], [kk], K[:, 0:256], T.IDB[:], T.CE[:], False, True)
-        one_hot(z, K[:, 0:256], kk, "RSE", "SC" + z, "OF" + z, A.max)
-        mm(["OF" + z, "IDB"], ["PA:n"], T.PA[:, 0:128], T["OF" + z][:, 0:128], T.IDB[:], True, True)
-        op("tt", ["PA:n", "CD.%d" % n], ["SP" + y], T["SP" + y][:], T.PA[:, 0:128], T.CD[:, cs(n)], A.mult)
-        op("act", ["PA:n"], ["OB" + y], T["OB" + y][:], T.PA[:, 0:128], F.Copy)
-        mm(["SP" + y, "BOF"], ["PB:r"], T.PB[:, 128:256], T["SP" + y][:], T.BOF[:], True, True, w=4)
-        mm(["OB" + y, "BO"], ["PB:n"], T.PB[:, 0:128], T.BO[:], T["OB" + y][:], True, True)
-        mm(["SP" + y, "BOF"], ["PB:o"], T.PB[:, 384:512], T.BOF[:], T["SP" + y][:], True, False, w=4)
-        mm(["OB" + y, "BO4"], ["PB:o"], T.PB[:, 384:512], T.BO4[:], T["OB" + y][:], False, True)
-        to_list(y)
-        op("tt", ["PL" + y, xk] + TXK, ["DX" + y], T["DX" + y][:], T.TX[:, 0:W].indirect(T["PL" + y][:]), x, A.subtract)
-        op("tt", ["DX" + y, "PB:n"], ["DY" + y], T["DY" + y][:], T["DX" + y][:], T.PB[:, 0:128], A.mult)
-        mm([xk, "IDB"], ["PA:x"], T.PA[:, 128:256], T.IDB[:], x, True, False)
-        mm(["DY" + y, "IDH"], ["PA:x"], T.PA[:, 128:256], T.IDH[:], T["DY" + y][:], False, True)
-        op("act", ["PA:x"], [oxk], T.OX[:, cs(n, r)], T.PA[:, 128:256], F.Identity, bias=-0.2)
-        op("tt", ["ONK.%d" % n, "PB:o"], ["UU" + y], T["UU" + y][:], T.ONK[:, cs(n)], T.PB[:, 384:512], A.mult)
-        op("tt", ["UU" + y, pfk], ["WI" + y], T["WI" + y][:], PF[:, cs(n)], T["UU" + y][:], A.max)
-        op("ts", ["WI" + y], ["WI" + y], T["WI" + y][:], T["WI" + y][:], 4095, None, A.bitwise_and)
-        if r < RO - 1:
-            op("cp", ["WI" + y], [opk], T.OP[:, cs(n, r)], T["WI" + y][:])
-            sem = T.sem["a%d%d" % (r, n)]
-            s = send([oxk, opk], [
-                RemoteDMATransfer(dst_ids=[to(nxt)], dma_engine_mask=bits(es), remote_sem=sem, src=T[o][:, cs(n, r)],
-                                  dst=T["%s%d" % (l, r + 1)][:, cs(n)])
-                for es, o, l in ((enx[:hn], "OP", "LP"), (enx[hn:], "OX", "LX"))], 2 * hn)
-            arrives("a%d%d" % (r, n), 2 * hn, ["LP%d.%d" % (r + 1, n), "LX%d.%d" % (r + 1, n)], s, 4.0)
+    def repeat(p, r, q):
+        y = "%d" % (p % 2)
+        XR, xr, xk = T["XR" + y], "XR%s:x" % y, "LX%d.%d" % (r, q)
+        mm(["ONE", "CX"], [xr], XR[:, 0:384], T.ONE[0:1, 0:128], T.CX[0:1, :], True, False)
+        for j in range(4):
+            mm(["IDB", xk], [xr], XR[:, j:384:4], T.IDB[:], T.LX[:, cs(q, r)], False, j == 3)
+
+    def one_hot(K, kk, s1, s2, Z, zk, O, ok, limit=None):
+        if limit is None:
+            op("scan", [kk, "RS"], [s1], T[s1][v, :], T.RS[v, :], K, 0.0, A.add, A.min)
+            op("cp", [s1], [zk], Z[0], T[s1][v, 15:128:16])
         else:
-            op("cp", ["WI" + y], ["YP.%d" % n], T.YP[:, cs(n)], T["WI" + y][:])
-            op("act", [oxk], ["YX.%d" % n], T.YX[:, cs(n)], T.OX[:, cs(n, r)], F.Identity, bias=-128.0)
-            dma("y", ["YP.%d" % n], [], "d%d" % (6 + n), T.yp[:, cs(n)], T.YP[:, cs(n)])
-            dma("y", ["YX.%d" % n], [], "d%d" % (9 + n), T.yx[:, cs(n)], T.YX[:, cs(n)])
+            op("scan", [kk, "RE"], [s1], T[s1][v, :], T.RE[v, :], K, 0.0, A.min, A.max)
+            op("tt", [s1, limit[1]], [zk], Z[0], T[s1][v, 15:128:16], limit[0], A.max)
+        op("scan", [zk, "KP"], [s2], T[s2][v, :], T.KP[v, :], Z[1], 0.0, A.mult, A.add)
+        op("tt", [kk, s2], [ok], O, K, T[s2][v, :], A.is_equal)
+
+    def to_list(bank, src, pl):
+        for j in range(16):
+            mm([src, "EE"], [bank + ":l"], T[bank][:, 96:102], T.EE[:, 15 - j:143 - j], T[src][:, j::16], j == 0, j == 15)
+        op("ts", [bank + ":l"], [pl], T[pl][:, 0:6], T[bank][:, 96:102], OFF, None, A.add)
+
+    def first_half(r, q, p):
+        y, a = "%d" % (p % 2), q // 2
+        PF, pfk, lk = T.PF[:, cs(q, r)], "PF%d.%d" % (r, q), "LP.%d" % q
+        K, kk, XR, c0 = T["K" + y], "K%s:k" % y, T["XR" + y], V * r + U * q
+        if r:
+            op("ts", [pfk], [lk], T.LP[:, cs(q)], PF, OFF, None, A.add, w=0.5)
+        repeat(p, r, q)
+        op("tt", [pfk], ["DF" + y], T["DF" + y][:], T.PF[:, c0:c0 + U:2], T.PF[:, c0 + 1:c0 + U:2], A.not_equal)
+        for j in range(2):
+            mm(["DF" + y, "TRI"], ["XR%s:n" % y], XR[:, 384 + j:480:2], T.TRI[:], T["DF" + y][:], j == 0, j == 1)
+        op("act", ["XR%s:n" % y, "ZB"], ["ZZ" + y], T["ZZ" + y][:], XR[:, 384:480], F.Relu, bias=T.ZB[:, 0:1], scale=-1.0)
+        distances(p, r, 0, q, T.LP, lk)
+        nk = 256 if r else 128
+        if r:
+            mm(["FR" + y, "IDN"], [kk], K[v, 128:256], T.IDN[v, v], T["FR" + y][v, :], False, False)
+        mm(["ZZ" + y, "IDZ"], [kk], K[v, 0:nk], T["ZZ" + y][:], T.IDZ[:, 0:nk], False, False)
+        mm(["ONE", "CK"], [kk], K[v, 0:nk], T.ONE[0:33, v], T.CK[0:33, 0:nk], False, True)
+        ZK, OK, zk, ok = (T.ZK[v, q, 0:128:16], T.ZK[v, q, :]), T.OK[v, q, 0:128], "ZK.%d" % q, "OK.%d" % q
+        if r:
+            O, o = T["OF" + y][v, :], "OF" + y
+            one_hot(K[v, 0:128], kk, "S1" + y, "S2" + y, (T["ZF" + y][v, 0:128:16], T["ZF" + y][v, :]), "ZF" + y, O, o)
+        else:
+            O, o = OK, ok
+            one_hot(K[v, 0:128], kk, "S1" + y, "S2" + y, ZK, zk, O, o)
+        sp = "SP" + y
+        mm([o, "IDB"], ["PA:t"], T.PA[:, v], O, I96, True, True)
+        op("tt", ["PA:t", pfk], [sp], T[sp][:], T.PA[:, v], PF, A.mult)
+        mm([sp, "BP"], ["PA:n"], T.PA[v, 96:104], T[sp][:], T.BP[:, 0:128:16], True, True)
+        mm(["ONE", "CT"], ["PA:s"], T.PA[v, 128:328], T.ONE[0:33, v], T.CT[0:33], True, False)
+        mm([sp, "TB"], ["PA:s"], T.PA[v, 128:328], T[sp][:], T.TB[:], False, True)
+        op("act", ["PA:n"], ["HH" + y], T["HH" + y][v, :], T.PA[v, 96:104], F.Identity, bias=OFF + 16512.0 - 63.5)
+        op("act", ["PA:n"], ["NN" + y], T["NN" + y][v, :], T.PA[v, 96:104], F.Identity, bias=OFF + 16512.0)
+        op("act", ["PA:s"], ["TM" + y], T["TM" + y][v], T.PA[v, 128:328], F.Sign)
+        if q % 2 == 0:
+            mm(["ZER", "ONE"], ["HI:h"], T.HI[:], T.ZER[:], T.ONE[:, 0:96], True, False)
+        op("tt", ["HH" + y, "NN" + y], ["NN" + y], T["NN" + y][v, :], T["NN" + y][v, :], T["HH" + y][v, :], A.subtract)
+        for j in range(8):
+            op("ts", ["NN" + y, "IOM"], ["OH%s.%d" % (y, j)], T["OH" + y][v, j, :], T.IOM[v, :], T["NN" + y][v, j:j + 1], None,
+               A.is_equal, w=0.5)
+            for d in range(2):
+                mm(["OH%s.%d" % (y, j), "TM" + y], ["HI:h"], T.HI[:, j % 4, :], T["OH" + y][v, j, :], T["TM" + y][v, j, d:d + 24],
+                   False, q % 2 == 1 and j == 7 and d == 1)
+        if q % 2:
+            spread(2 * r + a)
+        if r:
+            one_hot(K[v, 128:256], kk, "S3" + y, "S4" + y, ZK, zk, OK, ok)
+        mm([ok, "OK.e", "IDB"], ["PB:t"], T.PB[:, v], T.OK[v, q, 1:129], I96, True, True)
+        op("tt", ["PB:t", pfk], ["SQ" + y], T["SQ" + y][:], T.PB[:, v], PF, A.mult)
+        to_list("PB", "SQ" + y, "PM" + y)
+        op("cp", ["PM" + y, "PU%d.0" % a, "PU%d.1" % a], ["CU.%d" % q], T.CU[:, cs(q)], T["PU%d" % a][:, 0:W].indirect(T["PM" + y][:, 0:6]), w=1.9)
+        op("ts", ["CU.%d" % q], ["CD.%d" % q], T.CD[:, cs(q)], T.CU[:, cs(q)], -OFF, None, A.add, w=0.5)
+        if r == RO - 1:
+            op("ts", [pfk], ["YP.%d" % q], T.YP[:, cs(q)], PF, OFF, None, A.add)
+
+    def spread(m):
+        fs, FS = "FS%d" % m, T.FS[:, m, :]
+        op("ts", ["HI:h"], [fs], FS, T.HI[:], 0.0, None, A.not_equal)
+        s = send([fs], [RemoteDMATransfer(dst_ids=[to(c) for c in peers], dma_engine_mask=bits(efl), remote_sem=T.sem["fl%d" % m],
+                                          srcs=[FS], dsts=[T.FL[:, m, rank, :] for c in peers])], len(efl))
+        arrives("fl%d" % m, 7 * len(efl), ["FL%d" % m], s, 7.0)
+
+    def cuts(r, a):
+        m = 2 * r + a
+        cnt, a0, A0 = T.CF[v, 128:256], "A0.%d" % a, T.A0[v, a, :]
+        others = [k for k in range(NR) if k != rank]
+        mm(["ONE", "CY"], ["CF:c"], cnt, T.ONE[0:1, v], T.CY[0:1, :], True, False)
+        mm(["FS%d" % m, "ID4"], ["CF:c"], cnt, T.FS[:, m, :], T.ID4[:], False, False)
+        for k in others:
+            mm(["FL%d" % m, "ID4"], ["CF:c"], cnt, T.FL[:, m, k, :], T.ID4[:], False, k == others[-1])
+        op("tt", ["CF:c", a0], [a0], A0, cnt, A0, A.max)
+        op("ts", [a0], [a0], A0, A0, CUT, None, A.min, w=0.5)
+        for j in range(2):
+            dma("y", [a0], ["TX%d.%d" % (a, j)], T["TX%d" % a][64 * j:64 * j + 64:16, :], A0)
+        if r == RO - 1:
+            op("ts", [a0], ["YC%d" % a], T.YC[v, a, :], A0, 2000.0, None, A.is_ge)
+            dma("y", ["YC%d" % a], [], T.yc[4 * a:4 * a + 4, :], T.YC[v, a, :])
+
+    def second_half(r, q, p):
+        y, a, xk, x = "%d" % (p % 2), q // 2, "LX%d.%d" % (r, q), T.LX[:, cs(q, r)]
+        PF, pfk, oxk, opk = T.PF[:, cs(q, r)], "PF%d.%d" % (r, q), "OX%d.%d" % (r, q), "OP%d.%d" % (r, q)
+        K, kk = T["K" + y], "K%s:k" % y
+        O, o, sp, ob, ot = T["OF" + y][v, :], "OF" + y, "SP" + y, "OB" + y, "OT" + y
+        repeat(p, r, q)
+        distances(p, r, 1, q, T.CU, "CU.%d" % q)
+        mm(["ONE", "CE"], [kk], K[v, 0:128], T.ONE[0:33, v], T.CE[0:33, :], False, True)
+        one_hot(K[v, 0:128], kk, "S1" + y, "S2" + y, (T["ZF" + y][v, 0:128:16], T["ZF" + y][v, :]), "ZF" + y, O, o,
+                limit=(T.ZK[v, q, 0:128:16], "ZK.%d" % q))
+        mm([o, "IDB"], ["PA:t"], T.PA[:, v], O, I96, True, True)
+        mm([o, "IDB"], ["PB:t"], T.PB[:, v], O, I96, True, True)
+        op("tt", ["PA:t", "CD.%d" % q], [sp], T[sp][:], T.PA[:, v], T.CD[:, cs(q)], A.mult)
+        op("act", ["PB:t"], [ob], T[ob][:], T.PB[:, v], F.Copy)
+        for j in range(16):
+            mm([sp, "EE"], ["PA:l"], T.PA[:, 96:102], T.EE[:, 15 - j:143 - j], T[sp][:, j::16], j == 0, j == 15)
+        mm([ob, "BO"], ["PA:k"], T.PA[:, 128:224], T.BO[:], T[ob][:], True, True)
+        mm([pfk, "IDP"], ["PA:d"], T.PA[:, 256:352], T.IDP[:], PF, True, False)
+        mm([sp, "BP"], ["PA:d"], T.PA[:, 256:352], T.BP[:], T[sp][:], False, True)
+        mm(["OK.%d" % q, "IDB"], ["PB:o"], T.PB[:, 128:224], T.OK[v, q, 0:128], I96, True, False)
+        mm([ob, "BO"], ["PB:o"], T.PB[:, 128:224], T.BO[:], T[ob][:], False, True)
+        op("act", ["PB:o"], [ot], T[ot][:], T.PB[:, 128:224], F.Relu, bias=-1.0)
+        op("ts", ["PA:l"], ["PL" + y], T["PL" + y][:, 0:6], T.PA[:, 96:102], OFF, None, A.add)
+        op("tt", ["PL" + y, xk] + txk(a), ["DX" + y], T["DX" + y][:], T["TX%d" % a][:, 0:W].indirect(T["PL" + y][:, 0:6]), x,
+           A.subtract, w=1.9)
+        op("tt", ["DX" + y, "PA:k"], ["DY" + y], T["DY" + y][:], T["DX" + y][:], T.PA[:, 128:224], A.mult)
+        mm([xk, "IDB"], ["PB:x"], T.PB[:, 256:352], T.IDB[:], x, True, False)
+        mm([ob, "B64"], ["PB:x"], T.PB[:, 256:352], T.B64[:], T[ob][:], False, False)
+        mm(["DY" + y, "IDH"], ["PB:x"], T.PB[:, 256:352], T.IDH[:], T["DY" + y][:], False, True)
+        op("act", ["PB:x"], [oxk], T.OX[:, cs(q, r)], T.PB[:, 256:352], F.Identity, bias=-0.2)
+        op("tt", ["PA:d", ot], ["PA:d"], T.PA[:, 256:352], T.PA[:, 256:352], T[ot][:], A.mult)
+        if r < RO - 1:
+            op("tt", ["PA:d", pfk], [opk], T.OP[:, cs(q, r)], T.PA[:, 256:352], PF, A.add)
+            sem = T.sem["a%d%d" % (r, q)]
+            s = send([oxk, opk], [
+                RemoteDMATransfer(dst_ids=[to(nxt)], dma_engine_mask=bits(es), remote_sem=sem, src=T[o][:, cs(q, r)],
+                                  dst=T[l][:, cs(q, r + 1)])
+                for es, o, l in ((enx[:hn], "OP", "PF"), (enx[hn:], "OX", "LX"))], 2 * hn)
+            arrives("a%d%d" % (r, q), 2 * hn, ["PF%d.%d" % (r + 1, q), "LX%d.%d" % (r + 1, q)], s, 3.5)
+        else:
+            op("tt", ["PA:d", "YP.%d" % q], ["YP.%d" % q], T.YP[:, cs(q)], T.PA[:, 256:352], T.YP[:, cs(q)], A.add)
+            op("act", [oxk], ["YX.%d" % q], T.YX[:, cs(q)], T.OX[:, cs(q, r)], F.Identity, bias=-128.0)
+            for j in range(2):
+                c = slice(H * j + U * (q % 2), H * j + U * (q % 2) + U)
+                dma("y", ["YP.%d" % q], [], T.yp[64 * a:64 * a + 64, c], T.YP[64 * j:64 * j + 64, cs(q)])
+                dma("y", ["YX.%d" % q], [], T.yx[64 * a:64 * a + 64, c], T.YX[64 * j:64 * j + 64, cs(q)])
 
     for r in range(RO):
-        p = 6 * r
-        mm(["ZER", "ONE"], ["HI:h"], T.HI[:], T.ZER[:], T.ONE[:, 0:192], True, False)
-        for n in range(3):
-            first_half(r, n, p + n)
-        cuts(r)
-        for n in range(3):
-            second_half(r, n, p + 3 + n)
-        if r == RO - 1:
-            k = ["NC%d.%d" % (q, j) for q in range(RO) for j in range(2)]
-            op("tt", k[0:4], ["YCA"], T.YCA[0:96], T.NC0[0:96], T.NC1[0:96], A.min)
-            op("tt", ["YCA"] + k[4:6], ["YCA"], T.YCA[0:96], T.YCA[0:96], T.NC2[0:96], A.min)
-            op("ts", ["YCA"], ["YC"], T.YC[0:96], T.YCA[0:96], 128.0, None, A.is_lt)
-            for j in range(2):
-                dma("y", ["YC"], [], "d%d" % (12 + j), T.yc[:, 1536 * j:1536 * j + 1536], T.YC[0:96, j, :])
+        for q in range(4):
+            first_half(r, q, 8 * r + q)
+        for q in range(4):
+            if q % 2 == 0:
+                cuts(r, q // 2)
+            second_half(r, q, 8 * r + 4 + q)
     finish()

@@ -8,6 +8,10 @@ U, H = 96, 192
 BIG = 16777216.0
 OFF = 1536.0
 CUT = 2176.0
+GA = 1.56
+XL = (1.8, 0.4, 2.2)
+WAKE = 0.25
+TURNS = 4
 NG = 3
 CH = (0, 64, 96)
 VG = set()
@@ -32,8 +36,8 @@ for n, s in TWO.items():
 SCRATCH = {n: ("sbuf", [128] + list(s[1:]), s[0]) for n, s in SB.items()}
 BANKS = {"XR0": [512], "XR1": [512], "K0": [512], "K1": [512], "PA": [512], "PB": [512], "HI": [4, 24], "CF": [512]}
 SCRATCH.update({n: ("psum", [128] + s, f) for n, s in BANKS.items()})
-SEMAPHORES = ["cv", "cs", "cp", "cg", "loc"] + ["d%d" % n for n in range(56)] + ["fl%d" % n for n in range(2 * RO)] + \
-    ["a%d%d" % (s, n) for s in range(RO - 1) for n in range(4)]
+SEMAPHORES = ["cv", "cs", "cp", "cg", "loc"] + ["d%d" % n for n in range(56)] + ["fl%d%d" % (n, k) for n in range(2 * RO) for k in range(NR)] + \
+    ["%s%d%d" % (o, s, n) for o in ("OP", "OX") for s in range(RO - 1) for n in range(4)]
 
 
 def make_plan(g, T):
@@ -42,7 +46,7 @@ def make_plan(g, T):
     wr, rd, touch, last = {}, {}, {}, {}
     nd = [0]
 
-    def add(e, reads, writes, emit, sem, inc, cost, acc=False, lag=0.08, own=True, after=()):
+    def add(e, reads, writes, emit, sem, inc, cost, acc=False, lag=WAKE, own=True, after=()):
         deps, me = set(after), len(nodes)
         bks = sorted(set(k.split(":")[0] for k in list(reads) + list(writes) if k.split(":")[0] in BANKS))
         for bk in bks:
@@ -82,13 +86,13 @@ def make_plan(g, T):
         for s in out.shape[1:]:
             n *= int(s)
         if e == "p":
-            cost = 0.0005 * max(64, n) * w
+            cost = 0.00042 * max(64, n) * w
         elif e == "g":
-            cost = 0.15 + 0.002 * n
+            cost = 0.15 + 0.0017 * n
         else:
             if name == "tt" and w == 1.0 and not any(k.split(":")[0] in BANKS for k in reads):
                 w = 2.0
-            cost = 0.03 + 0.001 * max(64, n * w)
+            cost = 0.03 + 0.00085 * max(40, n * w)
         return add(e, reads, writes, lambda: fn(out, *args, **kw), "c" + e, 1, cost, acc=acc)
 
     def dma(e, reads, writes, out, in_, lag=2.3):
@@ -108,37 +112,42 @@ def make_plan(g, T):
             x["all"] = sorted(set(x["deps"] + ([x["prev"]] if "prev" in x else [])))
             for d in x["all"]:
                 succ[d].append(k)
+
+        def gap(d, k):
+            return 0.0 if nodes[k].get("prev") == d else nodes[d]["lag"]
+
+        def place(seq, before, wait, first):
+            start, busy = [0.0] * n, {e: [] for e in eng}
+            for k in seq:
+                x = nodes[k]
+                t = max([start[d] + nodes[d]["cost"] + wait(d, k) for d in before[k]] + [first(k)])
+                if x["e"] != "x":
+                    lst = busy[x["e"]]
+                    j = len(lst)
+                    while j and lst[j - 1][1] > t:
+                        j -= 1
+                    while j < len(lst) and lst[j][0] < t + x["cost"]:
+                        t = max(t, lst[j][1])
+                        j += 1
+                    lst.insert(j, (t, t + x["cost"]))
+                start[k] = t
+            return start
+
+        pred = [x["all"] for x in nodes]
         prio = [0.0] * n
         for k in range(n - 1, -1, -1):
-            x = nodes[k]
-            prio[k] = x["cost"] + max([prio[s] + (0.0 if nodes[s].get("prev") == k else x["lag"]) for s in succ[k]] + [x["lag"]])
-        left = [len(x["all"]) for x in nodes]
-        ready = {e: [] for e in "vspgyx"}
-        free = {e: 0.0 for e in "vspgyx"}
-        start = [0.0] * n
-        for k in range(n):
-            if not left[k]:
-                ready[nodes[k]["e"]].append(k)
-        order = []
-        while len(order) < n:
-            best = None
-            for e, lst in ready.items():
-                if lst:
-                    t = min(start[k] for k in lst)
-                    t = t if e == "x" else max(free[e], t)
-                    if best is None or t < best[0]:
-                        best = (t, e)
-            t, e = best
-            k = max((k for k in ready[e] if start[k] <= t + 1e-9), key=lambda k: (prio[k], -k))
-            ready[e].remove(k)
-            order.append(k)
-            x = nodes[k]
-            free[e] = t + x["cost"]
-            for s in succ[k]:
-                start[s] = max(start[s], t + x["cost"] + (0.0 if nodes[s].get("prev") == k else x["lag"]))
-                left[s] -= 1
-                if not left[s]:
-                    ready[nodes[s]["e"]].append(s)
+            prio[k] = nodes[k]["cost"] + max([prio[s] + gap(k, s) for s in succ[k]] + [nodes[k]["lag"]])
+        best = None
+        for turn in range(TURNS):
+            start = place(sorted(range(n), key=lambda k: (-prio[k], k)), pred, gap, lambda k: 0.0)
+            end = [start[k] + nodes[k]["cost"] for k in range(n)]
+            span = max(end[k] + nodes[k]["lag"] for k in range(n))
+            if best is None or span < best[0]:
+                best = (span, start)
+            back = place(sorted(range(n), key=lambda k: (-end[k], -k)), succ, lambda d, k: gap(k, d), lambda k: nodes[k]["lag"])
+            prio = [back[k] + nodes[k]["cost"] for k in range(n)]
+        start = best[1]
+        order = sorted(range(n), key=lambda k: (start[k], k))
         cnt, known, event, clock = {}, {e: {} for e in eng}, {}, {}
         for k in order:
             x = nodes[k]
@@ -176,11 +185,10 @@ def rank_program(g, core, T, topo):
     if rank is None:
         return
     op, dma, send, arrives, finish = make_plan(g, T)
-    peers = [c for c in T.cores if c != core]
+    peers = [T.cores[(rank + d) % NR] for d in range(1, NR)]
     nxt = T.cores[(rank + STEP) % NR]
     efl = [e for e in topo.engines(core, peers[0]) if all(e in topo.engines(core, c) for c in peers)]
     enx = topo.engines(core, nxt)
-    hn = len(enx) // 2
 
     def to(c):
         return DstId(rid=topo.addr(c)[0], pnc=topo.addr(c)[1])
@@ -274,9 +282,9 @@ def rank_program(g, core, T, topo):
             src = T["TX%d" % a][:, 0:W].indirect(lists[:, U * q + CH[c]:U * q + CH[c + 1]])
             dst = G[:, 16 * CH[c]:16 * CH[c + 1]]
             if (r, step, a, q % 2, c) in VG:
-                op("cp", txk(a) + [lkey], [gk + "%d" % c], dst, src, w=1.56)
+                op("cp", txk(a) + [lkey], [gk + "%d" % c], dst, src, w=GA)
             else:
-                op("act", txk(a) + [lkey], [gk + "%d" % c], dst, src, F.Copy, w=1.56)
+                op("act", txk(a) + [lkey], [gk + "%d" % c], dst, src, F.Copy, w=GA)
         gs = [gk + "%d" % c for c in range(nc)]
         for k in range(16):
             mm(gs + ["BG"], [kk], K[v, k:nk:16], G[:, k::16], T.BG[:, 0:nk // 16], False, False)
@@ -288,9 +296,15 @@ def rank_program(g, core, T, topo):
             for j in range(4):
                 s = slice(16 * CH[c] + j, 16 * CH[c + 1], 4)
                 op("tt", [gk + "%d" % c, xr], [mk + "%d.%d" % (c, j)], M[:, s], G[:, s], XR[:, 4 * CH[c]:4 * CH[c + 1]], A.max)
+        ck = "CE" if step else "CK"
+        mm(["ONE", ck], [kk], K[v, 0:nk], T.ONE[0:33, v], T[ck][0:33, 0:nk], False, False)
         for j in range(4):
+            if j == 3 and step == 0:
+                mm(["ZZ" + y, "IDZ"], [kk], K[v, 0:nk], T["ZZ" + y][:], T.IDZ[:, 0:nk], False, False)
+                if r:
+                    mm(["FR" + y, "IDN"], [kk], K[v, 128:256], T.IDN[v, v], T["FR" + y][v, :], False, False)
             for k in range(j, 16, 4):
-                mm([mk + "%d.%d" % (c, j) for c in range(nc)] + ["BM"], [kk], K[v, k:nk:16], M[:, k::16], T.BM[:, 0:nk // 16], False, False)
+                mm([mk + "%d.%d" % (c, j) for c in range(nc)] + ["BM"], [kk], K[v, k:nk:16], M[:, k::16], T.BM[:, 0:nk // 16], False, k == 15)
 
     def repeat(p, r, q):
         y = "%d" % (p % 2)
@@ -317,20 +331,15 @@ def rank_program(g, core, T, topo):
     def first_half(r, q, p):
         y, a = "%d" % (p % 2), q // 2
         PF, pfk, lk = T.PF[:, cs(q, r)], "PF%d.%d" % (r, q), "LP.%d" % q
-        K, kk, XR, c0 = T["K" + y], "K%s:k" % y, T["XR" + y], V * r + U * q
+        K, kk, c0 = T["K" + y], "K%s:k" % y, V * r + U * q
         if r:
             op("ts", [pfk], [lk], T.LP[:, cs(q)], PF, OFF, None, A.add, w=0.5)
         repeat(p, r, q)
         op("tt", [pfk], ["DF" + y], T["DF" + y][:], T.PF[:, c0:c0 + U:2], T.PF[:, c0 + 1:c0 + U:2], A.not_equal)
         for j in range(2):
-            mm(["DF" + y, "TRI"], ["XR%s:n" % y], XR[:, 384 + j:480:2], T.TRI[:], T["DF" + y][:], j == 0, j == 1)
-        op("act", ["XR%s:n" % y, "ZB"], ["ZZ" + y], T["ZZ" + y][:], XR[:, 384:480], F.Relu, bias=T.ZB[:, 0:1], scale=-1.0)
+            mm(["DF" + y, "TRI"], ["CF:n"], T.CF[:, 256 + j:352:2], T.TRI[:], T["DF" + y][:], j == 0, j == 1)
+        op("act", ["CF:n", "ZB"], ["ZZ" + y], T["ZZ" + y][:], T.CF[:, 256:352], F.Relu, bias=T.ZB[:, 0:1], scale=-1.0)
         distances(p, r, 0, q, T.LP, lk)
-        nk = 256 if r else 128
-        if r:
-            mm(["FR" + y, "IDN"], [kk], K[v, 128:256], T.IDN[v, v], T["FR" + y][v, :], False, False)
-        mm(["ZZ" + y, "IDZ"], [kk], K[v, 0:nk], T["ZZ" + y][:], T.IDZ[:, 0:nk], False, False)
-        mm(["ONE", "CK"], [kk], K[v, 0:nk], T.ONE[0:33, v], T.CK[0:33, 0:nk], False, True)
         ZK, OK, zk, ok = (T.ZK[v, q, 0:128:16], T.ZK[v, q, :]), T.OK[v, q, 0:128], "ZK.%d" % q, "OK.%d" % q
         if r:
             O, o = T["OF" + y][v, :], "OF" + y
@@ -344,15 +353,14 @@ def rank_program(g, core, T, topo):
         mm([sp, "BP"], ["PA:n"], T.PA[v, 96:104], T[sp][:], T.BP[:, 0:128:16], True, True)
         mm(["ONE", "CT"], ["PA:s"], T.PA[v, 128:328], T.ONE[0:33, v], T.CT[0:33], True, False)
         mm([sp, "TB"], ["PA:s"], T.PA[v, 128:328], T[sp][:], T.TB[:], False, True)
-        op("act", ["PA:n"], ["HH" + y], T["HH" + y][v, :], T.PA[v, 96:104], F.Identity, bias=OFF + 16512.0 - 63.5)
-        op("act", ["PA:n"], ["NN" + y], T["NN" + y][v, :], T.PA[v, 96:104], F.Identity, bias=OFF + 16512.0)
+        op("ts", ["PA:n"], ["HH" + y], T["HH" + y][v, :], T.PA[v, 96:104], OFF + 16512.0 - 63.5, None, A.add)
+        op("tt", ["PA:n", "HH" + y], ["NN" + y], T["NN" + y][v, :], T.PA[v, 96:104], T["HH" + y][v, :], A.subtract)
         op("act", ["PA:s"], ["TM" + y], T["TM" + y][v], T.PA[v, 128:328], F.Sign)
         if q % 2 == 0:
             mm(["ZER", "ONE"], ["HI:h"], T.HI[:], T.ZER[:], T.ONE[:, 0:96], True, False)
-        op("tt", ["HH" + y, "NN" + y], ["NN" + y], T["NN" + y][v, :], T["NN" + y][v, :], T["HH" + y][v, :], A.subtract)
         for j in range(8):
-            op("ts", ["NN" + y, "IOM"], ["OH%s.%d" % (y, j)], T["OH" + y][v, j, :], T.IOM[v, :], T["NN" + y][v, j:j + 1], None,
-               A.is_equal, w=0.5)
+            op("ts", ["NN" + y, "IOM"], ["OH%s.%d" % (y, j)], T["OH" + y][v, j, :], T.IOM[v, :], -OFF - 16512.0,
+               T["NN" + y][v, j:j + 1], A.add, A.is_equal, w=0.5)
             for d in range(2):
                 mm(["OH%s.%d" % (y, j), "TM" + y], ["HI:h"], T.HI[:, j % 4, :], T["OH" + y][v, j, :], T["TM" + y][v, j, d:d + 24],
                    False, q % 2 == 1 and j == 7 and d == 1)
@@ -363,7 +371,7 @@ def rank_program(g, core, T, topo):
         mm([ok, "OK.e", "IDB"], ["PB:t"], T.PB[:, v], T.OK[v, q, 1:129], I96, True, True)
         op("tt", ["PB:t", pfk], ["SQ" + y], T["SQ" + y][:], T.PB[:, v], PF, A.mult)
         to_list("PB", "SQ" + y, "PM" + y)
-        op("cp", ["PM" + y, "PU%d.0" % a, "PU%d.1" % a], ["CU.%d" % q], T.CU[:, cs(q)], T["PU%d" % a][:, 0:W].indirect(T["PM" + y][:, 0:6]), w=1.9)
+        op("cp", ["PM" + y, "PU%d.0" % a, "PU%d.1" % a], ["CU.%d" % q], T.CU[:, cs(q)], T["PU%d" % a][:, 0:W].indirect(T["PM" + y][:, 0:6]), w=GA)
         op("ts", ["CU.%d" % q], ["CD.%d" % q], T.CD[:, cs(q)], T.CU[:, cs(q)], -OFF, None, A.add, w=0.5)
         if r == RO - 1:
             op("ts", [pfk], ["YP.%d" % q], T.YP[:, cs(q)], PF, OFF, None, A.add)
@@ -371,18 +379,20 @@ def rank_program(g, core, T, topo):
     def spread(m):
         fs, FS = "FS%d" % m, T.FS[:, m, :]
         op("ts", ["HI:h"], [fs], FS, T.HI[:], 0.0, None, A.not_equal)
-        s = send([fs], [RemoteDMATransfer(dst_ids=[to(c) for c in peers], dma_engine_mask=bits(efl), remote_sem=T.sem["fl%d" % m],
+        s = send([fs], [RemoteDMATransfer(dst_ids=[to(c) for c in peers], dma_engine_mask=bits(efl), remote_sem=T.sem["fl%d%d" % (m, rank)],
                                           srcs=[FS], dsts=[T.FL[:, m, rank, :] for c in peers])], len(efl))
-        arrives("fl%d" % m, 7 * len(efl), ["FL%d" % m], s, 7.0)
+        for d in range(1, NR):
+            k = (rank - d) % NR
+            arrives("fl%d%d" % (m, k), len(efl), ["FL%d.%d" % (m, k)], s, XL[0] + XL[1] * d)
 
     def cuts(r, a):
         m = 2 * r + a
         cnt, a0, A0 = T.CF[v, 128:256], "A0.%d" % a, T.A0[v, a, :]
-        others = [k for k in range(NR) if k != rank]
+        others = [(rank - d) % NR for d in range(1, NR)]
         mm(["ONE", "CY"], ["CF:c"], cnt, T.ONE[0:1, v], T.CY[0:1, :], True, False)
         mm(["FS%d" % m, "ID4"], ["CF:c"], cnt, T.FS[:, m, :], T.ID4[:], False, False)
         for k in others:
-            mm(["FL%d" % m, "ID4"], ["CF:c"], cnt, T.FL[:, m, k, :], T.ID4[:], False, k == others[-1])
+            mm(["FL%d.%d" % (m, k), "ID4"], ["CF:c"], cnt, T.FL[:, m, k, :], T.ID4[:], False, k == others[-1])
         op("tt", ["CF:c", a0], [a0], A0, cnt, A0, A.max)
         op("ts", [a0], [a0], A0, A0, CUT, None, A.min, w=0.5)
         for j in range(2):
@@ -398,7 +408,6 @@ def rank_program(g, core, T, topo):
         O, o, sp, ob, ot = T["OF" + y][v, :], "OF" + y, "SP" + y, "OB" + y, "OT" + y
         repeat(p, r, q)
         distances(p, r, 1, q, T.CU, "CU.%d" % q)
-        mm(["ONE", "CE"], [kk], K[v, 0:128], T.ONE[0:33, v], T.CE[0:33, :], False, True)
         one_hot(K[v, 0:128], kk, "S1" + y, "S2" + y, (T["ZF" + y][v, 0:128:16], T["ZF" + y][v, :]), "ZF" + y, O, o,
                 limit=(T.ZK[v, q, 0:128:16], "ZK.%d" % q))
         mm([o, "IDB"], ["PA:t"], T.PA[:, v], O, I96, True, True)
@@ -415,7 +424,7 @@ def rank_program(g, core, T, topo):
         op("act", ["PB:o"], [ot], T[ot][:], T.PB[:, 128:224], F.Relu, bias=-1.0)
         op("ts", ["PA:l"], ["PL" + y], T["PL" + y][:, 0:6], T.PA[:, 96:102], OFF, None, A.add)
         op("tt", ["PL" + y, xk] + txk(a), ["DX" + y], T["DX" + y][:], T["TX%d" % a][:, 0:W].indirect(T["PL" + y][:, 0:6]), x,
-           A.subtract, w=1.9)
+           A.subtract, w=GA)
         op("tt", ["DX" + y, "PA:k"], ["DY" + y], T["DY" + y][:], T["DX" + y][:], T.PA[:, 128:224], A.mult)
         mm([xk, "IDB"], ["PB:x"], T.PB[:, 256:352], T.IDB[:], x, True, False)
         mm([ob, "B64"], ["PB:x"], T.PB[:, 256:352], T.B64[:], T[ob][:], False, False)
@@ -424,12 +433,11 @@ def rank_program(g, core, T, topo):
         op("tt", ["PA:d", ot], ["PA:d"], T.PA[:, 256:352], T.PA[:, 256:352], T[ot][:], A.mult)
         if r < RO - 1:
             op("tt", ["PA:d", pfk], [opk], T.OP[:, cs(q, r)], T.PA[:, 256:352], PF, A.add)
-            sem = T.sem["a%d%d" % (r, q)]
-            s = send([oxk, opk], [
-                RemoteDMATransfer(dst_ids=[to(nxt)], dma_engine_mask=bits(es), remote_sem=sem, src=T[o][:, cs(q, r)],
-                                  dst=T[l][:, cs(q, r + 1)])
-                for es, o, l in ((enx[:hn], "OP", "PF"), (enx[hn:], "OX", "LX"))], 2 * hn)
-            arrives("a%d%d" % (r, q), 2 * hn, ["PF%d.%d" % (r + 1, q), "LX%d.%d" % (r + 1, q)], s, 3.5)
+            for key, o, l in ((opk, "OP", "PF"), (oxk, "OX", "LX")):
+                sem = "%s%d%d" % (o, r, q)
+                s = send([key], [RemoteDMATransfer(dst_ids=[to(nxt)], dma_engine_mask=bits(enx), remote_sem=T.sem[sem],
+                                                   src=T[o][:, cs(q, r)], dst=T[l][:, cs(q, r + 1)])], len(enx))
+                arrives(sem, len(enx), ["%s%d.%d" % (l, r + 1, q)], s, XL[2])
         else:
             op("tt", ["PA:d", "YP.%d" % q], ["YP.%d" % q], T.YP[:, cs(q)], T.PA[:, 256:352], T.YP[:, cs(q)], A.add)
             op("act", [oxk], ["YX.%d" % q], T.YX[:, cs(q)], T.OX[:, cs(q, r)], F.Identity, bias=-128.0)

@@ -5,7 +5,8 @@ A = AluOpType
 F = ActivationFunctionType
 NR, W, V, RO, STEP = 8, 3072, 384, 3, 3
 U, H = 96, 192
-BIG = 16777216.0
+BIG = 33554432.0
+RND = 1610612736.0
 OFF = 1536.0
 CUT = 2176.0
 GA = 1.56
@@ -14,29 +15,29 @@ WAKE = 0.25
 TURNS = 4
 NG = 3
 CH = (0, 64, 96)
-VG = set()
+VG = {(0, 0, 0, 0, 1)} | {(r, 1, 0, n, 1) for r in range(RO) for n in range(2)}
 
 f, b, i, u, h = "float32", "bfloat16", "int32", "uint16", "float16"
 SB = {
     "LX": (b, RO * V), "PF": (h, RO * V), "OX": (b, RO * V), "OP": (h, RO * V), "LP": (u, V), "CU": (u, V), "CD": (h, V),
     "PI": (i, V), "YP": (f, V), "YX": (b, V), "YC": (f, 2, 128), "A0": (b, 2, 128), "FS": (b, 2 * RO, 96),
     "FL": (b, 2 * RO, 8, 96), "OK": (b, 4, 136), "ZK": (f, 4, 128),
-    "ONE": (b, 384), "IDB": (b, 128), "IDN": (b, 128), "IDP": (h, 128), "IDZ": (b, 256), "IDH": (b, 128), "ID4": (b, 128),
-    "BO": (b, 128), "BP": (h, 128), "B64": (b, 128), "BG": (b, 16), "BM": (b, 16), "XT": (b, 256), "TRI": (b, 128),
-    "WK": (b, 16, 8), "EE": (h, 144), "TB": (h, 8, 25), "CK": (b, 256), "CE": (b, 128), "CT": (b, 8, 25), "CX": (b, 384),
-    "CY": (b, 128), "RS": (f, 128), "RE": (f, 128), "KP": (f, 128), "ZB": (f, 1), "ZI": (i, 1), "IOM": (b, 128), "ZER": (b, 128),
+    "ONE": (b, 384), "IDB": (b, 128), "IDN": (b, 128), "IDP": (h, 128), "IDZ": (b, 384), "IDH": (b, 128), "ID4": (b, 128),
+    "BO": (b, 128), "BP": (h, 128), "B64": (b, 128), "BG": (b, 24), "BM": (b, 24), "XT": (b, 384), "TRI": (b, 128),
+    "WK": (b, 16, 8), "EE": (h, 144), "IDQ": (h, 128), "IDL": (b, 256), "CK": (b, 384), "CE": (b, 128), "CX": (b, 384),
+    "CY": (b, 128), "RS": (f, 256), "RE": (f, 128), "KP": (f, 128), "ZB": (f, 1), "ZI": (i, 1), "IOM": (b, 128), "ZER": (b, 128),
 }
 for n in range(NG):
     SB["G%d" % n] = (b, 16 * U)
 TWO = {"TX": (b, W), "PU": (i, W), "M": (b, 16 * U), "DF": (b, 48), "ZZ": (b, U), "S1": (f, 128), "S2": (f, 128), "ZF": (f, 128),
-       "OF": (b, 128), "SP": (h, U), "SQ": (h, U), "HH": (b, 8), "NN": (f, 8), "TM": (b, 8, 25), "OH": (b, 8, 128), "PL": (u, 8),
+       "OF": (b, 128), "SP": (h, U), "SQ": (h, U), "HP": (b, U), "YY": (f, 16), "SL": (f, 256), "OH": (b, 8, 112), "PL": (u, 8),
        "FR": (b, 128), "OB": (b, U), "OT": (b, U), "DX": (b, U), "DY": (b, U), "S3": (f, 128), "S4": (f, 128), "PM": (u, 8)}
 for n, s in TWO.items():
     SB.update({n + "0": s, n + "1": s})
 SCRATCH = {n: ("sbuf", [128] + list(s[1:]), s[0]) for n, s in SB.items()}
 BANKS = {"XR0": [512], "XR1": [512], "K0": [512], "K1": [512], "PA": [512], "PB": [512], "HI": [4, 24], "CF": [512]}
 SCRATCH.update({n: ("psum", [128] + s, f) for n, s in BANKS.items()})
-SEMAPHORES = ["cv", "cs", "cp", "cg", "loc"] + ["d%d" % n for n in range(56)] + ["fl%d%d" % (n, k) for n in range(2 * RO) for k in range(NR)] + \
+SEMAPHORES = ["cv", "cs", "cp", "cg", "loc"] + ["d%d" % n for n in range(50)] + ["fl%d%d" % (n, k) for n in range(2 * RO) for k in range(NR)] + \
     ["%s%d%d" % (o, s, n) for o in ("OP", "OX") for s in range(RO - 1) for n in range(4)]
 
 
@@ -44,7 +45,7 @@ def make_plan(g, T):
     eng = {"v": g.vector, "s": g.scalar, "p": g.tensor, "g": g, "y": g.sync}
     nodes = []
     wr, rd, touch, last = {}, {}, {}, {}
-    nd = [0]
+    nd = [0, 0]
 
     def add(e, reads, writes, emit, sem, inc, cost, acc=False, lag=WAKE, own=True, after=()):
         deps, me = set(after), len(nodes)
@@ -105,8 +106,11 @@ def make_plan(g, T):
     def arrives(sem, n, writes, sent, lag):
         add("x", [], writes, None, sem, n, 0.0, lag=lag, after=[sent])
 
-    def finish():
+    def finish(last=True):
         n = len(nodes)
+        if not last:
+            nd[1] = n
+            return
         succ = [[] for _ in range(n)]
         for k, x in enumerate(nodes):
             x["all"] = sorted(set(x["deps"] + ([x["prev"]] if "prev" in x else [])))
@@ -139,7 +143,7 @@ def make_plan(g, T):
             prio[k] = nodes[k]["cost"] + max([prio[s] + gap(k, s) for s in succ[k]] + [nodes[k]["lag"]])
         best = None
         for turn in range(TURNS):
-            start = place(sorted(range(n), key=lambda k: (-prio[k], k)), pred, gap, lambda k: 0.0)
+            start = place(sorted(range(n), key=lambda k: (0, k) if k < nd[1] else (1, -prio[k], k)), pred, gap, lambda k: 0.0)
             end = [start[k] + nodes[k]["cost"] for k in range(n)]
             span = max(end[k] + nodes[k]["lag"] for k in range(n))
             if best is None or span < best[0]:
@@ -202,19 +206,20 @@ def rank_program(g, core, T, topo):
     def txk(a):
         return ["TX%d.0" % a, "TX%d.1" % a]
 
-    for a in range(2):
-        rows, c = slice(64 * a, 64 * a + 64), slice(H * a, H * a + H)
+    def half(j):
+        return slice(64 * j, 64 * j + 64)
+
+    for what, a, lag in (("PI", 0, 2.0), ("TX", 0, 4.2), ("X", 0, 4.3), ("PI", 1, 4.6), ("X", 1, 4.7), ("TX", 1, 8.0),
+                         ("PU", 0, 13.0), ("PU", 1, 19.0)):
         for j in range(2):
-            p = slice(64 * j, 64 * j + 64)
-            dma("y" if a or j else "s", [], ["TX%d.%d" % (a, j)], T["TX%d" % a][p, :], T.tx[rows, :], lag=3.5)
-        for j in range(2):
-            p = slice(64 * j, 64 * j + 64)
-            dma("y" if a else "s", [], ["PI%d.%d" % (a, j)], T.PI[p, c], T.p0[rows, H * j:H * j + H])
-            dma("y", [], ["X%d.%d" % (a, j)], T.LX[p, c], T.x0[rows, H * j:H * j + H])
-    for a in range(2):
-        for j in range(2):
-            dma("y", [], ["PU%d.%d" % (a, j)], T["PU%d" % a][64 * j:64 * j + 64, :], T.pu[64 * a:64 * a + 64, :], lag=8.0 + 5 * a)
-        dma("y", [], ["A0.%d" % a], T.A0[0:96, a, :], T.tx[64 * a:64 * a + 64:16, :])
+            out, src = {"PI": (T.PI, T.p0), "X": (T.LX, T.x0), "TX": (T["TX%d" % a], T.tx), "PU": (T["PU%d" % a], T.pu)}[what]
+            if what in ("PI", "X"):
+                out, src = out[half(j), H * a:H * a + H], src[half(a), H * j:H * j + H]
+            else:
+                out, src = out[half(j), :], src[half(a), :]
+            dma("y" if j or lag > 5 else "s", [], ["%s%d.%d" % (what, a, j)], out, src, lag=lag)
+        if what == "PU":
+            dma("y", [], ["A0.%d" % a], T.A0[0:96, a, :], T.tx[64 * a:64 * a + 64:16, :], lag=lag)
     for a in range(2):
         c = slice(H * a, H * a + H)
         pi = ["PI%d.0" % a, "PI%d.1" % a]
@@ -230,32 +235,34 @@ def rank_program(g, core, T, topo):
     op("asel", ["BO"], ["TRI"], T.TRI[:], T.BO[:], [[1, 128]], A.is_ge, 0.0, 0, -1)
     op("ms", [], ["TRI"], T.TRI[:, 0:128:16], 0.0)
     for n, src, c in (("IDN", "IDB", -1.0), ("IDP", "IDB", -1.0), ("IDH", "IDB", 0.5), ("ID4", "IDB", 4096.0),
-                      ("BP", "BO", 1.0), ("B64", "BO", 64.0)):
+                      ("BP", "BO", 1.0), ("B64", "BO", 64.0), ("IDQ", "IDB", 1.0)):
         op("ts", [src], [n], T[n][:], T[src][:], c, None, A.mult, w=0.5)
-    for j in range(2):
-        op("ts", ["BO"], ["BM"], T.BM[:, 8 * j:8 * j + 8], T.BO[:, 0:128:16], -64.0, None, A.mult)
-        op("ts", ["BO"], ["BG"], T.BG[:, 8 * j:8 * j + 8], T.BO[:, 0:128:16], 32.0, None, A.mult)
-        op("ts", ["BO"], ["XT"], T.XT[:, 128 * j:128 * j + 128], T.BO[:], 32.0, None, A.mult, w=0.5)
-        op("ts", ["IDB"], ["IDZ"], T.IDZ[:, 128 * j:128 * j + 128], T.IDB[:], 131072.0, None, A.mult, w=0.5)
+    for j, c in enumerate((32.0, 2048.0, 2048.0)):
+        op("ts", ["BO"], ["BM"], T.BM[:, 8 * j:8 * j + 8], T.BO[:, 0:128:16], -2 * c, None, A.mult)
+        op("ts", ["BO"], ["BG"], T.BG[:, 8 * j:8 * j + 8], T.BO[:, 0:128:16], c, None, A.mult)
+        op("ts", ["BO"], ["XT"], T.XT[:, 128 * j:128 * j + 128], T.BO[:], c, None, A.mult, w=0.5)
+        op("ts", ["IDB"], ["IDZ"], T.IDZ[:, 128 * j:128 * j + 128], T.IDB[:], 4096 * c, None, A.mult, w=0.5)
+    for j, c in enumerate((-1.0, 1.0 / 64)):
+        op("ts", ["IDB"], ["IDL"], T.IDL[:, 128 * j:128 * j + 128], T.IDB[:], c, None, A.mult, w=0.5)
     op("iota", [], ["WK"], T.WK[:], [[-128, 16], [0, 8]], 2048, 0, **lo)
     op("asel", ["WK"], ["WK"], T.WK[:], T.WK[:], [[0, 16], [-16, 8]], A.is_equal, 0.0, 0, 1)
     op("ms", [], ["WK"], T.WK[:, 0, :], 0.0)
     op("ms", [], ["EE"], T.EE[:], 0.0)
     op("cp", ["BO"], ["EE"], T.EE[:, 15:143:16], T.BO[:, 0:128:16])
-    op("cp", ["BO"], ["TB"], T.TB[:, :, 0:16], T.BO[:])
-    op("cp", ["TB"], ["TB"], T.TB[:, :, 16:25], T.TB[:, :, 0:9])
-    op("ts", ["TB"], ["TB"], T.TB[:, :, 1:25:2], T.TB[:, :, 1:25:2], -1.0, None, A.mult)
-    for n, pat, base, c in (("CK", [[0, 16], [1, 16]], 0, -65536.0), ("CE", [[0, 8], [-1, 16]], 0, -65536.0),
-                            ("CT", [[0, 8], [-128, 25]], int(OFF), 0.5)):
-        op("ms", [], [n], T[n][0:32], 0.0)
-        op("iota", [], [n], T[n][0:1], pat, base, 0, **lo)
-        op("ms", [], [n], T[n][32:33], c)
-    op("ts", ["CT"], ["CT"], T.CT[0:33, :, 1:25:2], T.CT[0:33, :, 1:25:2], -1.0, None, A.mult)
+    for n in ("CK", "CE"):
+        op("ms", [], [n], T[n][0:65, :], 0.0, w=0.5)
+        op("ms", [], [n], T[n][32:33, 0:128], -65536.0)
+    op("iota", [], ["CK"], T.CK[0:1, 0:128], [[0, 8], [1, 16]], 0, 0, **lo)
+    op("iota", [], ["CE"], T.CE[0:1, :], [[0, 8], [-1, 16]], 0, 0, **lo)
+    for j, c in ((1, OFF + 8256.0), (2, -129.0)):
+        op("ts", ["CK"], ["CK"], T.CK[0:1, 128 * j:128 * j + 128], T.CK[0:1, 0:128], 128.0, None, A.mult, w=0.5)
+        op("ms", [], ["CK"], T.CK[64:65, 128 * j:128 * j + 128], c)
+    op("ms", [], ["CK"], T.CK[32:33, 128:384], -12582912.0)
     op("ms", [], ["CX"], T.CX[0:1, :], -128.0)
     op("ms", [], ["CY"], T.CY[0:1, :], -8192.0)
     for n, c0, c1 in (("RS", 0.0, BIG), ("RE", BIG, -65280.0), ("KP", 1.0, 0.0)):
         op("ms", [], [n], T[n][:], c0)
-        op("ms", [], [n], T[n][:, 0:128:16], c1)
+        op("ms", [], [n], T[n][:, 0::16], c1)
     op("iota", [], ["ZI"], T.ZI[:], [[0, 1]], 0, 1)
     op("ts", ["ZI"], ["ZI"], T.ZI[:], T.ZI[:], 15, None, A.bitwise_and)
     op("ts", ["ZI"], ["ZB"], T.ZB[:], T.ZI[:], 15.0, None, A.not_equal)
@@ -265,6 +272,7 @@ def rank_program(g, core, T, topo):
     op("ms", [], ["OK.e"], T.OK[:, :, 128:136], 0.0)
     for j in range(2):
         op("ms", [], ["ZF%d" % j], T["ZF%d" % j][:], 0.0)
+    finish(False)
 
     v = slice(0, U)
     I96 = T.IDB[v, v]
@@ -276,8 +284,13 @@ def rank_program(g, core, T, topo):
         y, a = "%d" % (p % 2), q // 2
         K, M, XR, X, G = T["K" + y], T["M" + y], T["XR" + y], T.LX[:, cs(q, r)], T["G%d" % (p % NG)]
         kk, mk, xr, xk, gk = "K%s:k" % y, "M%s." % y, "XR%s:x" % y, "LX%d.%d" % (r, q), "G%d." % (p % NG)
-        nc, nk = len(CH) - 1, 256 if step == 0 and r else 128
-        mm([xk, "XT"], [kk], K[v, 0:nk], X, T.XT[:, 0:nk], True, False)
+        nc, nk = len(CH) - 1, 128 if step else 384
+        ck = "CE" if step else "CK"
+        mm(["ONE", ck], [kk], K[v, 0:nk], T.ONE[0:65, v], T[ck][0:65, 0:nk], True, False)
+        mm([xk, "XT"], [kk], K[v, 0:nk], X, T.XT[:, 0:nk], False, False)
+        if step == 0:
+            mm(["PF%d.%d" % (r, q), "IDQ"], [kk], K[v, 128:256], T.PF[:, cs(q, r)], T.IDQ[:], False, False)
+            mm(["HP" + y, "IDL"], [kk], K[v, 128:384], T["HP" + y][:], T.IDL[:], False, False)
         for c in range(nc):
             src = T["TX%d" % a][:, 0:W].indirect(lists[:, U * q + CH[c]:U * q + CH[c + 1]])
             dst = G[:, 16 * CH[c]:16 * CH[c + 1]]
@@ -296,13 +309,11 @@ def rank_program(g, core, T, topo):
             for j in range(4):
                 s = slice(16 * CH[c] + j, 16 * CH[c + 1], 4)
                 op("tt", [gk + "%d" % c, xr], [mk + "%d.%d" % (c, j)], M[:, s], G[:, s], XR[:, 4 * CH[c]:4 * CH[c + 1]], A.max)
-        ck = "CE" if step else "CK"
-        mm(["ONE", ck], [kk], K[v, 0:nk], T.ONE[0:33, v], T[ck][0:33, 0:nk], False, False)
         for j in range(4):
             if j == 3 and step == 0:
                 mm(["ZZ" + y, "IDZ"], [kk], K[v, 0:nk], T["ZZ" + y][:], T.IDZ[:, 0:nk], False, False)
                 if r:
-                    mm(["FR" + y, "IDN"], [kk], K[v, 128:256], T.IDN[v, v], T["FR" + y][v, :], False, False)
+                    mm(["FR" + y, "IDN"], [kk], K[v, 0:128], T.IDN[v, v], T["FR" + y][v, :], False, False)
             for k in range(j, 16, 4):
                 mm([mk + "%d.%d" % (c, j) for c in range(nc)] + ["BM"], [kk], K[v, k:nk:16], M[:, k::16], T.BM[:, 0:nk // 16], False, k == 15)
 
@@ -315,7 +326,7 @@ def rank_program(g, core, T, topo):
 
     def one_hot(K, kk, s1, s2, Z, zk, O, ok, limit=None):
         if limit is None:
-            op("scan", [kk, "RS"], [s1], T[s1][v, :], T.RS[v, :], K, 0.0, A.add, A.min)
+            op("scan", [kk, "RS"], [s1], T[s1][v, :], T.RS[v, 0:128], K, 0.0, A.add, A.min)
             op("cp", [s1], [zk], Z[0], T[s1][v, 15:128:16])
         else:
             op("scan", [kk, "RE"], [s1], T[s1][v, :], T.RE[v, :], K, 0.0, A.min, A.max)
@@ -339,35 +350,26 @@ def rank_program(g, core, T, topo):
         for j in range(2):
             mm(["DF" + y, "TRI"], ["CF:n"], T.CF[:, 256 + j:352:2], T.TRI[:], T["DF" + y][:], j == 0, j == 1)
         op("act", ["CF:n", "ZB"], ["ZZ" + y], T["ZZ" + y][:], T.CF[:, 256:352], F.Relu, bias=T.ZB[:, 0:1], scale=-1.0)
+        op("ts", [pfk], ["HP" + y], T["HP" + y][:], PF, OFF + 8256.0 - 31.5, None, A.add, w=0.5)
         distances(p, r, 0, q, T.LP, lk)
         ZK, OK, zk, ok = (T.ZK[v, q, 0:128:16], T.ZK[v, q, :]), T.OK[v, q, 0:128], "ZK.%d" % q, "OK.%d" % q
-        if r:
-            O, o = T["OF" + y][v, :], "OF" + y
-            one_hot(K[v, 0:128], kk, "S1" + y, "S2" + y, (T["ZF" + y][v, 0:128:16], T["ZF" + y][v, :]), "ZF" + y, O, o)
-        else:
-            O, o = OK, ok
-            one_hot(K[v, 0:128], kk, "S1" + y, "S2" + y, ZK, zk, O, o)
-        sp = "SP" + y
-        mm([o, "IDB"], ["PA:t"], T.PA[:, v], O, I96, True, True)
-        op("tt", ["PA:t", pfk], [sp], T[sp][:], T.PA[:, v], PF, A.mult)
-        mm([sp, "BP"], ["PA:n"], T.PA[v, 96:104], T[sp][:], T.BP[:, 0:128:16], True, True)
-        mm(["ONE", "CT"], ["PA:s"], T.PA[v, 128:328], T.ONE[0:33, v], T.CT[0:33], True, False)
-        mm([sp, "TB"], ["PA:s"], T.PA[v, 128:328], T[sp][:], T.TB[:], False, True)
-        op("ts", ["PA:n"], ["HH" + y], T["HH" + y][v, :], T.PA[v, 96:104], OFF + 16512.0 - 63.5, None, A.add)
-        op("tt", ["PA:n", "HH" + y], ["NN" + y], T["NN" + y][v, :], T.PA[v, 96:104], T["HH" + y][v, :], A.subtract)
-        op("act", ["PA:s"], ["TM" + y], T["TM" + y][v], T.PA[v, 128:328], F.Sign)
+        SL, YY, OH = T["SL" + y], T["YY" + y], T["OH" + y]
+        op("scan", [kk, "RS"], ["SL" + y], SL[v, :], T.RS[v, :], K[v, 128:384], 0.0, A.add, A.min)
+        op("ts", ["SL" + y], ["YY" + y], YY[v, :], SL[v, 15:256:16], RND, RND, A.add, A.subtract)
         if q % 2 == 0:
             mm(["ZER", "ONE"], ["HI:h"], T.HI[:], T.ZER[:], T.ONE[:, 0:96], True, False)
         for j in range(8):
-            op("ts", ["NN" + y, "IOM"], ["OH%s.%d" % (y, j)], T["OH" + y][v, j, :], T.IOM[v, :], -OFF - 16512.0,
-               T["NN" + y][v, j:j + 1], A.add, A.is_equal, w=0.5)
+            oh = ["OH%s.%d.%d" % (y, j, d) for d in range(2)]
+            for d, c0, c1 in ((0, 0, 64), (1, 64, 112)):
+                m = 8 * d + j
+                op("ts", ["SL" + y, "YY" + y, "IOM"], [oh[d]], OH[v, j, c0:c1], T.IOM[v, 0:c1 - c0], YY[v, m:m + 1],
+                   SL[v, 16 * m + 15:16 * m + 16], A.add, A.is_equal, w=0.5)
             for d in range(2):
-                mm(["OH%s.%d" % (y, j), "TM" + y], ["HI:h"], T.HI[:, j % 4, :], T["OH" + y][v, j, :], T["TM" + y][v, j, d:d + 24],
-                   False, q % 2 == 1 and j == 7 and d == 1)
+                mm(oh, ["HI:h"], T.HI[64 * d:64 * d + 64, j % 4, :], OH[v, j, 0:64], OH[v, j, 64 + d:112:2], False, False)
         if q % 2:
+            mm(["ZER", "ONE"], ["HI:h"], T.HI[:], T.ZER[:], T.ONE[:, 0:96], False, True)
             spread(2 * r + a)
-        if r:
-            one_hot(K[v, 128:256], kk, "S3" + y, "S4" + y, ZK, zk, OK, ok)
+        one_hot(K[v, 0:128], kk, "S3" + y, "S4" + y, ZK, zk, OK, ok)
         mm([ok, "OK.e", "IDB"], ["PB:t"], T.PB[:, v], T.OK[v, q, 1:129], I96, True, True)
         op("tt", ["PB:t", pfk], ["SQ" + y], T["SQ" + y][:], T.PB[:, v], PF, A.mult)
         to_list("PB", "SQ" + y, "PM" + y)

@@ -4,40 +4,49 @@ from concourse.mybir import dt, AluOpType, ActivationFunctionType
 A = AluOpType
 F = ActivationFunctionType
 NR, W, V, RO, STEP = 8, 3072, 384, 3, 3
-U, H = 96, 192
+H = 192
+UNITS = ((0, 96, 1, 4), (96, 96, 1, 4))
+CH = ((0, 64, 96), (0, 64, 96))
+VG = {(0, 0, 0, 0, 1)} | {(r, 1, 0, 0, 1) for r in range(RO)}
+KEYS = ("K0", "K1", "PA", "PB")
 BIG = 33554432.0
+LANE = 262144.0
 RND = 1610612736.0
+FAR = 4096.0
 OFF = 1536.0
 CUT = 2176.0
 GA = 1.56
 XL = (1.8, 0.4, 2.2)
 WAKE = 0.25
-TURNS = 4
+TURNS = 48
+PLAN = []
 NG = 3
-CH = (0, 64, 96)
-VG = {(0, 0, 0, 0, 1)} | {(r, 1, 0, n, 1) for r in range(RO) for n in range(2)}
 
 f, b, i, u, h = "float32", "bfloat16", "int32", "uint16", "float16"
 SB = {
     "LX": (b, RO * V), "PF": (h, RO * V), "OX": (b, RO * V), "OP": (h, RO * V), "LP": (u, V), "CU": (u, V), "CD": (h, V),
     "PI": (i, V), "YP": (f, V), "YX": (b, V), "YC": (f, 2, 128), "A0": (b, 2, 128), "FS": (b, 2 * RO, 96),
-    "FL": (b, 2 * RO, 8, 96), "OK": (b, 4, 136), "ZK": (f, 4, 128),
-    "ONE": (b, 384), "IDB": (b, 128), "IDN": (b, 128), "IDP": (h, 128), "IDZ": (b, 384), "IDH": (b, 128), "ID4": (b, 128),
-    "BO": (b, 128), "BP": (h, 128), "B64": (b, 128), "BG": (b, 24), "BM": (b, 24), "XT": (b, 384), "TRI": (b, 128),
-    "WK": (b, 16, 8), "EE": (h, 144), "IDQ": (h, 128), "IDL": (b, 256), "CK": (b, 384), "CE": (b, 128), "CX": (b, 384),
-    "CY": (b, 128), "RS": (f, 256), "RE": (f, 128), "KP": (f, 128), "ZB": (f, 1), "ZI": (i, 1), "IOM": (b, 128), "ZER": (b, 128),
+    "FL": (b, 2 * RO, 8, 96), "OK": (b, 4, 136), "ZK": (f, 4, 128), "FR": (b, 4, 128),
+    "ONE": (b, 192), "IDB": (b, 128), "IDZ": (b, 3, 128), "IDH": (b, 128), "ID4": (b, 128),
+    "BO": (b, 128), "BP": (h, 128), "B64": (b, 128), "BG": (b, 3, 8), "BM": (b, 3, 8), "XT": (b, 3, 128), "TRI": (b, 128),
+    "WK": (b, 16, 8), "EE": (h, 144), "IDQ": (h, 128), "IDL": (b, 2, 128), "CK": (b, 3, 128), "CE": (b, 128),
+    "CY": (b, 128), "RS": (f, 256), "RE": (f, 128), "KP": (f, 128), "KB": (b, 128), "CL": (f, 16), "LN": (b, 128),
+    "RW": (b, 128), "ZB": (f, 1), "ZI": (i, 1), "IOM": (b, 64), "IB": (b, 2, 128), "CB": (b, 2, 2, 128), "ZER": (b, 128),
 }
 for n in range(NG):
-    SB["G%d" % n] = (b, 16 * U)
-TWO = {"TX": (b, W), "PU": (i, W), "M": (b, 16 * U), "DF": (b, 48), "ZZ": (b, U), "S1": (f, 128), "S2": (f, 128), "ZF": (f, 128),
-       "OF": (b, 128), "SP": (h, U), "SQ": (h, U), "HP": (b, U), "YY": (f, 16), "SL": (f, 256), "OH": (b, 8, 112), "PL": (u, 8),
-       "FR": (b, 128), "OB": (b, U), "OT": (b, U), "DX": (b, U), "DY": (b, U), "S3": (f, 128), "S4": (f, 128), "PM": (u, 8)}
+    SB["G%d" % n] = (b, 2048)
+TWO = {"TX": (b, W), "PU": (i, W), "M": (b, 2048), "DF": (b, 64), "ZZ": (b, 128), "S1": (f, 144), "S2": (f, 128),
+       "ZT": (b, 128), "OF": (b, 128), "SP": (h, 128), "SQ": (h, 128), "HP": (b, 128), "YY": (f, 16), "SL": (f, 256),
+       "OH": (b, 8, 112), "PL": (u, 8), "TK": (b, 128), "PT": (h, 128), "DX": (b, 128), "DY": (b, 128), "S3": (f, 128),
+       "S4": (f, 128), "PM": (u, 8)}
 for n, s in TWO.items():
     SB.update({n + "0": s, n + "1": s})
 SCRATCH = {n: ("sbuf", [128] + list(s[1:]), s[0]) for n, s in SB.items()}
-BANKS = {"XR0": [512], "XR1": [512], "K0": [512], "K1": [512], "PA": [512], "PB": [512], "HI": [4, 24], "CF": [512]}
+BANKS = {"K0": [512], "K1": [512], "PA": [512], "PB": [512], "HI": [512], "CF": [512]}
+BANKS.update({"XR%d" % n: [512 // UNITS[n][3], UNITS[n][3]] for n in range(2)})
 SCRATCH.update({n: ("psum", [128] + s, f) for n, s in BANKS.items()})
-SEMAPHORES = ["cv", "cs", "cp", "cg", "loc"] + ["d%d" % n for n in range(50)] + ["fl%d%d" % (n, k) for n in range(2 * RO) for k in range(NR)] + \
+SEMAPHORES = ["cv", "cs", "cp", "cg", "loc"] + ["d%d" % n for n in range(50)] + \
+    ["fl%d%d" % (n, k) for n in range(2 * RO) for k in range(NR)] + \
     ["%s%d%d" % (o, s, n) for o in ("OP", "OX") for s in range(RO - 1) for n in range(4)]
 
 
@@ -64,7 +73,8 @@ def make_plan(g, T):
                 if k in wr:
                     deps.add(wr[k])
                 deps.update(rd.get(k, ()))
-        nodes.append({"e": e, "deps": sorted(deps), "emit": emit, "sem": sem, "inc": inc, "cost": cost, "lag": lag, "own": own})
+        nodes.append({"e": e, "w": (list(writes) + list(reads))[0], "deps": sorted(deps), "emit": emit, "sem": sem, "inc": inc,
+                      "cost": cost, "lag": lag, "own": own})
         if e == "p":
             for bk in bks:
                 if bk in last:
@@ -93,7 +103,7 @@ def make_plan(g, T):
         else:
             if name == "tt" and w == 1.0 and not any(k.split(":")[0] in BANKS for k in reads):
                 w = 2.0
-            cost = 0.03 + 0.00085 * max(40, n * w)
+            cost = 0.00085 * max(64, n * w) + (0.08 if e == "s" else 0.0)
         return add(e, reads, writes, lambda: fn(out, *args, **kw), "c" + e, 1, cost, acc=acc)
 
     def dma(e, reads, writes, out, in_, lag=2.3):
@@ -120,6 +130,16 @@ def make_plan(g, T):
         def gap(d, k):
             return 0.0 if nodes[k].get("prev") == d else nodes[d]["lag"]
 
+        def replay(seq, slow):
+            end, free = [0.0] * n, {e: 0.0 for e in "vspgyx"}
+            for k in seq:
+                x = nodes[k]
+                t = max([end[d] + gap(d, k) for d in x["all"]] + [0.0])
+                if x["e"] != "x":
+                    t = free[x["e"]] = max(t, free[x["e"]]) + x["cost"] * (slow if x["e"] in "vsp" else 1.0)
+                end[k] = t
+            return max(end[k] + nodes[k]["lag"] for k in seq)
+
         def place(seq, before, wait, first):
             start, busy = [0.0] * n, {e: [] for e in eng}
             for k in seq:
@@ -142,16 +162,20 @@ def make_plan(g, T):
         for k in range(n - 1, -1, -1):
             prio[k] = nodes[k]["cost"] + max([prio[s] + gap(k, s) for s in succ[k]] + [nodes[k]["lag"]])
         best = None
-        for turn in range(TURNS):
+        for turn in range(0 if PLAN else TURNS):
             start = place(sorted(range(n), key=lambda k: (0, k) if k < nd[1] else (1, -prio[k], k)), pred, gap, lambda k: 0.0)
             end = [start[k] + nodes[k]["cost"] for k in range(n)]
-            span = max(end[k] + nodes[k]["lag"] for k in range(n))
+            seq = sorted(range(n), key=lambda k: (start[k], k))
+            span = (replay(seq, 1.0) + replay(seq, 1.4) / 1.3) / 2
             if best is None or span < best[0]:
                 best = (span, start)
-            back = place(sorted(range(n), key=lambda k: (-end[k], -k)), succ, lambda d, k: gap(k, d), lambda k: nodes[k]["lag"])
+            end = [best[1][k] + nodes[k]["cost"] for k in range(n)] if turn % 3 == 2 else end
+            more = [1.0 + 0.4 * ((k * 7919 + turn * 104729) % 1009 / 1009.0 - 0.5) if turn % 3 == 2 else 1.0 for k in range(n)]
+            back = place(sorted(range(n), key=lambda k: (-end[k], -k)), succ, lambda d, k: gap(k, d) * more[k], lambda k: nodes[k]["lag"])
             prio = [back[k] + nodes[k]["cost"] for k in range(n)]
-        start = best[1]
-        order = sorted(range(n), key=lambda k: (start[k], k))
+        if not PLAN:
+            PLAN.extend([sorted(range(n), key=lambda k: (best[1][k], k)), best[0], best[1], nodes])
+        order = PLAN[0]
         cnt, known, event, clock = {}, {e: {} for e in eng}, {}, {}
         for k in order:
             x = nodes[k]
@@ -201,7 +225,8 @@ def rank_program(g, core, T, topo):
         return sum(1 << e for e in es)
 
     def cs(q, r=0):
-        return slice(V * r + U * q, V * r + U * q + U)
+        c = V * r + H * (q // 2) + UNITS[q % 2][0]
+        return slice(c, c + UNITS[q % 2][1])
 
     def txk(a):
         return ["TX%d.0" % a, "TX%d.1" % a]
@@ -220,167 +245,203 @@ def rank_program(g, core, T, topo):
             dma("y" if j or lag > 5 else "s", [], ["%s%d.%d" % (what, a, j)], out, src, lag=lag)
         if what == "PU":
             dma("y", [], ["A0.%d" % a], T.A0[0:96, a, :], T.tx[64 * a:64 * a + 64:16, :], lag=lag)
-    for a in range(2):
+
+    def convert(a):
         c = slice(H * a, H * a + H)
         pi = ["PI%d.0" % a, "PI%d.1" % a]
         op("cp", pi, ["LP.%d" % (2 * a), "LP.%d" % (2 * a + 1)], T.LP[:, c], T.PI[:, c])
         op("ts", pi, ["PF0.%d" % (2 * a), "PF0.%d" % (2 * a + 1)], T.PF[:, c], T.PI[:, c], -OFF, None, A.add)
         op("ts", ["X%d.0" % a, "X%d.1" % a], ["LX0.%d" % (2 * a), "LX0.%d" % (2 * a + 1)], T.LX[:, c], T.LX[:, c], 128.0, None, A.add, w=0.5)
 
+    convert(0)
     lo = {"allow_small_or_imprecise_dtypes": True}
     op("ms", [], ["ONE"], T.ONE[:], 1.0, w=0.5)
     op("asel", ["ONE"], ["IDB"], T.IDB[:], T.ONE[:, 0:128], [[-1, 128]], A.is_equal, 0.0, 0, 1)
     op("asel", ["ONE"], ["BO"], T.BO[:], T.ONE[:, 0:128], [[-16, 8], [0, 16]], A.is_ge, 0.0, 0, 1)
     op("asel", ["BO"], ["BO"], T.BO[:], T.BO[:], [[16, 8], [0, 16]], A.is_ge, 0.0, 15, -1)
+    op("iota", [], ["RW"], T.RW[:], [[0, 8], [1, 16]], 0, 0, **lo)
+    op("iota", [], ["LN"], T.LN[:], [[-1, 8], [0, 16]], 0, 0, **lo)
     op("asel", ["BO"], ["TRI"], T.TRI[:], T.BO[:], [[1, 128]], A.is_ge, 0.0, 0, -1)
-    op("ms", [], ["TRI"], T.TRI[:, 0:128:16], 0.0)
-    for n, src, c in (("IDN", "IDB", -1.0), ("IDP", "IDB", -1.0), ("IDH", "IDB", 0.5), ("ID4", "IDB", 4096.0),
-                      ("BP", "BO", 1.0), ("B64", "BO", 64.0), ("IDQ", "IDB", 1.0)):
-        op("ts", [src], [n], T[n][:], T[src][:], c, None, A.mult, w=0.5)
-    for j, c in enumerate((32.0, 2048.0, 2048.0)):
-        op("ts", ["BO"], ["BM"], T.BM[:, 8 * j:8 * j + 8], T.BO[:, 0:128:16], -2 * c, None, A.mult)
-        op("ts", ["BO"], ["BG"], T.BG[:, 8 * j:8 * j + 8], T.BO[:, 0:128:16], c, None, A.mult)
-        op("ts", ["BO"], ["XT"], T.XT[:, 128 * j:128 * j + 128], T.BO[:], c, None, A.mult, w=0.5)
-        op("ts", ["IDB"], ["IDZ"], T.IDZ[:, 128 * j:128 * j + 128], T.IDB[:], 4096 * c, None, A.mult, w=0.5)
-    for j, c in enumerate((-1.0, 1.0 / 64)):
-        op("ts", ["IDB"], ["IDL"], T.IDL[:, 128 * j:128 * j + 128], T.IDB[:], c, None, A.mult, w=0.5)
-    op("iota", [], ["WK"], T.WK[:], [[-128, 16], [0, 8]], 2048, 0, **lo)
-    op("asel", ["WK"], ["WK"], T.WK[:], T.WK[:], [[0, 16], [-16, 8]], A.is_equal, 0.0, 0, 1)
-    op("ms", [], ["WK"], T.WK[:, 0, :], 0.0)
-    op("ms", [], ["EE"], T.EE[:], 0.0)
-    op("cp", ["BO"], ["EE"], T.EE[:, 15:143:16], T.BO[:, 0:128:16])
-    for n in ("CK", "CE"):
-        op("ms", [], [n], T[n][0:65, :], 0.0, w=0.5)
-        op("ms", [], [n], T[n][32:33, 0:128], -65536.0)
-    op("iota", [], ["CK"], T.CK[0:1, 0:128], [[0, 8], [1, 16]], 0, 0, **lo)
-    op("iota", [], ["CE"], T.CE[0:1, :], [[0, 8], [-1, 16]], 0, 0, **lo)
-    for j, c in ((1, OFF + 8256.0), (2, -129.0)):
-        op("ts", ["CK"], ["CK"], T.CK[0:1, 128 * j:128 * j + 128], T.CK[0:1, 0:128], 128.0, None, A.mult, w=0.5)
-        op("ms", [], ["CK"], T.CK[64:65, 128 * j:128 * j + 128], c)
-    op("ms", [], ["CK"], T.CK[32:33, 128:384], -12582912.0)
-    op("ms", [], ["CX"], T.CX[0:1, :], -128.0)
-    op("ms", [], ["CY"], T.CY[0:1, :], -8192.0)
-    for n, c0, c1 in (("RS", 0.0, BIG), ("RE", BIG, -65280.0), ("KP", 1.0, 0.0)):
-        op("ms", [], [n], T[n][:], c0)
-        op("ms", [], [n], T[n][:, 0::16], c1)
     op("iota", [], ["ZI"], T.ZI[:], [[0, 1]], 0, 1)
+    op("iota", [], ["IOM"], T.IOM[:], [[1, 64]], 0, 0, **lo)
+    op("iota", [], ["WK"], T.WK[:], [[-96, 16], [0, 8]], 1632, 0, **lo)
+    op("asel", ["WK"], ["WK"], T.WK[:], T.WK[:], [[0, 16], [-16, 8]], A.is_equal, 0.0, 0, 1)
+    XTK, BGK, BMK, CEK = [["%s%d" % (n, j) for j in range(3)] for n in ("XT", "BG", "BM", "CE")]
+    for j, c in enumerate((32.0, 2048.0, 2048.0)):
+        op("act", ["IDB"], ["IDZ%d" % j], T.IDZ[:, j, :], T.IDB[:], F.Copy, scale=4096 * c)
+        op("act", ["BO"], [XTK[j]], T.XT[:, j, :], T.BO[:], F.Copy, scale=c)
+        op("ts", ["BO"], [BMK[j]], T.BM[:, j, :], T.BO[:, 0:128:16], -2 * c, None, A.mult)
+        op("ts", ["BO"], [BGK[j]], T.BG[:, j, :], T.BO[:, 0:128:16], c, None, A.mult)
+    op("ms", [], ["CK"], T.CK[0:64], 0.0, w=0.5)
+    for j, c, d in ((0, 1.0, None), (1, 128.0, OFF + 8320.0), (2, 128.0, -130.0)):
+        op("ts", ["RW", "CK"], ["CK.%d" % j], T.CK[0:1, j, :], T.RW[0:1, :], c, None, A.mult, w=0.5)
+        if j:
+            op("ms", [], ["CK,%d" % j], T.CK[64:65, j, :], d)
+    op("ts", ["LN"], ["CK,0"], T.CK[64:65, 0, :], T.LN[64:65, :], LANE, None, A.mult, w=0.5)
+    op("ms", ["CK"], ["CK;"], T.CK[32:33, 1:3, :], -8388608.0)
+    op("tt", ["IDZ%d" % j for j in range(3)] + ["CK;"] + ["CK%s%d" % (s, j) for s in ".," for j in range(3)], ["IDZ"],
+       T.IDZ[0:65], T.IDZ[0:65], T.CK[0:65], A.add)
+    op("ms", [], ["TRI"], T.TRI[:, 0:128:16], 0.0)
     op("ts", ["ZI"], ["ZI"], T.ZI[:], T.ZI[:], 15, None, A.bitwise_and)
     op("ts", ["ZI"], ["ZB"], T.ZB[:], T.ZI[:], 15.0, None, A.not_equal)
-    op("iota", [], ["IOM"], T.IOM[:], [[1, 128]], 0, 0, **lo)
-    op("ms", [], ["ZER"], T.ZER[:], 0.0)
-    op("ms", [], ["ZK.%d" % q for q in range(4)], T.ZK[:], 0.0)
-    op("ms", [], ["OK.e"], T.OK[:, :, 128:136], 0.0)
+    op("ms", [], ["ZER"], T.ZER[:], 0.0, w=0.5)
+    for n, src, c in (("IDQ", "IDB", 1.0), ("BP", "BO", 1.0)):
+        op("ts", [src], [n], T[n][:], T[src][:], c, None, A.mult, w=0.5)
+    for j, c in enumerate((-1.0, 1.0 / 64)):
+        op("act", ["IDB"], ["IDL%d" % j], T.IDL[:, j, :], T.IDB[:], F.Copy, scale=c)
+    for n, c in (("IDH", 0.5), ("ID4", 4096.0), ("B64", 64.0)):
+        op("act", ["IDB"], [n], T[n][:], T.IDB[:], F.Copy, scale=c)
+    for n, c0, c1 in (("RS", 0.0, BIG), ("RE", 0.0, -BIG), ("KP", 1.0, 0.0), ("KB", 1.0, 0.0)):
+        op("ms", [], [n], T[n][:], c0)
+        op("ms", [], [n], T[n][:, 0::16], c1)
     for j in range(2):
-        op("ms", [], ["ZF%d" % j], T["ZF%d" % j][:], 0.0)
+        op("act", ["IDB"], ["IB%d" % j], T.IB[:, j, :], T.IDB[:], F.Copy, scale=FAR * (1 - 2 * j))
+        for l in range(2):
+            op("ms", [], ["CB%d%d" % (l, j)], T.CB[0:1, l, j, :], l * OFF - 2 * FAR * (1 - 2 * j))
+    op("ms", [], ["ZK.%d" % q for q in range(4)], T.ZK[:], 0.0)
+    op("ms", [], ["OK.%d" % q for q in range(4)], T.OK[:], 0.0, w=0.5)
+    op("ms", [], ["EE"], T.EE[:], 0.0, w=0.5)
+    op("ms", [], [CEK[0]], T.CE[0:64, :], 0.0, w=0.5)
+    for j in range(2):
+        nc = 128 // UNITS[j][2]
+        op("ms", [], ["ZT%d" % j], T["ZT%d" % j][:], 0.0, w=0.5)
+        op("ms", [], ["S1%d.e" % j], T["S1%d" % j][:, nc:nc + 16], -BIG)
+    op("ms", [], ["CY"], T.CY[0:1, :], -8192.0)
+    op("cp", ["BO"], ["EE"], T.EE[:, 15:143:16], T.BO[:, 0:128:16])
+    op("ts", ["RW", CEK[0]], [CEK[1]], T.CE[0:1, :], T.RW[0:1, :], -1.0, None, A.mult, w=0.5)
+    op("ts", ["LN"], [CEK[2]], T.CE[64:65, :], T.LN[64:65, :], LANE, None, A.mult, w=0.5)
+    op("ts", ["LN"], ["CL0"], T.CL[:, 0:8], T.LN[:, 0:128:16], LANE, -65280.0, A.mult, A.add)
+    for j in range(2):
+        op("ts", ["LN"], ["CL%d" % (1 + j)], T.CL[half(j), 8:12], T.LN[half(j), 64 * j:64 * j + 64:16], LANE, -65280.0, A.mult, A.add)
+    op("ms", [], ["WK"], T.WK[:, 0, :], 0.0)
     finish(False)
-
-    v = slice(0, U)
-    I96 = T.IDB[v, v]
+    convert(1)
 
     def mm(reads, writes, out, lhsT, rhs, start, stop):
         return op("mm", reads, writes, out, lhsT, rhs, start, stop, acc=not start)
 
+    def parts(q):
+        U, st = UNITS[q % 2][1:3]
+        return [(slice(U * j, U * j + U), slice(8 // st * j, 8 // st * (j + 1)), slice(128 // st * j, 128 // st * (j + 1))) for j in range(st)]
+
+    def turn(q, reads, key, out, src, c0, ident, start, stop):
+        for pv, _, pc in parts(q):
+            mm(reads, [key], out(pc), src(pv, slice(c0, c0 + pc.stop - pc.start)), ident[pv, pv], start, stop)
+
     def distances(p, r, step, q, lists, lkey):
-        y, a = "%d" % (p % 2), q // 2
-        K, M, XR, X, G = T["K" + y], T["M" + y], T["XR" + y], T.LX[:, cs(q, r)], T["G%d" % (p % NG)]
-        kk, mk, xr, xk, gk = "K%s:k" % y, "M%s." % y, "XR%s:x" % y, "LX%d.%d" % (r, q), "G%d." % (p % NG)
-        nc, nk = len(CH) - 1, 128 if step else 384
-        ck = "CE" if step else "CK"
-        mm(["ONE", ck], [kk], K[v, 0:nk], T.ONE[0:65, v], T[ck][0:65, 0:nk], True, False)
-        mm([xk, "XT"], [kk], K[v, 0:nk], X, T.XT[:, 0:nk], False, False)
-        if step == 0:
-            mm(["PF%d.%d" % (r, q), "IDQ"], [kk], K[v, 128:256], T.PF[:, cs(q, r)], T.IDQ[:], False, False)
-            mm(["HP" + y, "IDL"], [kk], K[v, 128:384], T["HP" + y][:], T.IDL[:], False, False)
+        y, a, (U, st, m), ch = "%d" % (q % 2), q // 2, UNITS[q % 2][1:], CH[q % 2]
+        kb = "K" + y if step else KEYS[q]
+        K, M, XR, X, G = T[kb], T["M" + y], T["XR" + y], T.LX[:, cs(q, r)], T["G%d" % (p % NG)]
+        kk, mk, xr, xk, gk = kb + ":k", "M%s." % y, "XR%s:" % y, "LX%d.%d" % (r, q), "G%d." % (p % NG)
+        nc, C, R = len(ch) - 1, 128 // st, 1 if step else 3
+        k0, c0 = 1 - step, cs(q).start
+        if st > 1:
+            mm(["ZER", "ONE"], [kk], K[:, 0:R * C], T.ZER[:], T.ONE[:, 0:R * C], True, False)
+        for pv, _, pc in parts(q):
+            mm([xk] + XTK, [kk], K[pv, 0:R * C], X, T.XT[:, 0:R, pc], st == 1, False)
+            if step:
+                mm(["ONE"] + CEK, [kk], K[pv, 0:C], T.ONE[0:65, 0:U], T.CE[0:65, pc], False, False)
+        for j in range(m):
+            mm(["IDB", xk], [xr + "%d" % j], XR[:, 0:U, j], T.IDB[:], X, True, True)
         for c in range(nc):
-            src = T["TX%d" % a][:, 0:W].indirect(lists[:, U * q + CH[c]:U * q + CH[c + 1]])
-            dst = G[:, 16 * CH[c]:16 * CH[c + 1]]
+            src = T["TX%d" % a][:, 0:W].indirect(lists[:, c0 + ch[c]:c0 + ch[c + 1]])
+            dst = G[:, 16 * ch[c]:16 * ch[c + 1]]
             if (r, step, a, q % 2, c) in VG:
-                op("cp", txk(a) + [lkey], [gk + "%d" % c], dst, src, w=GA)
+                op("ts", txk(a) + [lkey], [gk + "%d" % c], dst, src, 128.0, None, A.add, w=GA)
             else:
-                op("act", txk(a) + [lkey], [gk + "%d" % c], dst, src, F.Copy, w=GA)
+                op("act", txk(a) + [lkey], [gk + "%d" % c], dst, src, F.Identity, bias=128.0, w=GA)
         gs = [gk + "%d" % c for c in range(nc)]
-        for k in range(16):
-            mm(gs + ["BG"], [kk], K[v, k:nk:16], G[:, k::16], T.BG[:, 0:nk // 16], False, False)
+        for k in range(k0, 16):
+            for pv, pl, _ in parts(q):
+                mm(gs + BGK, [kk], K[pv, k:R * C:16], G[:, k:16 * U:16], T.BG[:, 0:R, pl], False, False)
         if step == 0 and r:
-            for k in range(16):
-                mm(gs + ["WK"], ["CF:f"], T.CF[v, k:128:16], G[:, k::16], T.WK[:, k, :], k == 0, k == 15)
-            op("act", ["CF:f"], ["FR" + y], T["FR" + y][v, :], T.CF[v, 0:128], F.Relu, bias=-245760.0)
+            for pv, pl, _ in parts(q):
+                for k in range(16):
+                    mm(gs + ["WK"], ["CF:f"], T.CF[pv, k:C:16], G[:, k:16 * U:16], T.WK[:, k, pl], k == 0, k == 15)
+            op("act", ["CF:f"], ["FR.%d" % q], T.FR[0:U * st, q, 0:C], T.CF[0:U * st, 0:C], F.Relu, bias=-393216.0)
+        n = 16 // m
         for c in range(nc):
-            for j in range(4):
-                s = slice(16 * CH[c] + j, 16 * CH[c + 1], 4)
-                op("tt", [gk + "%d" % c, xr], [mk + "%d.%d" % (c, j)], M[:, s], G[:, s], XR[:, 4 * CH[c]:4 * CH[c + 1]], A.max)
-        for j in range(4):
-            if j == 3 and step == 0:
-                mm(["ZZ" + y, "IDZ"], [kk], K[v, 0:nk], T["ZZ" + y][:], T.IDZ[:, 0:nk], False, False)
-                if r:
-                    mm(["FR" + y, "IDN"], [kk], K[v, 0:128], T.IDN[v, v], T["FR" + y][v, :], False, False)
-            for k in range(j, 16, 4):
-                mm([mk + "%d.%d" % (c, j) for c in range(nc)] + ["BM"], [kk], K[v, k:nk:16], M[:, k::16], T.BM[:, 0:nk // 16], False, k == 15)
+            for j in range(n):
+                s = slice(16 * ch[c] + j, 16 * ch[c + 1], n)
+                op("tt", [gk + "%d" % c] + [xr + "%d" % l for l in range(m)], [mk + "%d.%d" % (c, j)], M[:, s], G[:, s],
+                   XR[:, ch[c]:ch[c + 1], :], A.max)
+        for j in range(n):
+            if j == n - 1 and step == 0:
+                for pv, _, pc in parts(q):
+                    mm(["ZZ" + y, "IDZ"], [kk], K[pv, 0:R * C], T["ZZ" + y][:, 0:U], T.IDZ[:, :, pc], False, False)
+            for k in range(j or n * k0, 16, n):
+                for pv, pl, _ in parts(q):
+                    mm([mk + "%d.%d" % (c, j) for c in range(nc)] + BMK, [kk], K[pv, k:R * C:16], M[:, k:16 * U:16], T.BM[:, 0:R, pl],
+                       False, step == 1 and k == 15 and st == 1)
+        if step == 0:
+            for pv, _, pc in parts(q):
+                mm(["PF%d.%d" % (r, q), "IDQ"], [kk], K[pv, C:2 * C], T.PF[:, cs(q, r)], T.IDQ[:, pc], False, False)
+                mm(["HP" + y, "IDL0", "IDL1"], [kk], K[pv, C:3 * C], T["HP" + y][:, 0:U], T.IDL[:, :, pc], False, st == 1)
+        if st > 1:
+            mm(["ZER", "ONE"], [kk], K[:, 0:64], T.ZER[:], T.ONE[:, 0:64], False, True)
 
-    def repeat(p, r, q):
-        y = "%d" % (p % 2)
-        XR, xr, xk = T["XR" + y], "XR%s:x" % y, "LX%d.%d" % (r, q)
-        mm(["ONE", "CX"], [xr], XR[:, 0:384], T.ONE[0:1, 0:128], T.CX[0:1, :], True, False)
-        for j in range(4):
-            mm(["IDB", xk], [xr], XR[:, j:384:4], T.IDB[:], T.LX[:, cs(q, r)], False, j == 3)
-
-    def one_hot(K, kk, s1, s2, Z, zk, O, ok, limit=None):
-        if limit is None:
-            op("scan", [kk, "RS"], [s1], T[s1][v, :], T.RS[v, 0:128], K, 0.0, A.add, A.min)
-            op("cp", [s1], [zk], Z[0], T[s1][v, 15:128:16])
-        else:
-            op("scan", [kk, "RE"], [s1], T[s1][v, :], T.RE[v, :], K, 0.0, A.min, A.max)
-            op("tt", [s1, limit[1]], [zk], Z[0], T[s1][v, 15:128:16], limit[0], A.max)
-        op("scan", [zk, "KP"], [s2], T[s2][v, :], T.KP[v, :], Z[1], 0.0, A.mult, A.add)
-        op("tt", [kk, s2], [ok], O, K, T[s2][v, :], A.is_equal)
-
-    def to_list(bank, src, pl):
+    def to_list(bank, c0, src, pl, U):
+        n = U // 16
         for j in range(16):
-            mm([src, "EE"], [bank + ":l"], T[bank][:, 96:102], T.EE[:, 15 - j:143 - j], T[src][:, j::16], j == 0, j == 15)
-        op("ts", [bank + ":l"], [pl], T[pl][:, 0:6], T[bank][:, 96:102], OFF, None, A.add)
+            mm([src, "EE"], [bank + ":l"], T[bank][:, c0:c0 + n], T.EE[:, 15 - j:143 - j], T[src][:, j:U:16], j == 0, j == 15)
+        op("ts", [bank + ":l"], [pl], T[pl][:, 0:n], T[bank][:, c0:c0 + n], OFF, None, A.add)
 
-    def first_half(r, q, p):
-        y, a = "%d" % (p % 2), q // 2
-        PF, pfk, lk = T.PF[:, cs(q, r)], "PF%d.%d" % (r, q), "LP.%d" % q
-        K, kk, c0 = T["K" + y], "K%s:k" % y, V * r + U * q
+    def prepare(r, q):
+        y, (U, st) = "%d" % (q % 2), UNITS[q % 2][1:3]
+        v, w, C = slice(0, U * st), slice(0, U), 128 // st
+        PF, pfk, lk, c0 = T.PF[:, cs(q, r)], "PF%d.%d" % (r, q), "LP.%d" % q, cs(q, r).start
         if r:
             op("ts", [pfk], [lk], T.LP[:, cs(q)], PF, OFF, None, A.add, w=0.5)
-        repeat(p, r, q)
-        op("tt", [pfk], ["DF" + y], T["DF" + y][:], T.PF[:, c0:c0 + U:2], T.PF[:, c0 + 1:c0 + U:2], A.not_equal)
+        DF = T["DF" + y][:, 0:U // 2]
+        op("tt", [pfk], ["DF" + y], DF, T.PF[:, c0:c0 + U:2], T.PF[:, c0 + 1:c0 + U:2], A.not_equal)
         for j in range(2):
-            mm(["DF" + y, "TRI"], ["CF:n"], T.CF[:, 256 + j:352:2], T.TRI[:], T["DF" + y][:], j == 0, j == 1)
-        op("act", ["CF:n", "ZB"], ["ZZ" + y], T["ZZ" + y][:], T.CF[:, 256:352], F.Relu, bias=T.ZB[:, 0:1], scale=-1.0)
-        op("ts", [pfk], ["HP" + y], T["HP" + y][:], PF, OFF + 8256.0 - 31.5, None, A.add, w=0.5)
-        distances(p, r, 0, q, T.LP, lk)
-        ZK, OK, zk, ok = (T.ZK[v, q, 0:128:16], T.ZK[v, q, :]), T.OK[v, q, 0:128], "ZK.%d" % q, "OK.%d" % q
+            mm(["DF" + y, "TRI"], ["CF:n"], T.CF[:, 256 + j:256 + U:2], T.TRI[:], DF, j == 0, j == 1)
+        op("act", ["CF:n", "ZB"], ["ZZ" + y], T["ZZ" + y][:, w], T.CF[:, 256:256 + U], F.Relu, bias=T.ZB[:, 0:1], scale=-1.0)
+        op("ts", [pfk], ["HP" + y], T["HP" + y][:, w], PF, OFF + 8320.0 - 31.5, None, A.add, w=0.5)
+
+    def first_half(r, q, p):
+        y, a, (U, st) = "%d" % (q % 2), q // 2, UNITS[q % 2][1:3]
+        v, w, C, L = slice(0, U * st), slice(0, U), 128 // st, 8 // st
+        PF, pfk, kb = T.PF[:, cs(q, r)], "PF%d.%d" % (r, q), KEYS[q]
+        K, kk = T[kb], kb + ":k"
+        distances(p, r, 0, q, T.LP, "LP.%d" % q)
         SL, YY, OH = T["SL" + y], T["YY" + y], T["OH" + y]
-        op("scan", [kk, "RS"], ["SL" + y], SL[v, :], T.RS[v, :], K[v, 128:384], 0.0, A.add, A.min)
-        op("ts", ["SL" + y], ["YY" + y], YY[v, :], SL[v, 15:256:16], RND, RND, A.add, A.subtract)
+        op("scan", [kk, "RS"], ["SL" + y], SL[v, 0:2 * C], T.RS[v, 0:2 * C], K[v, C:3 * C], 0.0, A.add, A.min)
+        op("ts", ["SL" + y], ["YY" + y], YY[v, 0:2 * L], SL[v, 15:2 * C:16], RND, RND, A.add, A.subtract)
         if q % 2 == 0:
-            mm(["ZER", "ONE"], ["HI:h"], T.HI[:], T.ZER[:], T.ONE[:, 0:96], True, False)
-        for j in range(8):
+            mm(["ZER", "ONE"], ["HI:h"], T.HI[:, 0:96], T.ZER[:], T.ONE[:, 0:96], True, False)
+        for j in range(L):
             oh = ["OH%s.%d.%d" % (y, j, d) for d in range(2)]
-            for d, c0, c1 in ((0, 0, 64), (1, 64, 112)):
-                m = 8 * d + j
-                op("ts", ["SL" + y, "YY" + y, "IOM"], [oh[d]], OH[v, j, c0:c1], T.IOM[v, 0:c1 - c0], YY[v, m:m + 1],
-                   SL[v, 16 * m + 15:16 * m + 16], A.add, A.is_equal, w=0.5)
+            for d, e0, e1 in ((0, 0, 64), (1, 64, 112)):
+                m = L * d + j
+                op("ts", ["SL" + y, "YY" + y, "IOM"], [oh[d]], OH[v, j, e0:e1], T.IOM[v, 0:e1 - e0], YY[v, m:m + 1],
+                   SL[v, 16 * m + 15:16 * m + 16], A.add, A.is_equal)
             for d in range(2):
-                mm(oh, ["HI:h"], T.HI[64 * d:64 * d + 64, j % 4, :], OH[v, j, 0:64], OH[v, j, 64 + d:112:2], False, False)
+                mm(oh, ["HI:h"], T.HI[half(d), 24 * (j % 4):24 * (j % 4) + 24], OH[v, j, 0:64], OH[v, j, 64 + d:112:2], False, False)
         if q % 2:
-            mm(["ZER", "ONE"], ["HI:h"], T.HI[:], T.ZER[:], T.ONE[:, 0:96], False, True)
+            mm(["ZER", "ONE"], ["HI:h"], T.HI[:, 0:96], T.ZER[:], T.ONE[:, 0:96], False, True)
             spread(2 * r + a)
-        one_hot(K[v, 0:128], kk, "S3" + y, "S4" + y, ZK, zk, OK, ok)
-        mm([ok, "OK.e", "IDB"], ["PB:t"], T.PB[:, v], T.OK[v, q, 1:129], I96, True, True)
-        op("tt", ["PB:t", pfk], ["SQ" + y], T["SQ" + y][:], T.PB[:, v], PF, A.mult)
-        to_list("PB", "SQ" + y, "PM" + y)
-        op("cp", ["PM" + y, "PU%d.0" % a, "PU%d.1" % a], ["CU.%d" % q], T.CU[:, cs(q)], T["PU%d" % a][:, 0:W].indirect(T["PM" + y][:, 0:6]), w=GA)
+        s1, s2, zk, ok, ZK = "S3" + y, "S4" + y, "ZK.%d" % q, "OK.%d" % q, T.ZK[v, q, 0:C:16]
+        if r:
+            op("tt", [kk, "FR.%d" % q], [kk], K[v, 0:C], K[v, 0:C], T.FR[v, q, 0:C], A.subtract)
+        op("scan", [kk, "RS"], [s1], T[s1][v, 0:C], T.RS[v, 0:C], K[v, 0:C], 0.0, A.add, A.min)
+        op("act", [s1], [zk], ZK, T[s1][v, 15:C:16], F.Copy)
+        op("scan", [zk, "KP"], [s2], T[s2][v, 0:C], T.KP[v, 0:C], T.ZK[v, q, 0:C], 0.0, A.mult, A.add)
+        op("tt", [kk, s2], [ok], T.OK[v, q, 0:C], K[v, 0:C], T[s2][v, 0:C], A.is_equal)
+        if r:
+            op("tt", [zk, "CL0", "CL1", "CL2"], [zk], ZK, ZK, T.CL[v, 8 * (st - 1):8 * (st - 1) + L], A.max)
+        turn(q, [ok, "IDB"], kb + ":t", lambda pc: K[pc, 384:384 + U], lambda pv, c: T.OK[pv, q, c], 1, T.IDB, True, True)
+        op("tt", [kb + ":t", pfk], ["SQ" + y], T["SQ" + y][:, w], K[:, 384:384 + U], PF, A.mult)
+        to_list(kb, 0, "SQ" + y, "PM" + y, U)
+        op("cp", ["PM" + y, "PU%d.0" % a, "PU%d.1" % a], ["CU.%d" % q], T.CU[:, cs(q)],
+           T["PU%d" % a][:, 0:W].indirect(T["PM" + y][:, 0:U // 16]), w=GA)
         op("ts", ["CU.%d" % q], ["CD.%d" % q], T.CD[:, cs(q)], T.CU[:, cs(q)], -OFF, None, A.add, w=0.5)
         if r == RO - 1:
             op("ts", [pfk], ["YP.%d" % q], T.YP[:, cs(q)], PF, OFF, None, A.add)
 
     def spread(m):
         fs, FS = "FS%d" % m, T.FS[:, m, :]
-        op("ts", ["HI:h"], [fs], FS, T.HI[:], 0.0, None, A.not_equal)
+        op("ts", ["HI:h"], [fs], FS, T.HI[:, 0:96], 0.0, None, A.not_equal)
         s = send([fs], [RemoteDMATransfer(dst_ids=[to(c) for c in peers], dma_engine_mask=bits(efl), remote_sem=T.sem["fl%d%d" % (m, rank)],
                                           srcs=[FS], dsts=[T.FL[:, m, rank, :] for c in peers])], len(efl))
         for d in range(1, NR):
@@ -388,7 +449,7 @@ def rank_program(g, core, T, topo):
             arrives("fl%d%d" % (m, k), len(efl), ["FL%d.%d" % (m, k)], s, XL[0] + XL[1] * d)
 
     def cuts(r, a):
-        m = 2 * r + a
+        m, v = 2 * r + a, slice(0, 96)
         cnt, a0, A0 = T.CF[v, 128:256], "A0.%d" % a, T.A0[v, a, :]
         others = [(rank - d) % NR for d in range(1, NR)]
         mm(["ONE", "CY"], ["CF:c"], cnt, T.ONE[0:1, v], T.CY[0:1, :], True, False)
@@ -404,52 +465,59 @@ def rank_program(g, core, T, topo):
             dma("y", ["YC%d" % a], [], T.yc[4 * a:4 * a + 4, :], T.YC[v, a, :])
 
     def second_half(r, q, p):
-        y, a, xk, x = "%d" % (p % 2), q // 2, "LX%d.%d" % (r, q), T.LX[:, cs(q, r)]
+        y, a, (U, st) = "%d" % (q % 2), q // 2, UNITS[q % 2][1:3]
+        v, w, C = slice(0, U * st), slice(0, U), 128 // st
+        xk, x = "LX%d.%d" % (r, q), T.LX[:, cs(q, r)]
         PF, pfk, oxk, opk = T.PF[:, cs(q, r)], "PF%d.%d" % (r, q), "OX%d.%d" % (r, q), "OP%d.%d" % (r, q)
-        K, kk = T["K" + y], "K%s:k" % y
-        O, o, sp, ob, ot = T["OF" + y][v, :], "OF" + y, "SP" + y, "OB" + y, "OT" + y
-        repeat(p, r, q)
+        K, kk = T["K" + y][v, 0:C], "K%s:k" % y
+        o, sp, pt, s1, s2, zt, tk = "OF" + y, "SP" + y, "PT" + y, "S1" + y, "S2" + y, "ZT" + y, "TK" + y
+        PAd, PAe, PBx = T.PB[:, 0:U], T.PB[:, U:2 * U], T.PB[:, 256:256 + U]
         distances(p, r, 1, q, T.CU, "CU.%d" % q)
-        one_hot(K[v, 0:128], kk, "S1" + y, "S2" + y, (T["ZF" + y][v, 0:128:16], T["ZF" + y][v, :]), "ZF" + y, O, o,
-                limit=(T.ZK[v, q, 0:128:16], "ZK.%d" % q))
-        mm([o, "IDB"], ["PA:t"], T.PA[:, v], O, I96, True, True)
-        mm([o, "IDB"], ["PB:t"], T.PB[:, v], O, I96, True, True)
-        op("tt", ["PA:t", "CD.%d" % q], [sp], T[sp][:], T.PA[:, v], T.CD[:, cs(q)], A.mult)
-        op("act", ["PB:t"], [ob], T[ob][:], T.PB[:, v], F.Copy)
-        for j in range(16):
-            mm([sp, "EE"], ["PA:l"], T.PA[:, 96:102], T.EE[:, 15 - j:143 - j], T[sp][:, j::16], j == 0, j == 15)
-        mm([ob, "BO"], ["PA:k"], T.PA[:, 128:224], T.BO[:], T[ob][:], True, True)
-        mm([pfk, "IDP"], ["PA:d"], T.PA[:, 256:352], T.IDP[:], PF, True, False)
-        mm([sp, "BP"], ["PA:d"], T.PA[:, 256:352], T.BP[:], T[sp][:], False, True)
-        mm(["OK.%d" % q, "IDB"], ["PB:o"], T.PB[:, 128:224], T.OK[v, q, 0:128], I96, True, False)
-        mm([ob, "BO"], ["PB:o"], T.PB[:, 128:224], T.BO[:], T[ob][:], False, True)
-        op("act", ["PB:o"], [ot], T[ot][:], T.PB[:, 128:224], F.Relu, bias=-1.0)
-        op("ts", ["PA:l"], ["PL" + y], T["PL" + y][:, 0:6], T.PA[:, 96:102], OFF, None, A.add)
-        op("tt", ["PL" + y, xk] + txk(a), ["DX" + y], T["DX" + y][:], T["TX%d" % a][:, 0:W].indirect(T["PL" + y][:, 0:6]), x,
+        op("scan", [kk, "RE"], [s1], T[s1][v, 0:C], T.RE[v, 0:C], K, 0.0, A.add, A.max)
+        op("scan", [s1, s1 + ".e", "RE"], [s2], T[s2][v, 0:C], T.RE[v, 0:C], T[s1][v, 15:15 + C], 0.0, A.add, A.max)
+        op("tt", [kk, s2], [o], T[o][v, 0:C], K, T[s2][v, 0:C], A.is_equal)
+        op("tt", [s1, "ZK.%d" % q], [zt], T[zt][v, 0:C:16], T[s1][v, 15:C:16], T.ZK[v, q, 0:C:16], A.is_gt)
+        op("scan", [zt, "KB"], [tk], T[tk][v, 0:C], T.KB[v, 0:C], T[zt][v, 0:C], 0.0, A.mult, A.add, w=0.5)
+        turn(q, [tk, "IDB"], "PA:k", lambda pc: T.PA[pc, 128:128 + U], lambda pv, c: T[tk][pv, c], 0, T.IDB, True, True)
+        turn(q, [o, "IDB"], "PA:t", lambda pc: T.PA[pc, w], lambda pv, c: T[o][pv, c], 0, T.IDB, True, True)
+        op("tt", ["PA:t", "CD.%d" % q], [sp], T[sp][:, w], T.PA[:, w], T.CD[:, cs(q)], A.mult)
+        l = int(r == RO - 1)
+        mm(["ONE", "CB%d0" % l, "CB%d1" % l], ["PB:d"], T.PB[:, 0:2 * U], T.ONE[0:1, 0:128], T.CB[0:1, l, :, w], True, False)
+        for pv, _, pc in parts(q):
+            for key, src in (("OK.%d" % q, T.OK[pv, q, 0:C]), (tk, T[tk][pv, 0:C])):
+                mm([key, "IB0", "IB1"], ["PB:d"], T.PB[pc, 0:2 * U], src, T.IB[pv, :, pv], False, False)
+        for j in range(2):
+            mm([sp, "BP"], ["PB:d"], T.PB[:, U * j:U * j + U], T.BP[:], T[sp][:, w], False, j == 1)
+        if l:
+            for bound, how in ((PAd, A.max), (PAe, A.min)):
+                op("tt", ["PB:d", "YP.%d" % q], ["YP.%d" % q], T.YP[:, cs(q)], bound, T.YP[:, cs(q)], how)
+        else:
+            op("tt", ["PB:d", pfk], [pt], T[pt][:, w], PAd, PF, A.max)
+            op("tt", ["PB:d", pt], [opk], T.OP[:, cs(q, r)], PAe, T[pt][:, w], A.min)
+        to_list("HI", 480, sp, "PL" + y, U)
+        op("tt", ["PL" + y, xk] + txk(a), ["DX" + y], T["DX" + y][:, w], T["TX%d" % a][:, 0:W].indirect(T["PL" + y][:, 0:U // 16]), x,
            A.subtract, w=GA)
-        op("tt", ["DX" + y, "PA:k"], ["DY" + y], T["DY" + y][:], T["DX" + y][:], T.PA[:, 128:224], A.mult)
-        mm([xk, "IDB"], ["PB:x"], T.PB[:, 256:352], T.IDB[:], x, True, False)
-        mm([ob, "B64"], ["PB:x"], T.PB[:, 256:352], T.B64[:], T[ob][:], False, False)
-        mm(["DY" + y, "IDH"], ["PB:x"], T.PB[:, 256:352], T.IDH[:], T["DY" + y][:], False, True)
-        op("act", ["PB:x"], [oxk], T.OX[:, cs(q, r)], T.PB[:, 256:352], F.Identity, bias=-0.2)
-        op("tt", ["PA:d", ot], ["PA:d"], T.PA[:, 256:352], T.PA[:, 256:352], T[ot][:], A.mult)
+        op("tt", ["DX" + y, "PA:k"], ["DY" + y], T["DY" + y][:, w], T["DX" + y][:, w], T.PA[:, 128:128 + U], A.mult)
+        mm([xk, "IDB"], ["PB:x"], PBx, T.IDB[:], x, True, False)
+        turn(q, [tk, "B64"], "PB:x", lambda pc: T.PB[pc, 256:256 + U], lambda pv, c: T[tk][pv, c], 0, T.B64, False, False)
+        mm(["DY" + y, "IDH"], ["PB:x"], PBx, T.IDH[:], T["DY" + y][:, w], False, True)
+        op("ts", ["PB:x"], [oxk], T.OX[:, cs(q, r)], PBx, -0.2, None, A.add)
         if r < RO - 1:
-            op("tt", ["PA:d", pfk], [opk], T.OP[:, cs(q, r)], T.PA[:, 256:352], PF, A.add)
             for key, o, l in ((opk, "OP", "PF"), (oxk, "OX", "LX")):
                 sem = "%s%d%d" % (o, r, q)
                 s = send([key], [RemoteDMATransfer(dst_ids=[to(nxt)], dma_engine_mask=bits(enx), remote_sem=T.sem[sem],
                                                    src=T[o][:, cs(q, r)], dst=T[l][:, cs(q, r + 1)])], len(enx))
                 arrives(sem, len(enx), ["%s%d.%d" % (l, r + 1, q)], s, XL[2])
         else:
-            op("tt", ["PA:d", "YP.%d" % q], ["YP.%d" % q], T.YP[:, cs(q)], T.PA[:, 256:352], T.YP[:, cs(q)], A.add)
             op("act", [oxk], ["YX.%d" % q], T.YX[:, cs(q)], T.OX[:, cs(q, r)], F.Identity, bias=-128.0)
             for j in range(2):
-                c = slice(H * j + U * (q % 2), H * j + U * (q % 2) + U)
-                dma("y", ["YP.%d" % q], [], T.yp[64 * a:64 * a + 64, c], T.YP[64 * j:64 * j + 64, cs(q)])
-                dma("y", ["YX.%d" % q], [], T.yx[64 * a:64 * a + 64, c], T.YX[64 * j:64 * j + 64, cs(q)])
+                c = slice(H * j + UNITS[q % 2][0], H * j + UNITS[q % 2][0] + U)
+                dma("y", ["YP.%d" % q], [], T.yp[half(a), c], T.YP[half(j), cs(q)])
+                dma("y", ["YX.%d" % q], [], T.yx[half(a), c], T.YX[half(j), cs(q)])
 
     for r in range(RO):
         for q in range(4):
+            prepare(r, q)
             first_half(r, q, 8 * r + q)
         for q in range(4):
             if q % 2 == 0:

from concourse.bass import DstId, RemoteDMATransfer
from concourse.mybir import dt, AluOpType, ActivationFunctionType

A = AluOpType
F = ActivationFunctionType
NR, W, V, RO, STEP = 8, 3072, 384, 3, 3
H = 192
UNITS = ((0, 96, 1, 4), (96, 96, 1, 4))
CH = ((0, 64, 96), (0, 64, 96))
VG = {(0, 0, 0, 0, 1)} | {(r, 1, 0, 0, 1) for r in range(RO)}
KEYS = ("K0", "K1", "PA", "PB")
BIG = 33554432.0
LANE = 262144.0
RND = 1610612736.0
FAR = 4096.0
OFF = 1536.0
CUT = 2176.0
GA = 1.56
XL = (1.8, 0.4, 2.2)
WAKE = 0.25
TURNS = 48
PLAN = []
NG = 3

f, b, i, u, h = "float32", "bfloat16", "int32", "uint16", "float16"
SB = {
    "LX": (b, RO * V), "PF": (h, RO * V), "OX": (b, RO * V), "OP": (h, RO * V), "LP": (u, V), "CU": (u, V), "CD": (h, V),
    "PI": (i, V), "YP": (f, V), "YX": (b, V), "YC": (f, 2, 128), "A0": (b, 2, 128), "FS": (b, 2 * RO, 96),
    "FL": (b, 2 * RO, 8, 96), "OK": (b, 4, 136), "ZK": (f, 4, 128), "FR": (b, 4, 128),
    "ONE": (b, 192), "IDB": (b, 128), "IDZ": (b, 3, 128), "IDH": (b, 128), "ID4": (b, 128),
    "BO": (b, 128), "BP": (h, 128), "B64": (b, 128), "BG": (b, 3, 8), "BM": (b, 3, 8), "XT": (b, 3, 128), "TRI": (b, 128),
    "WK": (b, 16, 8), "EE": (h, 144), "IDQ": (h, 128), "IDL": (b, 2, 128), "CK": (b, 3, 128), "CE": (b, 128),
    "CY": (b, 128), "RS": (f, 256), "RE": (f, 128), "KP": (f, 128), "KB": (b, 128), "CL": (f, 16), "LN": (b, 128),
    "RW": (b, 128), "ZB": (f, 1), "ZI": (i, 1), "IOM": (b, 64), "IB": (b, 2, 128), "CB": (b, 2, 2, 128), "ZER": (b, 128),
}
for n in range(NG):
    SB["G%d" % n] = (b, 2048)
TWO = {"TX": (b, W), "PU": (i, W), "M": (b, 2048), "DF": (b, 64), "ZZ": (b, 128), "S1": (f, 144), "S2": (f, 128),
       "ZT": (b, 128), "OF": (b, 128), "SP": (h, 128), "SQ": (h, 128), "HP": (b, 128), "YY": (f, 16), "SL": (f, 256),
       "OH": (b, 8, 112), "PL": (u, 8), "TK": (b, 128), "PT": (h, 128), "DX": (b, 128), "DY": (b, 128), "S3": (f, 128),
       "S4": (f, 128), "PM": (u, 8)}
for n, s in TWO.items():
    SB.update({n + "0": s, n + "1": s})
SCRATCH = {n: ("sbuf", [128] + list(s[1:]), s[0]) for n, s in SB.items()}
BANKS = {"K0": [512], "K1": [512], "PA": [512], "PB": [512], "HI": [512], "CF": [512]}
BANKS.update({"XR%d" % n: [512 // UNITS[n][3], UNITS[n][3]] for n in range(2)})
SCRATCH.update({n: ("psum", [128] + s, f) for n, s in BANKS.items()})
SEMAPHORES = ["cv", "cs", "cp", "cg", "loc"] + ["d%d" % n for n in range(50)] + \
    ["fl%d%d" % (n, k) for n in range(2 * RO) for k in range(NR)] + \
    ["%s%d%d" % (o, s, n) for o in ("OP", "OX") for s in range(RO - 1) for n in range(4)]


def make_plan(g, T):
    eng = {"v": g.vector, "s": g.scalar, "p": g.tensor, "g": g, "y": g.sync}
    nodes = []
    wr, rd, touch, last = {}, {}, {}, {}
    nd = [0, 0]

    def add(e, reads, writes, emit, sem, inc, cost, acc=False, lag=WAKE, own=True, after=()):
        deps, me = set(after), len(nodes)
        bks = sorted(set(k.split(":")[0] for k in list(reads) + list(writes) if k.split(":")[0] in BANKS))
        for bk in bks:
            t = touch.setdefault(bk, [e, [], []])
            if t[0] != e:
                t[:] = [e, [], t[1]]
            deps.update(t[2])
            t[1].append(me)
        for k in reads:
            if k in wr:
                deps.add(wr[k])
        for k in writes:
            if not acc:
                if k in wr:
                    deps.add(wr[k])
                deps.update(rd.get(k, ()))
        nodes.append({"e": e, "w": (list(writes) + list(reads))[0], "deps": sorted(deps), "emit": emit, "sem": sem, "inc": inc,
                      "cost": cost, "lag": lag, "own": own})
        if e == "p":
            for bk in bks:
                if bk in last:
                    nodes[me]["prev"] = last[bk]
                last[bk] = me
        for k in reads:
            rd.setdefault(k, []).append(me)
        for k in writes:
            wr[k] = me
            rd[k] = []
        return me

    fns = {"mm": ("p", g.tensor.matmul), "tt": ("v", g.vector.tensor_tensor), "ts": ("v", g.vector.tensor_scalar),
           "cp": ("v", g.vector.tensor_copy), "ms": ("v", g.vector.memset), "scan": ("v", g.vector.tensor_tensor_scan),
           "act": ("s", g.scalar.activation), "iota": ("g", g.iota), "asel": ("g", g.affine_select)}

    def op(name, reads, writes, out, *args, acc=False, w=1.0, **kw):
        e, fn = fns[name]
        n = 1
        for s in out.shape[1:]:
            n *= int(s)
        if e == "p":
            cost = 0.00042 * max(64, n) * w
        elif e == "g":
            cost = 0.15 + 0.0017 * n
        else:
            if name == "tt" and w == 1.0 and not any(k.split(":")[0] in BANKS for k in reads):
                w = 2.0
            cost = 0.00085 * max(64, n * w) + (0.08 if e == "s" else 0.0)
        return add(e, reads, writes, lambda: fn(out, *args, **kw), "c" + e, 1, cost, acc=acc)

    def dma(e, reads, writes, out, in_, lag=2.3):
        nd[0] += 1
        return add(e, reads, writes, lambda: eng[e].dma_start(out, in_), "d%d" % (nd[0] - 1), 16, 0.06, lag=lag)

    def send(reads, transfers, n):
        return add("g", reads, [], lambda: g.remote_dma_fused(transfers, local_sem=T.sem.loc), "loc", n, 0.7, own=False)

    def arrives(sem, n, writes, sent, lag):
        add("x", [], writes, None, sem, n, 0.0, lag=lag, after=[sent])

    def finish(last=True):
        n = len(nodes)
        if not last:
            nd[1] = n
            return
        succ = [[] for _ in range(n)]
        for k, x in enumerate(nodes):
            x["all"] = sorted(set(x["deps"] + ([x["prev"]] if "prev" in x else [])))
            for d in x["all"]:
                succ[d].append(k)

        def gap(d, k):
            return 0.0 if nodes[k].get("prev") == d else nodes[d]["lag"]

        def replay(seq, slow):
            end, free = [0.0] * n, {e: 0.0 for e in "vspgyx"}
            for k in seq:
                x = nodes[k]
                t = max([end[d] + gap(d, k) for d in x["all"]] + [0.0])
                if x["e"] != "x":
                    t = free[x["e"]] = max(t, free[x["e"]]) + x["cost"] * (slow if x["e"] in "vsp" else 1.0)
                end[k] = t
            return max(end[k] + nodes[k]["lag"] for k in seq)

        def place(seq, before, wait, first):
            start, busy = [0.0] * n, {e: [] for e in eng}
            for k in seq:
                x = nodes[k]
                t = max([start[d] + nodes[d]["cost"] + wait(d, k) for d in before[k]] + [first(k)])
                if x["e"] != "x":
                    lst = busy[x["e"]]
                    j = len(lst)
                    while j and lst[j - 1][1] > t:
                        j -= 1
                    while j < len(lst) and lst[j][0] < t + x["cost"]:
                        t = max(t, lst[j][1])
                        j += 1
                    lst.insert(j, (t, t + x["cost"]))
                start[k] = t
            return start

        pred = [x["all"] for x in nodes]
        prio = [0.0] * n
        for k in range(n - 1, -1, -1):
            prio[k] = nodes[k]["cost"] + max([prio[s] + gap(k, s) for s in succ[k]] + [nodes[k]["lag"]])
        best = None
        for turn in range(0 if PLAN else TURNS):
            start = place(sorted(range(n), key=lambda k: (0, k) if k < nd[1] else (1, -prio[k], k)), pred, gap, lambda k: 0.0)
            end = [start[k] + nodes[k]["cost"] for k in range(n)]
            seq = sorted(range(n), key=lambda k: (start[k], k))
            span = (replay(seq, 1.0) + replay(seq, 1.4) / 1.3) / 2
            if best is None or span < best[0]:
                best = (span, start)
            end = [best[1][k] + nodes[k]["cost"] for k in range(n)] if turn % 3 == 2 else end
            more = [1.0 + 0.4 * ((k * 7919 + turn * 104729) % 1009 / 1009.0 - 0.5) if turn % 3 == 2 else 1.0 for k in range(n)]
            back = place(sorted(range(n), key=lambda k: (-end[k], -k)), succ, lambda d, k: gap(k, d) * more[k], lambda k: nodes[k]["lag"])
            prio = [back[k] + nodes[k]["cost"] for k in range(n)]
        if not PLAN:
            PLAN.extend([sorted(range(n), key=lambda k: (best[1][k], k)), best[0], best[1], nodes])
        order = PLAN[0]
        cnt, known, event, clock = {}, {e: {} for e in eng}, {}, {}
        for k in order:
            x = nodes[k]
            e = x["e"]
            if e == "x":
                event[k] = (x["sem"], x["inc"])
                clock[event[k]] = {x["sem"]: x["inc"]}
                continue
            need = {}
            for d in x["deps"]:
                s, m = event[d]
                need[s] = max(need.get(s, 0), m)
            todo = [(s, m) for s, m in need.items() if known[e].get(s, 0) < m]
            todo = [p for p in todo if not any(q != p and clock[q].get(p[0], 0) >= p[1] for q in todo)]
            for p in todo:
                eng[e].wait_ge(T.sem[p[0]], p[1])
                for s, m in clock[p].items():
                    known[e][s] = max(known[e].get(s, 0), m)
            ins = x["emit"]()
            cnt[x["sem"]] = cnt.get(x["sem"], 0) + x["inc"]
            if x["own"]:
                ins.then_inc(T.sem[x["sem"]], x["inc"])
            event[k] = (x["sem"], cnt[x["sem"]])
            clock[event[k]] = dict(known[e])
            clock[event[k]][x["sem"]] = cnt[x["sem"]]
        for s, m in cnt.items():
            if known["g"].get(s, 0) < m:
                g.wait_ge(T.sem[s], m)

    return op, dma, send, arrives, finish


def rank_program(g, core, T, topo):
    rank = T.rank_of(core)
    if rank is None:
        return
    op, dma, send, arrives, finish = make_plan(g, T)
    peers = [T.cores[(rank + d) % NR] for d in range(1, NR)]
    nxt = T.cores[(rank + STEP) % NR]
    efl = [e for e in topo.engines(core, peers[0]) if all(e in topo.engines(core, c) for c in peers)]
    enx = topo.engines(core, nxt)

    def to(c):
        return DstId(rid=topo.addr(c)[0], pnc=topo.addr(c)[1])

    def bits(es):
        return sum(1 << e for e in es)

    def cs(q, r=0):
        c = V * r + H * (q // 2) + UNITS[q % 2][0]
        return slice(c, c + UNITS[q % 2][1])

    def txk(a):
        return ["TX%d.0" % a, "TX%d.1" % a]

    def half(j):
        return slice(64 * j, 64 * j + 64)

    for what, a, lag in (("PI", 0, 2.0), ("TX", 0, 4.2), ("X", 0, 4.3), ("PI", 1, 4.6), ("X", 1, 4.7), ("TX", 1, 8.0),
                         ("PU", 0, 13.0), ("PU", 1, 19.0)):
        for j in range(2):
            out, src = {"PI": (T.PI, T.p0), "X": (T.LX, T.x0), "TX": (T["TX%d" % a], T.tx), "PU": (T["PU%d" % a], T.pu)}[what]
            if what in ("PI", "X"):
                out, src = out[half(j), H * a:H * a + H], src[half(a), H * j:H * j + H]
            else:
                out, src = out[half(j), :], src[half(a), :]
            dma("y" if j or lag > 5 else "s", [], ["%s%d.%d" % (what, a, j)], out, src, lag=lag)
        if what == "PU":
            dma("y", [], ["A0.%d" % a], T.A0[0:96, a, :], T.tx[64 * a:64 * a + 64:16, :], lag=lag)

    def convert(a):
        c = slice(H * a, H * a + H)
        pi = ["PI%d.0" % a, "PI%d.1" % a]
        op("cp", pi, ["LP.%d" % (2 * a), "LP.%d" % (2 * a + 1)], T.LP[:, c], T.PI[:, c])
        op("ts", pi, ["PF0.%d" % (2 * a), "PF0.%d" % (2 * a + 1)], T.PF[:, c], T.PI[:, c], -OFF, None, A.add)
        op("ts", ["X%d.0" % a, "X%d.1" % a], ["LX0.%d" % (2 * a), "LX0.%d" % (2 * a + 1)], T.LX[:, c], T.LX[:, c], 128.0, None, A.add, w=0.5)

    convert(0)
    lo = {"allow_small_or_imprecise_dtypes": True}
    op("ms", [], ["ONE"], T.ONE[:], 1.0, w=0.5)
    op("asel", ["ONE"], ["IDB"], T.IDB[:], T.ONE[:, 0:128], [[-1, 128]], A.is_equal, 0.0, 0, 1)
    op("asel", ["ONE"], ["BO"], T.BO[:], T.ONE[:, 0:128], [[-16, 8], [0, 16]], A.is_ge, 0.0, 0, 1)
    op("asel", ["BO"], ["BO"], T.BO[:], T.BO[:], [[16, 8], [0, 16]], A.is_ge, 0.0, 15, -1)
    op("iota", [], ["RW"], T.RW[:], [[0, 8], [1, 16]], 0, 0, **lo)
    op("iota", [], ["LN"], T.LN[:], [[-1, 8], [0, 16]], 0, 0, **lo)
    op("asel", ["BO"], ["TRI"], T.TRI[:], T.BO[:], [[1, 128]], A.is_ge, 0.0, 0, -1)
    op("iota", [], ["ZI"], T.ZI[:], [[0, 1]], 0, 1)
    op("iota", [], ["IOM"], T.IOM[:], [[1, 64]], 0, 0, **lo)
    op("iota", [], ["WK"], T.WK[:], [[-96, 16], [0, 8]], 1632, 0, **lo)
    op("asel", ["WK"], ["WK"], T.WK[:], T.WK[:], [[0, 16], [-16, 8]], A.is_equal, 0.0, 0, 1)
    XTK, BGK, BMK, CEK = [["%s%d" % (n, j) for j in range(3)] for n in ("XT", "BG", "BM", "CE")]
    for j, c in enumerate((32.0, 2048.0, 2048.0)):
        op("act", ["IDB"], ["IDZ%d" % j], T.IDZ[:, j, :], T.IDB[:], F.Copy, scale=4096 * c)
        op("act", ["BO"], [XTK[j]], T.XT[:, j, :], T.BO[:], F.Copy, scale=c)
        op("ts", ["BO"], [BMK[j]], T.BM[:, j, :], T.BO[:, 0:128:16], -2 * c, None, A.mult)
        op("ts", ["BO"], [BGK[j]], T.BG[:, j, :], T.BO[:, 0:128:16], c, None, A.mult)
    op("ms", [], ["CK"], T.CK[0:64], 0.0, w=0.5)
    for j, c, d in ((0, 1.0, None), (1, 128.0, OFF + 8320.0), (2, 128.0, -130.0)):
        op("ts", ["RW", "CK"], ["CK.%d" % j], T.CK[0:1, j, :], T.RW[0:1, :], c, None, A.mult, w=0.5)
        if j:
            op("ms", [], ["CK,%d" % j], T.CK[64:65, j, :], d)
    op("ts", ["LN"], ["CK,0"], T.CK[64:65, 0, :], T.LN[64:65, :], LANE, None, A.mult, w=0.5)
    op("ms", ["CK"], ["CK;"], T.CK[32:33, 1:3, :], -8388608.0)
    op("tt", ["IDZ%d" % j for j in range(3)] + ["CK;"] + ["CK%s%d" % (s, j) for s in ".," for j in range(3)], ["IDZ"],
       T.IDZ[0:65], T.IDZ[0:65], T.CK[0:65], A.add)
    op("ms", [], ["TRI"], T.TRI[:, 0:128:16], 0.0)
    op("ts", ["ZI"], ["ZI"], T.ZI[:], T.ZI[:], 15, None, A.bitwise_and)
    op("ts", ["ZI"], ["ZB"], T.ZB[:], T.ZI[:], 15.0, None, A.not_equal)
    op("ms", [], ["ZER"], T.ZER[:], 0.0, w=0.5)
    for n, src, c in (("IDQ", "IDB", 1.0), ("BP", "BO", 1.0)):
        op("ts", [src], [n], T[n][:], T[src][:], c, None, A.mult, w=0.5)
    for j, c in enumerate((-1.0, 1.0 / 64)):
        op("act", ["IDB"], ["IDL%d" % j], T.IDL[:, j, :], T.IDB[:], F.Copy, scale=c)
    for n, c in (("IDH", 0.5), ("ID4", 4096.0), ("B64", 64.0)):
        op("act", ["IDB"], [n], T[n][:], T.IDB[:], F.Copy, scale=c)
    for n, c0, c1 in (("RS", 0.0, BIG), ("RE", 0.0, -BIG), ("KP", 1.0, 0.0), ("KB", 1.0, 0.0)):
        op("ms", [], [n], T[n][:], c0)
        op("ms", [], [n], T[n][:, 0::16], c1)
    for j in range(2):
        op("act", ["IDB"], ["IB%d" % j], T.IB[:, j, :], T.IDB[:], F.Copy, scale=FAR * (1 - 2 * j))
        for l in range(2):
            op("ms", [], ["CB%d%d" % (l, j)], T.CB[0:1, l, j, :], l * OFF - 2 * FAR * (1 - 2 * j))
    op("ms", [], ["ZK.%d" % q for q in range(4)], T.ZK[:], 0.0)
    op("ms", [], ["OK.%d" % q for q in range(4)], T.OK[:], 0.0, w=0.5)
    op("ms", [], ["EE"], T.EE[:], 0.0, w=0.5)
    op("ms", [], [CEK[0]], T.CE[0:64, :], 0.0, w=0.5)
    for j in range(2):
        nc = 128 // UNITS[j][2]
        op("ms", [], ["ZT%d" % j], T["ZT%d" % j][:], 0.0, w=0.5)
        op("ms", [], ["S1%d.e" % j], T["S1%d" % j][:, nc:nc + 16], -BIG)
    op("ms", [], ["CY"], T.CY[0:1, :], -8192.0)
    op("cp", ["BO"], ["EE"], T.EE[:, 15:143:16], T.BO[:, 0:128:16])
    op("ts", ["RW", CEK[0]], [CEK[1]], T.CE[0:1, :], T.RW[0:1, :], -1.0, None, A.mult, w=0.5)
    op("ts", ["LN"], [CEK[2]], T.CE[64:65, :], T.LN[64:65, :], LANE, None, A.mult, w=0.5)
    op("ts", ["LN"], ["CL0"], T.CL[:, 0:8], T.LN[:, 0:128:16], LANE, -65280.0, A.mult, A.add)
    for j in range(2):
        op("ts", ["LN"], ["CL%d" % (1 + j)], T.CL[half(j), 8:12], T.LN[half(j), 64 * j:64 * j + 64:16], LANE, -65280.0, A.mult, A.add)
    op("ms", [], ["WK"], T.WK[:, 0, :], 0.0)
    finish(False)
    convert(1)

    def mm(reads, writes, out, lhsT, rhs, start, stop):
        return op("mm", reads, writes, out, lhsT, rhs, start, stop, acc=not start)

    def parts(q):
        U, st = UNITS[q % 2][1:3]
        return [(slice(U * j, U * j + U), slice(8 // st * j, 8 // st * (j + 1)), slice(128 // st * j, 128 // st * (j + 1))) for j in range(st)]

    def turn(q, reads, key, out, src, c0, ident, start, stop):
        for pv, _, pc in parts(q):
            mm(reads, [key], out(pc), src(pv, slice(c0, c0 + pc.stop - pc.start)), ident[pv, pv], start, stop)

    def distances(p, r, step, q, lists, lkey):
        y, a, (U, st, m), ch = "%d" % (q % 2), q // 2, UNITS[q % 2][1:], CH[q % 2]
        kb = "K" + y if step else KEYS[q]
        K, M, XR, X, G = T[kb], T["M" + y], T["XR" + y], T.LX[:, cs(q, r)], T["G%d" % (p % NG)]
        kk, mk, xr, xk, gk = kb + ":k", "M%s." % y, "XR%s:" % y, "LX%d.%d" % (r, q), "G%d." % (p % NG)
        nc, C, R = len(ch) - 1, 128 // st, 1 if step else 3
        k0, c0 = 1 - step, cs(q).start
        if st > 1:
            mm(["ZER", "ONE"], [kk], K[:, 0:R * C], T.ZER[:], T.ONE[:, 0:R * C], True, False)
        for pv, _, pc in parts(q):
            mm([xk] + XTK, [kk], K[pv, 0:R * C], X, T.XT[:, 0:R, pc], st == 1, False)
            if step:
                mm(["ONE"] + CEK, [kk], K[pv, 0:C], T.ONE[0:65, 0:U], T.CE[0:65, pc], False, False)
        for j in range(m):
            mm(["IDB", xk], [xr + "%d" % j], XR[:, 0:U, j], T.IDB[:], X, True, True)
        for c in range(nc):
            src = T["TX%d" % a][:, 0:W].indirect(lists[:, c0 + ch[c]:c0 + ch[c + 1]])
            dst = G[:, 16 * ch[c]:16 * ch[c + 1]]
            if (r, step, a, q % 2, c) in VG:
                op("ts", txk(a) + [lkey], [gk + "%d" % c], dst, src, 128.0, None, A.add, w=GA)
            else:
                op("act", txk(a) + [lkey], [gk + "%d" % c], dst, src, F.Identity, bias=128.0, w=GA)
        gs = [gk + "%d" % c for c in range(nc)]
        for k in range(k0, 16):
            for pv, pl, _ in parts(q):
                mm(gs + BGK, [kk], K[pv, k:R * C:16], G[:, k:16 * U:16], T.BG[:, 0:R, pl], False, False)
        if step == 0 and r:
            for pv, pl, _ in parts(q):
                for k in range(16):
                    mm(gs + ["WK"], ["CF:f"], T.CF[pv, k:C:16], G[:, k:16 * U:16], T.WK[:, k, pl], k == 0, k == 15)
            op("act", ["CF:f"], ["FR.%d" % q], T.FR[0:U * st, q, 0:C], T.CF[0:U * st, 0:C], F.Relu, bias=-393216.0)
        n = 16 // m
        for c in range(nc):
            for j in range(n):
                s = slice(16 * ch[c] + j, 16 * ch[c + 1], n)
                op("tt", [gk + "%d" % c] + [xr + "%d" % l for l in range(m)], [mk + "%d.%d" % (c, j)], M[:, s], G[:, s],
                   XR[:, ch[c]:ch[c + 1], :], A.max)
        for j in range(n):
            if j == n - 1 and step == 0:
                for pv, _, pc in parts(q):
                    mm(["ZZ" + y, "IDZ"], [kk], K[pv, 0:R * C], T["ZZ" + y][:, 0:U], T.IDZ[:, :, pc], False, False)
            for k in range(j or n * k0, 16, n):
                for pv, pl, _ in parts(q):
                    mm([mk + "%d.%d" % (c, j) for c in range(nc)] + BMK, [kk], K[pv, k:R * C:16], M[:, k:16 * U:16], T.BM[:, 0:R, pl],
                       False, step == 1 and k == 15 and st == 1)
        if step == 0:
            for pv, _, pc in parts(q):
                mm(["PF%d.%d" % (r, q), "IDQ"], [kk], K[pv, C:2 * C], T.PF[:, cs(q, r)], T.IDQ[:, pc], False, False)
                mm(["HP" + y, "IDL0", "IDL1"], [kk], K[pv, C:3 * C], T["HP" + y][:, 0:U], T.IDL[:, :, pc], False, st == 1)
        if st > 1:
            mm(["ZER", "ONE"], [kk], K[:, 0:64], T.ZER[:], T.ONE[:, 0:64], False, True)

    def to_list(bank, c0, src, pl, U):
        n = U // 16
        for j in range(16):
            mm([src, "EE"], [bank + ":l"], T[bank][:, c0:c0 + n], T.EE[:, 15 - j:143 - j], T[src][:, j:U:16], j == 0, j == 15)
        op("ts", [bank + ":l"], [pl], T[pl][:, 0:n], T[bank][:, c0:c0 + n], OFF, None, A.add)

    def prepare(r, q):
        y, (U, st) = "%d" % (q % 2), UNITS[q % 2][1:3]
        v, w, C = slice(0, U * st), slice(0, U), 128 // st
        PF, pfk, lk, c0 = T.PF[:, cs(q, r)], "PF%d.%d" % (r, q), "LP.%d" % q, cs(q, r).start
        if r:
            op("ts", [pfk], [lk], T.LP[:, cs(q)], PF, OFF, None, A.add, w=0.5)
        DF = T["DF" + y][:, 0:U // 2]
        op("tt", [pfk], ["DF" + y], DF, T.PF[:, c0:c0 + U:2], T.PF[:, c0 + 1:c0 + U:2], A.not_equal)
        for j in range(2):
            mm(["DF" + y, "TRI"], ["CF:n"], T.CF[:, 256 + j:256 + U:2], T.TRI[:], DF, j == 0, j == 1)
        op("act", ["CF:n", "ZB"], ["ZZ" + y], T["ZZ" + y][:, w], T.CF[:, 256:256 + U], F.Relu, bias=T.ZB[:, 0:1], scale=-1.0)
        op("ts", [pfk], ["HP" + y], T["HP" + y][:, w], PF, OFF + 8320.0 - 31.5, None, A.add, w=0.5)

    def first_half(r, q, p):
        y, a, (U, st) = "%d" % (q % 2), q // 2, UNITS[q % 2][1:3]
        v, w, C, L = slice(0, U * st), slice(0, U), 128 // st, 8 // st
        PF, pfk, kb = T.PF[:, cs(q, r)], "PF%d.%d" % (r, q), KEYS[q]
        K, kk = T[kb], kb + ":k"
        distances(p, r, 0, q, T.LP, "LP.%d" % q)
        SL, YY, OH = T["SL" + y], T["YY" + y], T["OH" + y]
        op("scan", [kk, "RS"], ["SL" + y], SL[v, 0:2 * C], T.RS[v, 0:2 * C], K[v, C:3 * C], 0.0, A.add, A.min)
        op("ts", ["SL" + y], ["YY" + y], YY[v, 0:2 * L], SL[v, 15:2 * C:16], RND, RND, A.add, A.subtract)
        if q % 2 == 0:
            mm(["ZER", "ONE"], ["HI:h"], T.HI[:, 0:96], T.ZER[:], T.ONE[:, 0:96], True, False)
        for j in range(L):
            oh = ["OH%s.%d.%d" % (y, j, d) for d in range(2)]
            for d, e0, e1 in ((0, 0, 64), (1, 64, 112)):
                m = L * d + j
                op("ts", ["SL" + y, "YY" + y, "IOM"], [oh[d]], OH[v, j, e0:e1], T.IOM[v, 0:e1 - e0], YY[v, m:m + 1],
                   SL[v, 16 * m + 15:16 * m + 16], A.add, A.is_equal)
            for d in range(2):
                mm(oh, ["HI:h"], T.HI[half(d), 24 * (j % 4):24 * (j % 4) + 24], OH[v, j, 0:64], OH[v, j, 64 + d:112:2], False, False)
        if q % 2:
            mm(["ZER", "ONE"], ["HI:h"], T.HI[:, 0:96], T.ZER[:], T.ONE[:, 0:96], False, True)
            spread(2 * r + a)
        s1, s2, zk, ok, ZK = "S3" + y, "S4" + y, "ZK.%d" % q, "OK.%d" % q, T.ZK[v, q, 0:C:16]
        if r:
            op("tt", [kk, "FR.%d" % q], [kk], K[v, 0:C], K[v, 0:C], T.FR[v, q, 0:C], A.subtract)
        op("scan", [kk, "RS"], [s1], T[s1][v, 0:C], T.RS[v, 0:C], K[v, 0:C], 0.0, A.add, A.min)
        op("act", [s1], [zk], ZK, T[s1][v, 15:C:16], F.Copy)
        op("scan", [zk, "KP"], [s2], T[s2][v, 0:C], T.KP[v, 0:C], T.ZK[v, q, 0:C], 0.0, A.mult, A.add)
        op("tt", [kk, s2], [ok], T.OK[v, q, 0:C], K[v, 0:C], T[s2][v, 0:C], A.is_equal)
        if r:
            op("tt", [zk, "CL0", "CL1", "CL2"], [zk], ZK, ZK, T.CL[v, 8 * (st - 1):8 * (st - 1) + L], A.max)
        turn(q, [ok, "IDB"], kb + ":t", lambda pc: K[pc, 384:384 + U], lambda pv, c: T.OK[pv, q, c], 1, T.IDB, True, True)
        op("tt", [kb + ":t", pfk], ["SQ" + y], T["SQ" + y][:, w], K[:, 384:384 + U], PF, A.mult)
        to_list(kb, 0, "SQ" + y, "PM" + y, U)
        op("cp", ["PM" + y, "PU%d.0" % a, "PU%d.1" % a], ["CU.%d" % q], T.CU[:, cs(q)],
           T["PU%d" % a][:, 0:W].indirect(T["PM" + y][:, 0:U // 16]), w=GA)
        op("ts", ["CU.%d" % q], ["CD.%d" % q], T.CD[:, cs(q)], T.CU[:, cs(q)], -OFF, None, A.add, w=0.5)
        if r == RO - 1:
            op("ts", [pfk], ["YP.%d" % q], T.YP[:, cs(q)], PF, OFF, None, A.add)

    def spread(m):
        fs, FS = "FS%d" % m, T.FS[:, m, :]
        op("ts", ["HI:h"], [fs], FS, T.HI[:, 0:96], 0.0, None, A.not_equal)
        s = send([fs], [RemoteDMATransfer(dst_ids=[to(c) for c in peers], dma_engine_mask=bits(efl), remote_sem=T.sem["fl%d%d" % (m, rank)],
                                          srcs=[FS], dsts=[T.FL[:, m, rank, :] for c in peers])], len(efl))
        for d in range(1, NR):
            k = (rank - d) % NR
            arrives("fl%d%d" % (m, k), len(efl), ["FL%d.%d" % (m, k)], s, XL[0] + XL[1] * d)

    def cuts(r, a):
        m, v = 2 * r + a, slice(0, 96)
        cnt, a0, A0 = T.CF[v, 128:256], "A0.%d" % a, T.A0[v, a, :]
        others = [(rank - d) % NR for d in range(1, NR)]
        mm(["ONE", "CY"], ["CF:c"], cnt, T.ONE[0:1, v], T.CY[0:1, :], True, False)
        mm(["FS%d" % m, "ID4"], ["CF:c"], cnt, T.FS[:, m, :], T.ID4[:], False, False)
        for k in others:
            mm(["FL%d.%d" % (m, k), "ID4"], ["CF:c"], cnt, T.FL[:, m, k, :], T.ID4[:], False, k == others[-1])
        op("tt", ["CF:c", a0], [a0], A0, cnt, A0, A.max)
        op("ts", [a0], [a0], A0, A0, CUT, None, A.min, w=0.5)
        for j in range(2):
            dma("y", [a0], ["TX%d.%d" % (a, j)], T["TX%d" % a][64 * j:64 * j + 64:16, :], A0)
        if r == RO - 1:
            op("ts", [a0], ["YC%d" % a], T.YC[v, a, :], A0, 2000.0, None, A.is_ge)
            dma("y", ["YC%d" % a], [], T.yc[4 * a:4 * a + 4, :], T.YC[v, a, :])

    def second_half(r, q, p):
        y, a, (U, st) = "%d" % (q % 2), q // 2, UNITS[q % 2][1:3]
        v, w, C = slice(0, U * st), slice(0, U), 128 // st
        xk, x = "LX%d.%d" % (r, q), T.LX[:, cs(q, r)]
        PF, pfk, oxk, opk = T.PF[:, cs(q, r)], "PF%d.%d" % (r, q), "OX%d.%d" % (r, q), "OP%d.%d" % (r, q)
        K, kk = T["K" + y][v, 0:C], "K%s:k" % y
        o, sp, pt, s1, s2, zt, tk = "OF" + y, "SP" + y, "PT" + y, "S1" + y, "S2" + y, "ZT" + y, "TK" + y
        PAd, PAe, PBx = T.PB[:, 0:U], T.PB[:, U:2 * U], T.PB[:, 256:256 + U]
        distances(p, r, 1, q, T.CU, "CU.%d" % q)
        op("scan", [kk, "RE"], [s1], T[s1][v, 0:C], T.RE[v, 0:C], K, 0.0, A.add, A.max)
        op("scan", [s1, s1 + ".e", "RE"], [s2], T[s2][v, 0:C], T.RE[v, 0:C], T[s1][v, 15:15 + C], 0.0, A.add, A.max)
        op("tt", [kk, s2], [o], T[o][v, 0:C], K, T[s2][v, 0:C], A.is_equal)
        op("tt", [s1, "ZK.%d" % q], [zt], T[zt][v, 0:C:16], T[s1][v, 15:C:16], T.ZK[v, q, 0:C:16], A.is_gt)
        op("scan", [zt, "KB"], [tk], T[tk][v, 0:C], T.KB[v, 0:C], T[zt][v, 0:C], 0.0, A.mult, A.add, w=0.5)
        turn(q, [tk, "IDB"], "PA:k", lambda pc: T.PA[pc, 128:128 + U], lambda pv, c: T[tk][pv, c], 0, T.IDB, True, True)
        turn(q, [o, "IDB"], "PA:t", lambda pc: T.PA[pc, w], lambda pv, c: T[o][pv, c], 0, T.IDB, True, True)
        op("tt", ["PA:t", "CD.%d" % q], [sp], T[sp][:, w], T.PA[:, w], T.CD[:, cs(q)], A.mult)
        l = int(r == RO - 1)
        mm(["ONE", "CB%d0" % l, "CB%d1" % l], ["PB:d"], T.PB[:, 0:2 * U], T.ONE[0:1, 0:128], T.CB[0:1, l, :, w], True, False)
        for pv, _, pc in parts(q):
            for key, src in (("OK.%d" % q, T.OK[pv, q, 0:C]), (tk, T[tk][pv, 0:C])):
                mm([key, "IB0", "IB1"], ["PB:d"], T.PB[pc, 0:2 * U], src, T.IB[pv, :, pv], False, False)
        for j in range(2):
            mm([sp, "BP"], ["PB:d"], T.PB[:, U * j:U * j + U], T.BP[:], T[sp][:, w], False, j == 1)
        if l:
            for bound, how in ((PAd, A.max), (PAe, A.min)):
                op("tt", ["PB:d", "YP.%d" % q], ["YP.%d" % q], T.YP[:, cs(q)], bound, T.YP[:, cs(q)], how)
        else:
            op("tt", ["PB:d", pfk], [pt], T[pt][:, w], PAd, PF, A.max)
            op("tt", ["PB:d", pt], [opk], T.OP[:, cs(q, r)], PAe, T[pt][:, w], A.min)
        to_list("HI", 480, sp, "PL" + y, U)
        op("tt", ["PL" + y, xk] + txk(a), ["DX" + y], T["DX" + y][:, w], T["TX%d" % a][:, 0:W].indirect(T["PL" + y][:, 0:U // 16]), x,
           A.subtract, w=GA)
        op("tt", ["DX" + y, "PA:k"], ["DY" + y], T["DY" + y][:, w], T["DX" + y][:, w], T.PA[:, 128:128 + U], A.mult)
        mm([xk, "IDB"], ["PB:x"], PBx, T.IDB[:], x, True, False)
        turn(q, [tk, "B64"], "PB:x", lambda pc: T.PB[pc, 256:256 + U], lambda pv, c: T[tk][pv, c], 0, T.B64, False, False)
        mm(["DY" + y, "IDH"], ["PB:x"], PBx, T.IDH[:], T["DY" + y][:, w], False, True)
        op("ts", ["PB:x"], [oxk], T.OX[:, cs(q, r)], PBx, -0.2, None, A.add)
        if r < RO - 1:
            for key, o, l in ((opk, "OP", "PF"), (oxk, "OX", "LX")):
                sem = "%s%d%d" % (o, r, q)
                s = send([key], [RemoteDMATransfer(dst_ids=[to(nxt)], dma_engine_mask=bits(enx), remote_sem=T.sem[sem],
                                                   src=T[o][:, cs(q, r)], dst=T[l][:, cs(q, r + 1)])], len(enx))
                arrives(sem, len(enx), ["%s%d.%d" % (l, r + 1, q)], s, XL[2])
        else:
            op("act", [oxk], ["YX.%d" % q], T.YX[:, cs(q)], T.OX[:, cs(q, r)], F.Identity, bias=-128.0)
            for j in range(2):
                c = slice(H * j + UNITS[q % 2][0], H * j + UNITS[q % 2][0] + U)
                dma("y", ["YP.%d" % q], [], T.yp[half(a), c], T.YP[half(j), cs(q)])
                dma("y", ["YX.%d" % q], [], T.yx[half(a), c], T.YX[half(j), cs(q)])

    for r in range(RO):
        for q in range(4):
            prepare(r, q)
            first_half(r, q, 8 * r + q)
        for q in range(4):
            if q % 2 == 0:
                cuts(r, q // 2)
            second_half(r, q, 8 * r + 4 + q)
    finish()
